import numpy as np, ml_dtypes
CORES = [23,119,17,113]
N = 4
BF = ml_dtypes.bfloat16
V, P, L, RO, Q, CAP = 2688, 4096, 256, 3, 3, 64
H, ST = 2048, 10
MS, PO = (4, 4, 5, 5, 6, 6, 7, 8), 14
def rings(rng, hole):
    pool = 1 + np.argsort(rng.random((8, 16, 255)), axis=-1)[..., :PO]
    ms = np.stack([rng.permutation(np.array(MS)) for r in range(N)])
    pal = np.take_along_axis(np.broadcast_to(pool, (N, 8, 16, PO)), np.argsort(rng.random((N, 8, 16, PO)), axis=-1), 3)
    k = np.take_along_axis(pal, (rng.random((N, 8, 16, V)) * ms[:, :, None, None]).astype(np.int64), 3)
    u = rng.random((N, 8, 16, V))
    return np.where(u < hole, 0, np.where(u < hole + 0.05, rng.integers(1, 256, (N, 8, 16, V)), k))
def parts(rng, hole=0.12):
    t = rng.choice(np.array([0, 300, 500, 700, 850]), (N, 8, 16, 1)) + rng.integers(0, 100, (N, 8, 16, 1))
    return rings(rng, hole), rng.integers(0, V, (N, 8, 16, V)), rng.integers(0, 256, (N, 8, 16, P)), rng.integers(0, 256, (N, 8, 16, L)), t
def pack(k, b, x, z, t):
    def bf(a): return np.ascontiguousarray(a.reshape(N, 128, -1)).astype(np.float32).astype(BF)
    return {"ring": bf(k), "nbr": np.ascontiguousarray(b.reshape(N, 128, V)).astype(np.int32), "mat": bf(x), "z0": bf(z), "thr": np.ascontiguousarray(t.reshape(N, 128, 1)).astype(np.int32)}
def setup_inputs(rng):
    return pack(*parts(rng))
def setup_inputs_spread(rng):
    k, b, x, z, t = parts(rng)
    e = rng.integers(5, 13, (N, 8, 1, 1)); ix = np.minimum((255 * rng.random((N, 8, 16, V)) ** e).astype(np.int64), 254)
    keys = 1 + np.argsort(rng.random((8, 16, 255)), axis=-1)
    k = np.take_along_axis(np.broadcast_to(keys, (N, 8, 16, 255)), ix, 3)
    k = np.where(rng.random((N, 8, 16, V)) < rng.random((N, 8, 1, V)) ** 3, 0, k)
    b[:, ::2] = np.minimum((V * rng.random((N, 4, 16, V)) ** 2).astype(np.int64), V - 1)
    x = np.minimum((np.exp2(8 * rng.random((N, 8, 1, P))) * rng.random((N, 8, 16, P))).astype(np.int64), 255)
    z = np.minimum((np.exp2(8 * rng.random((N, 8, 1, L))) * rng.random((N, 8, 16, L))).astype(np.int64), 255)
    t = np.minimum(np.exp2(12 * rng.random((N, 8, 16, 1))).astype(np.int64), 4095)
    return pack(k, b, x, z, t)
def setup_inputs_ends(rng):
    k, b, x, z, t = parts(rng)
    c = rng.random((N, 8, 1, V)); dens = rng.choice(np.array([0.25, 0.25, 0.5]), (N, 8, 1, V))
    k = np.where(c < 0.25, 255, np.where(c < 0.4, 0, np.where(c < 0.85, 255 * (rng.random((N, 8, 16, V)) < dens), k)))
    k[:, 6, :, 2 * ST:ST * (L - 4):ST] = 255
    b = np.where(rng.random((N, 8, 16, V)) < 0.7, (V - 1) * rng.integers(0, 2, (N, 8, 16, V)), b)
    share = np.array([0.5, 0, 0.5, 0, 0, 0, 0, 0]).reshape(8, 1, 1)
    x = np.where(rng.random((N, 8, 1, P)) < share + 0.05, 255 * rng.integers(0, 2, (N, 8, 1, P)), 255 * rng.integers(0, 2, (N, 8, 16, P)))
    z = np.where(rng.random((N, 8, 1, L)) < share, 255 * rng.integers(0, 2, (N, 8, 1, L)), 255 * rng.integers(0, 2, (N, 8, 16, L)))
    t = np.broadcast_to(4095 * (rng.random((1, 8, 16, 1)) < 0.25), (N, 8, 16, 1)); t = np.where(rng.random((N, 8, 16, 1)) < 0.05, 4095 - t, t)
    t[:, 0, 0] = 4095; t[:, 7, 14] = 0; t[:, 7, 15] = 4095
    k[..., V - 1] = 255; k[..., 0] = 255 * (np.argsort(np.argsort(rng.random((N, 8, 16)), axis=-1), axis=-1) < 5)
    x[..., 0] = 0; x[..., P - 1] = 255
    p = np.arange(16)
    for lane in (1, L - 1):
        v = ST * lane; z[..., lane] = 255; k[..., v] = 0; b[:, :, 0, v] = V - 1
        x[..., ((255 * (2 * v + 1) >> 2) + 811 * p) & (P - 1)] = 0 if lane == 1 else 255 * ((p + 1) & 1)
    z[..., 0] = 0; z[..., L - 2] = 0; k[..., ST * (L - 2)] = 0
    a = (15 + Q) >> 1; v = ST * (L - 4); z[..., L - 4] = 0
    k[..., v] = 255 * (p < a); k[..., V - 2] = 255 * (p >= 16 - a); b[:, :, 0, v] = V - 2
    k[..., V - 3] = 255; k[..., V - 4] = 255; b[:, :, 0, V - 2] = V - 2
    for i, u in ((1, V - 1), (14, V - 3), (15, V - 4)): b[:, :, i, V - 2] = u
    return pack(k, b, x, z, t)
def setup_inputs_corners(rng):
    k, b, x, z, t = parts(rng)
    code = rng.integers(1, 256, (N, 8, 16, 1)); code[:, ::2] = code[:1, ::2]; row = np.arange(16)[:, None]
    u = rng.random((N, 8, 1, V))
    k = np.where((row < Q) | (u < 0.33), code, np.where(u < 0.66, rng.integers(1, 256, (N, 8, 16, V)), 0))
    own = np.broadcast_to(np.arange(V), (16, V)); many = (0, 1, CAP - 1, CAP, CAP + 1, L, CAP, L >> 1)
    for r in range(N):
        for g in range(8):
            n = many[(g + r) & 7]; lanes = rng.permutation(L)[:n]; vf = ST * lanes
            if g & 3 == 1: b[r, g] = np.where(rng.random((16, V)) < 0.5, own, b[r, g])
            if g & 3 == 2: b[r, g] = np.where(rng.random((16, V)) < 0.3, (V - 1) * rng.integers(0, 2, (16, V)), b[r, g])
            if g & 3 == 3: b[r, g] = np.where(rng.random((16, V)) < 0.5, rng.integers(0, V, (1, V)), b[r, g])
            gone = np.zeros(V, bool); gone[vf] = True
            b[r, g] = b[r, g] + gone[b[r, g]]
            if g & 3 == 1: b[r, g][:, vf[::2]] = vf[::2]
            k[r, g][:, vf] = np.where((row < Q - 1) & (rng.random(n) < 0.5), code[r, g], 0)
    t = np.where(rng.random((N, 8, 16, 1)) < 0.5, rng.choice(np.array([0, 1, 15, 600, 1000, 4095]), (N, 8, 16, 1)), t); t[:, ::2, :Q] = 0; t[:, 1, 15] = 4095
    x = np.where(rng.random((N, 8, 1, P)) < 0.2, rng.choice(np.array([0, 128, 255]), (N, 8, 1, P)), x)
    z = np.where(rng.random((N, 8, 1, L)) < 0.3, rng.choice(np.array([0, 1, 254, 255]), (N, 8, 1, L)), z)
    return pack(k, b, x, z, t)
def setup_inputs_crowd(rng):
    k, b, x, z, t = parts(rng, 0.22)
    k = np.where(rng.random((N, 8, 1, V)) < 0.03, 0, k)
    hubs = np.argsort(rng.random((N, 8, V)), axis=-1)[..., :12]
    h = np.take_along_axis(hubs, rng.integers(0, 12, (N, 8, 16 * V)), 2).reshape(N, 8, 16, V)
    b = np.where(rng.random((N, 8, 16, V)) < 0.6, h, b)
    x[:, 1::2] = np.take_along_axis(x[:, 1::2], np.broadcast_to(rng.integers(0, 8, (N, 4, 1, P)), (N, 4, 16, P)), 3)
    z[..., 1::2] = z[..., ::2]
    return pack(k, b, x, z, t)
def setup_inputs_far(rng):
    k, b, x, z, t = parts(rng); a = (15 + Q) >> 1; kk = np.arange(16)[:, None]
    up = rng.integers(0, 2, (N, 8, 1, 1)); up[0, 0] = 0; up[N - 1, 7] = 1
    x = rng.integers(0, 48, (N, 8, 16, P)) + 208 * up; z = rng.integers(0, 48, (N, 8, 16, L)) + 208 * (1 - up)
    t = np.where(rng.random((N, 8, 16, 1)) < 0.4, rng.integers(3000, 3500, (N, 8, 16, 1)), t)
    first = ST * np.arange(L); rest = np.setdiff1d(np.arange(V), first)
    for r in range(N):
        for g in range(8):
            if (g + r) & 1: continue
            code = rng.integers(1, 256, (16, 1)); o = rng.permutation(16)[:, None]
            rare = 1 + (code - 1 + rng.integers(1, 255, (16, V))) % 255
            other = np.where(rng.random((16, V)) < 0.7, 0, rare)
            u = rng.permutation(rest); q = len(u) >> 2; near = u[:q]; full = u[q:2 * q]; right = u[2 * q:3 * q]
            kr = k[r, g]; br = b[r, g]
            kr[:, first] = np.where(o < a, code, other[:, first])
            kr[:, right] = np.where(o >= 16 - a, code, other[:, right])
            kr[:, full] = code
            kr[:, near] = np.where(o == rng.integers(a, 16, q), rare[:, near], code)
            e = ST * rng.permutation(L)[:L >> 4]
            kr[:, e[::2]] = 0; kr[:, e[1::2]] = code
            br[:, first] = rng.choice(right, (16, L))
            i = rng.integers(0, 15, q); m = i + 1 + (rng.random(q) * (15 - i)).astype(np.int64)
            pick = rng.random((16, q)); low = rng.choice(near, (16, q)); top = rng.choice(full, (16, q)); poor = rng.choice(np.concatenate([first, u[2 * q:]]), (16, q))
            late = np.where((kk == m) | (pick < 0.4), top, np.where(pick < 0.7, low, poor))
            early = np.where((kk == i) | ((kk > i) & (pick < 0.5)), low, poor)
            br[:, right] = np.where(kk < m, early, late)
    return pack(k, b, x, z, t)
def check_inputs(d):
    bad = []
    for k, lo, hi in (("ring", 0, 255), ("nbr", 0, V - 1), ("mat", 0, 255), ("z0", 0, 255), ("thr", 0, 4095)):
        a = np.asarray(d[k]).astype(np.float64)
        if not (np.min(a) >= lo and np.max(a) <= hi): bad.append("range of " + k)
        elif np.any(a != np.floor(a)): bad.append("whole numbers in " + k)
    return bad
def columns(a, ix):
    return np.take_along_axis(a, ix[:, :, None, :], 3)
def by_lane(a):
    return np.ascontiguousarray(a.transpose(0, 1, 3, 2)).reshape(N, 8, L * 16)
def reference(ring, nbr, mat, z0, thr):
    K = ring.astype(np.float32).astype(np.int64).reshape(N, 8, 16, V); B = nbr.astype(np.int64).reshape(N, 8, 16, V)
    X = mat.astype(np.float32).astype(np.int64).reshape(N, 8, 16, P); z = z0.astype(np.float32).astype(np.int64).reshape(N, 8, 16, L)
    th = thr.astype(np.int64).reshape(N, 8, 16, 1); v = np.array(np.broadcast_to(ST * np.arange(L), (N, 8, L)))
    failures = np.zeros(N, np.int64); rv_old = np.zeros((N, 8, 16), np.int64); row = np.arange(16)[:, None]
    for t in range(RO):
        j = (np.sum(z, axis=2) + t) & 15
        n = np.take_along_axis(columns(B, v), j[:, :, None, :], 2)[:, :, 0]
        Kv = columns(K, v); Kn = columns(K, n)
        direct = np.sum((Kv == Kn) & (Kv > 0), axis=2) >= Q
        cand = by_lane(columns(B, n)); Kc = columns(K, cand).reshape(N, 8, 16, L, 16)
        score = np.minimum(np.sum((Kc == Kv[..., None]) & (Kc > 0), axis=2), np.sum((Kc == Kn[..., None]) & (Kc > 0), axis=2))
        k = np.argmax(score, axis=3)
        bridged = ~direct & (np.max(score, axis=3) >= Q); failed = ~direct & ~bridged
        w = np.where(bridged, np.take_along_axis(cand.reshape(N, 8, L, 16), k[..., None], 3)[..., 0], n)
        Kw = columns(K, w)
        place = (((Kw * (2 * v + 1)[:, :, None, :]) >> 2) + 811 * row + t) & (P - 1)
        Xc = columns(X, by_lane(place)).reshape(N, 8, 16, L, 16)
        d = np.sum(np.abs(Xc - z[..., None]), axis=2)
        p = np.argmin(d, axis=3)
        x = np.take_along_axis(Xc, p[:, :, None, :, None], 4)[..., 0]
        caught = (d.transpose(0, 1, 3, 2) < th + (failures & 15)[:, None, None, None]) & (Kw > 0)
        low = np.argmax(caught, axis=3)
        rv = np.where(np.any(caught, axis=3), np.take_along_axis(Kw, low[..., None], 3)[..., 0], 0)
        fi = failed.astype(np.int64); served = failed & (np.add.accumulate(fi, axis=2) - fi < CAP)
        h = np.sum(Kw * z, axis=2) & (H - 1)
        given = columns(np.roll(K, -1, axis=0), h)
        filled = np.where(Kv > 0, Kv, np.where(bridged[:, :, None, :], Kw, given))
        K2 = np.array(K); B2 = np.array(B); active = bridged | served
        for a in range(N):
            for g in range(8):
                i = np.nonzero(active[a, g])[0]
                u, first = np.unique(v[a, g, i], return_index=True); i = i[first]
                K2[a, g][:, u] = filled[a, g][:, i]
                i = i[bridged[a, g, i]]; B2[a, g, j[a, g, i], v[a, g, i]] = w[a, g, i]
        come = np.roll(rv_old, 1, axis=0)
        K = np.where((K2 == rv[..., None]) | (K2 == come[..., None]), 0, K2); B = B2
        z = (z + x) >> 1; v = w; rv_old = rv; failures = np.sum(fi, axis=(1, 2))
    return {"yk": K.reshape(N, 128, V).astype(np.float32).astype(BF), "yz": z.reshape(N, 128, L).astype(np.float32)}

@@ -1,0 +1,762 @@
+from concourse.mybir import AluOpType, AxisListType, ActivationFunctionType
+
+OP = AluOpType
+AF = ActivationFunctionType
+V, PL, L, NR, H = 2688, 4096, 256, 3, 2048
+REM = V + L
+NC, NL = 2, 128
+S17 = float(2 ** 17)
+BIG = float(2 ** 20)
+CYC, PEC, VF, SF, WK, GA, SCA = 0.83, 0.42, 80.0, 100.0, 60.0, 1.5, 3.0
+CLB = 15000.0
+BT = {"v": (0.0, 0.0), "n": (1700.0, 0.0), "c": (2000.0, 0.0), "w": (8800.0, 600.0), "d": (3800.0, 700.0), "f": (0.0,)}
+CAP = 64
+NSB, E3S = 16, 0
+NSV, NSN, EQB, SUBK, SUBX = 0, 16, 1, 2, 2
+CBN = {}
+ALIAS = {}
+SCRATCH = {}
+
+
+def _lay(d, names):
+    o = 0
+    for nm, w in names:
+        d[nm] = (o, o + w)
+        o += w
+    return o
+
+
+def _small(big, dtype, names):
+    o = 0
+    for nm in names:
+        ALIAS[nm] = (big, o)
+        o += 32 if nm[:3] == "wfl" else 16
+    SCRATCH[big] = ("sbuf", [128, o], dtype)
+
+
+def _bufs(dtype, width, names):
+    for nm in names:
+        SCRATCH[nm] = ("sbuf", [128, width], dtype)
+
+
+CBW = _lay(CBN, [("u17", 144), ("u32", 144), ("u1", 144), ("bo1", 128), ("boh", 128), ("i1", 128),
+                 ("im", 128), ("imh", 128), ("i256", 128), ("i1k", 128), ("kb", 128), ("pt", 128), ("io", 256), ("tri", 256),
+                 ("on", 128), ("lt", 128), ("ones", 128), ("sl", 512), ("rq", 2048), ("c13", 16), ("c75", 2),
+                 ("m512", 128), ("ih", 128), ("u64", 144), ("um32", 144), ("bv16", 128), ("bv32", 128)])
+_bufs("bfloat16", REM, ("tab0", "tab1", "tab2", "tab3"))
+_bufs("bfloat16", H + 16, ("rem0", "rem1", "rem2"))
+_bufs("bfloat16", H, ("kc0", "kc1", "e10", "e11", "e20", "e21", "xc0", "xc1", "mx0", "mx1", "da0",
+                      "da1", "db0", "db1"))
+_bufs("bfloat16", V, ("cln", "clb", "fin"))
+_bufs("bfloat16", L, ("zi", "zb", "kv", "kn", "q0", "qa", "qb", "e0", "kw", "kwc", "src", "sa", "sb", "f1", "hb", "ug",
+                      "flr", "nfr", "kvr", "knp", "kvp", "fi", "ed", "cnb"))
+_bufs("float16", L, ("bv", "nm", "cdh", "wm"))
+_bufs("float16", 8, ("pc",))
+_bufs("float32", L, ("wrp0", "wrp1", "row", "jr", "tmpc", "av", "val", "vt", "sc", "v2", "pz", "dt", "ds", "xm", "sz", "zs", "bn", "yzf"))
+_bufs("float32", 128, ("m32", "mxm", "mnm"))
+_bufs("int32", L, ("yi", "yj", "pi", "pj", "pk"))
+_bufs("uint16", L, ("cd", "pl"))
+_bufs("float32", 4, ("ra0", "ra1", "ra2", "rb0", "rb1", "rc0", "rc1"))
+_bufs("float32", 8, ("fs", "rr"))
+_bufs("int32", 8, ("ipc",))
+_small("smu", "uint16", ("nl", "pw", "sl2", "sl", "wl0", "wl1", "wl2"))
+_small("sm32", "float32", ("dk", "nk16", "tot", "th", "hH", "h2", "vb", "sy", "pH", "dum", "v0w"))
+_small("sm16", "float16", ("w16", "fl", "dr", "iah", "vah", "p16", "wfl0", "wfl1"))
+SCRATCH["nb"] = ("sbuf", [128, REM], "int32")
+SCRATCH["X"] = ("sbuf", [128, PL], "bfloat16")
+SCRATCH["thi"] = ("sbuf", [128, 1], "int32")
+SCRATCH["cb"] = ("sbuf", [128, CBW], "bfloat16")
+SCRATCH["u1f"] = ("sbuf", [128, 144], "float32")
+SCRATCH["col"] = ("sbuf", [128, 64], "float32")
+SCRATCH["e3"] = ("sbuf", [128, 1920], "bfloat16")
+for _b in range(8):
+    SCRATCH["ps%d" % _b] = ("psum", [128, 512], "float32")
+SEMAPHORES = ["qv", "qs", "qp", "qg"] + ["d%d" % i for i in range(40)] \
+    + [a + str(i) for a in ("pusha", "pushb", "pla", "plb", "rvs", "rvl", "rws", "rwl") for i in range(3)]
+
+
+def rank_program(g, core, T, topo):
+    rank = T.rank_of(core)
+    if rank is None:
+        return
+    nranks = len(T.cores)
+    nxt, prv = T.cores[(rank + 1) % nranks], T.cores[(rank - 1) % nranks]
+    ops, hist, ndma, bon, nb_ = [], {}, [0], [0.0], [0]
+
+    def A(name, lo, hi, st=1):
+        if name in ALIAS:
+            name, o = ALIAS[name]
+            lo, hi = lo + o, hi + o
+        ap = T[name][:, lo:hi] if st == 1 else T[name][:, lo:hi:st]
+        return ([(name, lo, hi)], ap, (hi - lo + st - 1) // st)
+
+    def cb(nm, lo=0, w=None):
+        o, e = CBN[nm]
+        return A("cb", o + lo, e if w is None else o + lo + w)
+
+    def U(nm, q):
+        return cb(nm, 15 - q, 128)
+
+    def ind(win, lst):
+        return (win[0] + lst[0], win[1].indirect(lst[1]), 16 * lst[2], 1)
+
+    def op(q, dur, rd, wr, call, sem=None, val=1, lat=0.0):
+        i = len(ops)
+        deps = {}
+        for regs, w in ((rd, 0), (wr, 1)):
+            for nm, lo, hi in regs:
+                if nm[:2] == "ps":
+                    for q2, j in hist.get(nm, {}).items():
+                        if j != i:
+                            deps[j] = deps.get(j, False) or q2 != q or q != "p"
+                else:
+                    for j, l2, h2, w2 in hist.get(nm, []):
+                        if j != i and l2 < hi and lo < h2 and (w or w2):
+                            deps[j] = True
+        for regs, w in ((rd, 0), (wr, 1)):
+            for nm, lo, hi in regs:
+                if nm[:2] == "ps":
+                    hist.setdefault(nm, {})[q] = i
+                else:
+                    a = hist.setdefault(nm, [])
+                    if w:
+                        a[:] = [e for e in a if e[0] == i or not (lo <= e[1] and e[2] <= hi)]
+                    a.append((i, lo, hi, w))
+        ops.append({"q": q, "dur": dur, "deps": deps, "call": call, "sem": sem, "val": val, "lat": lat, "bon": bon[0]})
+        return i
+
+    def vdur(n, f):
+        return max(64.0, n * f) * CYC + VF
+
+    def two(*xs):
+        return all(SCRATCH[x[0][0][0]][2] in ("bfloat16", "float16", "uint16") for x in xs)
+
+    def sc_(x):
+        return (x[1], x[0]) if isinstance(x, tuple) else (x, [])
+
+    def ts(out, a, s1, s2, o0, o1=None):
+        x1, r1 = sc_(s1)
+        x2, r2 = sc_(s2)
+        f = GA if len(a) > 3 else (0.5 if two(out, a) else 1.0)
+        if o1 is None:
+            def call():
+                return g.vector.tensor_scalar(out[1], a[1], x1, None, o0)
+        else:
+            def call():
+                return g.vector.tensor_scalar(out[1], a[1], x1, x2, o0, o1)
+        return op("v", vdur(a[2], f), a[0] + r1 + r2, out[0], call)
+
+    def tt(out, a, b, o):
+        ps = a[0][0][0][:2] == "ps" or b[0][0][0][:2] == "ps"
+        return op("v", vdur(b[2], GA if len(a) > 3 else 1.0 if ps else 2.0), a[0] + b[0], out[0],
+                  lambda: g.vector.tensor_tensor(out[1], a[1], b[1], o))
+
+    def cp(out, a):
+        f = SCA if len(out) > 3 else GA if len(a) > 3 else (0.5 if two(out, a) else 1.0)
+        wr = out[0][:1] if len(out) > 3 else out[0]
+        rd = a[0] + (out[0][1:] if len(out) > 3 else [])
+        return op("v", vdur(a[2], f), rd, wr, lambda: g.vector.tensor_copy(out[1], a[1]))
+
+    def red(out, a, o):
+        return op("v", vdur(a[2], 1.0), a[0], out[0], lambda: g.vector.tensor_reduce(out[1], a[1], AxisListType.X, o))
+
+    def scan(out, d0, d1, o0, o1):
+        return op("v", vdur(d1[2], 1.0), d0[0] + d1[0], out[0],
+                  lambda: g.vector.tensor_tensor_scan(out[1], d0[1], d1[1], 0.0, o0, o1))
+
+    def tr(out, a):
+        return op("v", vdur(a[2], 1.0), a[0], out[0], lambda: g.vector.transpose(out[1], a[1]))
+
+    def fill(out, c):
+        return op("v", vdur(out[2], 0.5), [], out[0], lambda: g.vector.memset(out[1], c))
+
+    def act(out, a, func=None, scale=1.0, bias=0.0):
+        x, r = sc_(bias)
+        y, r2 = sc_(scale)
+        fn = AF.Identity if func is None else func
+        return op("s", a[2] * (GA if len(a) > 3 else 1.0) * CYC + SF, a[0] + r + r2, out[0],
+                  lambda: g.scalar.activation(out[1], a[1], fn, bias=x, scale=y))
+
+    def mm(out, lhsT, rhs, start, stop):
+        f = 4 if SCRATCH[rhs[0][0][0]][2] == "float32" else 1
+        return op("p", max(min(64.0, lhsT[2]), rhs[2]) * f * PEC, lhsT[0] + rhs[0], out[0],
+                  lambda: g.tensor.matmul(out[1], lhsT[1], rhs[1], start, stop))
+
+    def group(out, pairs):
+        for i, pr in enumerate(pairs):
+            mm(pr[2] if len(pr) > 2 else out, pr[0], pr[1], i == 0, i == len(pairs) - 1)
+
+    def iota(out, pat, base, mul):
+        if SCRATCH[out[0][0][0]][2] != "int32":
+            def call():
+                return g.iota(out[1], pat, base, mul, allow_small_or_imprecise_dtypes=True)
+        else:
+            def call():
+                return g.iota(out[1], pat, base, mul)
+        return op("g", 130 + 2 * out[2] * CYC, [], out[0], call)
+
+    def dma(q, out, a, nbytes, add=False, after=()):
+        s = "d%d" % ndma[0]
+        ndma[0] += 1
+        eng = {"y": g.sync, "s": g.scalar, "g": g}[q]
+        if add:
+            def call():
+                return eng.dma_start(out[1], a[1], accum_op=OP.add)
+        else:
+            def call():
+                return eng.dma_start(out[1], a[1])
+        return op(q, 1000 if q == "g" else 60, a[0] + (out[0] if add else []) + [(x, 0, 1) for x in after], out[0], call, sem=s, val=16,
+                  lat=1900 + nbytes / 180.0)
+
+    def hbm(name, lo, hi):
+        return ([("hbm_" + name, lo, hi)], T[name][:, lo:hi], hi - lo)
+
+    def remote(dst, src, out, frm, rsem, lsem, nbytes):
+        rid, pid, _se = topo.addr(dst)
+        msk = topo.mask(core, dst)
+        ne = len(topo.engines(core, dst))
+        op("g", 1000, src[0], [], lambda: g.remote_dma(out[1], src[1], T.sem[rsem], T.sem[lsem], pid, rid, msk),
+           sem=lsem, val=ne, lat=2000 + nbytes / 60.0)
+        ops[-1]["remote"] = True
+        op("ext", 0, [], out[0], None, sem=rsem, val=len(topo.engines(frm, core)))
+        ops[-1]["after"] = len(ops) - 2
+
+    def KA(c, lo, hi, st=1): return A("ps%d" % c, lo, hi, st)
+    def AC(c, lo, hi): return A("ps%d" % (2 + c), lo, hi)
+    def SM(c, lo, hi, st=1): return A("ps%d" % (4 + c), lo, hi, st)
+    def DB(b, lo, hi): return A("ps%d" % (6 + b), lo, hi)
+    def F1(lo, hi): return A("ps1", 384 + lo, 384 + hi)
+    def col(i): return A("col", i, i + 1)
+    def ck(name, c): return A(name, NL * c, NL * c + NL)
+    def cw(name, c): return A(name, 8 * c, 8 * c + 8)
+    def fu(name): return A(name, 0, 16)
+    def tabw(t): return A("tab%d" % t, 0, V)
+    def zbuf(t): return "zi" if t == 0 else "zb"
+
+    dma("s", A("zi", 0, L), hbm("z0", 0, L), 2 * 128 * L)
+    dma("y", A("nb", 0, V), hbm("nbr", 0, V), 4 * 128 * V)
+    dma("s", A("tab0", 0, V), hbm("ring", 0, V), 2 * 128 * V)
+    dma("s", A("thi", 0, 1), hbm("thr", 0, 1), 512)
+    dma("y", A("X", 0, PL), hbm("mat", 0, PL), 2 * 128 * PL, after=("nb", "tab0"))
+    dma("y", A("tab1", 0, V), hbm("ring", 0, V), 2 * 128 * V, after=("X",))
+
+    iota(A("ipc", 0, 1), [[0, 1]], 0, 1)
+    iota(A("row", 0, 256), [[1, 256]], 0, 0)
+    iota(A("jr", 0, 256), [[0, 16], [1, 16]], 0, 0)
+    iota(A("m32", 0, 128), [[32, 4], [0, 32]], 0, 0)
+    iota(fu("dum"), [[16, 16]], V, 1)
+    iota(fu("v0w"), [[160, 16]], 0, 10)
+    iota(A("v2", 0, 256), [[20, 256]], 1, 0)
+    ip = A("ipc", 0, 1)
+    ts(A("ipc", 1, 2), ip, 15, None, OP.bitwise_and)
+    ts(A("ipc", 2, 3), ip, 96, None, OP.bitwise_and)
+    ts(A("ipc", 3, 4), ip, 4, 1, OP.logical_shift_right, OP.bitwise_and)
+    cp(A("col", 0, 2), A("ipc", 0, 2))
+    cp(A("col", 4, 6), A("ipc", 2, 4))
+    tt(col(2), col(0), col(1), OP.subtract)
+    ts(col(3), col(2), 15.0, None, OP.add)
+    ts(col(36), col(1), -1.0, 16.0, OP.mult, OP.add)
+    ts(col(8), col(1), 3244.0, None, OP.mult)
+    row128 = A("row", 0, 128)
+    row144 = A("row", 0, 144)
+    j128 = A("jr", 0, 128)
+    tt(A("tmpc", 0, 256), A("row", 0, 256), A("jr", 0, 256), OP.subtract)
+    m16 = A("tmpc", 0, 128)
+    ts(cb("i1"), row128, col(0), None, OP.is_equal)
+    act(cb("im"), cb("i1"), AF.Copy, scale=-1.0)
+    ts(cb("bo1"), m16, col(2), None, OP.is_equal)
+    ts(cb("u1"), row144, col(3), None, OP.is_equal)
+    act(cb("u17"), cb("u1"), AF.Copy, scale=S17)
+    ts(col(7), col(1), -4096.0, 61440.0 - 2.5 * S17, OP.mult, OP.add)
+    act(cb("kb"), row128, scale=0.0, bias=col(7))
+    ts(A("mxm", 0, 128), j128, 0.5, 2e9, OP.is_ge, OP.mult)
+    ts(A("mxm", 0, 128), A("mxm", 0, 128), -1e9, None, OP.add)
+    ts(col(12), col(5), 10000.0, col(0), OP.mult, OP.add)
+    ts(col(13), col(5), -10000.0, col(0), OP.mult, OP.add)
+    for g2 in range(2):
+        for c2 in range(2):
+            ts(cb("sl", 128 * (2 * g2 + c2), 128), row128, float(-16 * g2 if c2 == 0 else 16 * (1 - g2) - 10000), col(12 + c2),
+               OP.add, OP.is_equal)
+    act(cb("u32"), cb("u1"), AF.Copy, scale=32.0)
+    ts(col(6), col(1), -8.0, None, OP.add)
+    act(cb("pt"), row128, scale=0.0, bias=col(6))
+    act(A("mnm", 0, 128), A("mxm", 0, 128), AF.Copy, scale=-1.0)
+    iota(cb("io"), [[512, 256]], 0, 0)
+    fill(col(16), BIG)
+    ts(fu("dum"), fu("dum"), col(2), None, OP.subtract)
+    ts(col(17), col(2), -10.0, None, OP.mult)
+    ts(fu("v0w"), fu("v0w"), col(17), None, OP.add)
+    ts(A("pc", 0, 8), A("dum", 0, 8), 16.0, float(8 - 16 * V), OP.mult, OP.add)
+    act(A("u1f", 0, 144), cb("u1"), AF.Copy)
+    ts(cb("on"), A("m32", 0, 128), col(4), None, OP.is_equal)
+    ts(cb("lt"), row128, col(0), None, OP.is_ge)
+    tt(cb("lt"), cb("lt"), cb("on"), OP.mult)
+    act(cb("ones"), row128, scale=0.0, bias=1.0)
+    act(cb("c13"), A("row", 0, 16), scale=0.0, bias=1344.0)
+    if NSB < 16:
+        act(cb("ih"), cb("i1"), AF.Copy, scale=0.5)
+        act(cb("u64"), cb("u1"), AF.Copy, scale=64.0)
+        act(cb("um32"), cb("u1"), AF.Copy, scale=-32.0)
+        ts(cb("bv16"), j128, float(NSB), -16.0, OP.is_ge, OP.mult)
+        tt(cb("bv16"), cb("bv16"), cb("bo1"), OP.mult)
+        act(cb("bv32"), cb("bv16"), AF.Copy, scale=2.0)
+    act(cb("m512"), row128, scale=0.0, bias=-512.0)
+    act(cb("c75"), A("row", 0, 2), scale=0.0, bias=-7.5)
+    ts(A("col", 40, 56), A("jr", 0, 16), col(1), None, OP.is_equal)
+    for q in range(16):
+        act(cb("rq", 128 * q, 128), cb("bo1"), AF.Copy, scale=col(40 + q))
+    for c in range(NC):
+        ts(A("wfl1", 16 * c, 16 * c + 8), cw("v0w", c), -1344.0, None, OP.add)
+    act(A("wrp1", 0, L), A("v2", 0, L), scale=0.5, bias=-1344.5)
+    cp(col(18), A("thi", 0, 1))
+    ts(col(22), col(18), 32.0, col(6), OP.mult, OP.add)
+    ts(col(23), col(22), -BIG, BIG, OP.mult, OP.add)
+    act(cb("i1k"), cb("i1"), AF.Copy, scale=1024.0)
+    act(cb("imh"), cb("i1"), AF.Copy, scale=-0.5)
+    act(cb("i256"), cb("i1"), AF.Copy, scale=-256.0)
+    act(cb("boh"), cb("bo1"), AF.Copy, scale=0.5)
+    ts(cb("tri"), A("jr", 0, 256), col(1), 32768.0, OP.is_le, OP.mult)
+    def pushes(t):
+        for x, lo, hi, to in (("a", 1024, 2048, 0), ("b", 0, 1026, 1024)):
+            remote(prv, A("tab%d" % t, lo, hi), A("rem%d" % t, to, to + hi - lo), nxt, "push%s%d" % (x, t), "pl%s%d" % (x, t),
+                   256 * (hi - lo))
+
+    pushes(0)
+
+    def l2p(out, src):
+        (nm, lo, hi), (sn, slo, shi) = out, src
+        return [(cb("sl", 128 * (2 * g2 + c2), 128), A(sn, slo + g2, shi, 2), A(nm, lo + c2, hi, 2))
+                for c2 in range(2) for g2 in range(2)]
+
+    def l2wrap(out, src):
+        prs = l2p(out, src)
+        group(None, prs[:2])
+        group(None, prs[2:])
+
+    def l2direct(c, o, nm):
+        a = NL * c
+        lo = CBN["bo1"][0]
+        bank = "ps%d" % (4 + c)
+        for pa in range(4):
+            for ib in range(4):
+                out = ([(bank, 0, 1)], T[bank][32 * pa:32 * pa + 32, o + 2 * ib:o + 2 * ib + 2], 2)
+                mm(out, A(nm, a + 32 * ib, a + 32 * ib + 32), A("cb", lo + 32 * pa, lo + 32 * pa + 32, 16), True, True)
+
+    def clean_q(t, c, nm):
+        x = ck(nm, c)
+        prs = [(cb("i1"), x)]
+        ts(ck("q0", c), x, 0.0, None, OP.is_equal)
+        prs.append((cb("im"), ck("q0", c)))
+        if t >= 2:
+            ts(ck("qb", c), x, A("rb0", 0, 1), A("rb0", 1, 2), OP.is_equal, OP.mult)
+            prs.append((cb("im"), ck("qb", c)))
+        if t >= 1:
+            ra = "ra%d" % (t - 1)
+            ts(ck("qa", c), x, A(ra, 0, 1), A(ra, 1, 2), OP.is_equal, OP.mult)
+            prs.append((cb("im"), ck("qa", c)))
+        return prs
+
+    def stage_v(t, c):
+        a = NL * c
+        if t == 0:
+            cp(ck("kv", c), A("tab0", 10 * a, 10 * (a + NL), 10))
+            ts(ck("bv", c), A("nb", 10 * a, 10 * (a + NL), 10), -1344.0, None, OP.add)
+        else:
+            vl = cw("wl%d" % (t - 1), c)
+            act(ck("kv", c), ind(tabw(t), vl))
+            ts(ck("bv", c), ind(A("nb", 0, V), vl), -1344.0, None, OP.add)
+        group(KA(c, 0, 128), clean_q(t, c, "kv"))
+
+    def stage_n(t, c):
+        a = NL * c
+        z = ck(zbuf(t), c)
+        m = AC(c, 128, 256)
+        mm(SM(c, 0, 128), cb("bo1" if t == 0 else "boh"), z, True, True)
+        act(ck("zs", c), z, scale=1.0 if t == 0 else 0.5, bias=-0.5)
+        ts(ck("yi", c), SM(c, 0, 128), col(36), float(t), OP.add, OP.add)
+        ts(ck("yj", c), ck("yi", c), 15, None, OP.bitwise_and)
+        ts(m, ck("yj", c), 0.0, None, OP.is_equal)
+        tt(ck("nm", c), ck("bv", c), m, OP.mult)
+        group(SM(c, 128, 136), [(U("u1", q), A("nm", a + q, a + NL, 16)) for q in range(16)])
+        ts(cw("nl", c), SM(c, 128, 136), 1344.0, None, OP.add)
+        cp(ck("cd", c), ind(A("nb", 0, V), cw("nl", c)))
+        kc = "kc%d" % c
+        for s in range(SUBK):
+            act(A(kc, 2048 // SUBK * s, 2048 // SUBK * (s + 1)),
+                ind(tabw(t), A("cd", a + 128 // SUBK * s, a + 128 // SUBK * (s + 1))))
+        cp(ck("kn", c), ind(tabw(t), cw("nl", c)))
+        l2direct(c, 160, "nm")
+        tt(ck("e0", c), ck("kn", c), KA(c, 0, 128), OP.is_equal)
+        l2direct(c, 168, "e0")
+        ts(ck("cdh", c), ck("cd", c), -1344.0, None, OP.add)
+        group(KA(c, 128, 256), clean_q(t, c, "kn"))
+        if NSV:
+            act(ck("kvp", c), KA(c, 0, 128), AF.Copy)
+        if NSN:
+            act(ck("knp", c), KA(c, 128, 256), AF.Copy)
+        ts(cw("dk", c), SM(c, 168, 176), 2.5, 15 * S17, OP.is_ge, OP.mult)
+        tt(cw("nk16", c), cw("dk", c), SM(c, 160, 168), OP.add)
+
+    def stage_cmp(t, c):
+        kc = "kc%d" % c
+        a = NL * c
+        for e, db, ns, neg, lo in (("e1%d" % c, "da%d" % c, NSV, "kvp", 0), ("e2%d" % c, "db%d" % c, NSN, "knp", 128)):
+            out = SM(c, 384, 512) if lo == 0 else AC(c, 0, 128)
+            for b in range(ns // 4):
+                hi = 512 * (4 - b)
+                bk = nb_[0] % 2
+                nb_[0] += 1
+                for j in range(4):
+                    o = DB(bk, 128 * j, 128 * j + 128)
+                    mm(o, cb("i1"), A(kc, 12 - 4 * b + j, 2048, 16), True, False)
+                    mm(o, cb("im"), ck(neg, c), False, True)
+                act(A(db, hi - 512, hi), DB(bk, 0, 512), AF.Copy)
+                if b % EQB == EQB - 1:
+                    w = 512 * EQB
+                    ts(A(e, hi - 512, hi - 512 + w), A(db, hi - 512, hi - 512 + w), 0.0, None, OP.is_equal)
+            mm(out, cb("i1"), ck("cdh", c), True, False)
+            mm(out, cb("i1"), cb("kb"), False, False)
+            for k in range(16):
+                ek = A(e, 128 * k, 128 * k + 128)
+                if k < 16 - ns:
+                    tt(ek, A(kc, k, 2048, 16), KA(c, lo, lo + 128), OP.is_equal)
+                mm(out, U("u17", k), ek, False, k == 15)
+            if lo == 0:
+                cp(ck("av", c), out)
+        act(ck("kvr", c), KA(c, 0, 128), AF.Relu)
+        tt(ck("val", c), ck("av", c), AC(c, 0, 128), OP.min)
+        tr(ck("vt", c), ck("val", c))
+        scan(ck("sc", c), A("mxm", 0, 128), ck("vt", c), OP.min, OP.max)
+        tt(cw("tot", c), A("sc", a + 15, a + NL, 16), cw("nk16", c), OP.max)
+        big = 1.5 * 2 ** 35
+        ts(cw("th", c), cw("tot", c), big, -big, OP.add, OP.add)
+        tt(cw("w16", c), cw("tot", c), cw("th", c), OP.subtract)
+        ts(cw("fl", c), cw("tot", c), 350000.0 - 2.5 * S17, None, OP.is_lt)
+        sm = "ps%d" % (4 + c)
+        l2wrap((sm, 136, 144), ("w16", 8 * c, 8 * c + 8))
+        l2wrap((sm, 144, 152), ("fl", 8 * c, 8 * c + 8))
+        ts(cw("wl%d" % t, c), SM(c, 136, 144), 1344.0, None, OP.add)
+        cp(A("wfl%d" % (t & 1), 16 * c, 16 * c + 16), SM(c, 136, 152))
+
+    def stage_w(t, c):
+        a = NL * c
+        cp(ck("kw", c), ind(tabw(t), cw("wl%d" % t, c)))
+        prs = [(cb("i1"), ck("kw", c))]
+        if t >= 1:
+            ra = A("ra%d" % (t - 1), 3, 4)
+            ts(ck("qa", c), ck("kw", c), ra, ra, OP.is_equal, OP.mult)
+            prs.append((cb("im"), ck("qa", c)))
+        if t >= 2:
+            rb = A("rb0", 0, 1)
+            ts(ck("qb", c), ck("kw", c), rb, rb, OP.is_equal, OP.mult)
+            prs.append((cb("im"), ck("qb", c)))
+        kw = SM(c, 0, 128)
+        group(kw, prs)
+        tt(ck("pi", c), ck("v2", c), kw, OP.mult)
+        ts(ck("pj", c), ck("pi", c), col(8), float(4 * t), OP.add, OP.add)
+        ts(ck("pk", c), ck("pj", c), 2, PL - 1, OP.arith_shift_right, OP.bitwise_and)
+        cp(ck("pl", c), ck("pk", c))
+        for s in range(SUBX):
+            act(A("xc%d" % c, 2048 // SUBX * s, 2048 // SUBX * (s + 1)),
+                ind(A("X", 0, PL), A("pl", a + 128 // SUBX * s, a + 128 // SUBX * (s + 1))))
+        tt(ck("pz", c), ck(zbuf(t), c), kw, OP.mult)
+        act(ck("kwc", c), kw, AF.Copy)
+        act(ck("hb", c), ck("kwc", c), AF.Relu, scale=-BIG, bias=col(16))
+        for q in range(16):
+            mm(SM(c, 256 + q, 512, 16), cb("rq", 128 * q, 128), A("wfl%d" % (t & 1), 16 * c, 16 * c + 16), True, True)
+        act(ck("flr", c), SM(c, 384, 512), scale=-512.0)
+        if t < NR - 1:
+            act(ck("v2", c), SM(c, 256, 384), scale=2.0, bias=2689.0)
+            vr = ck("wrp%d" % (t & 1), c)
+            act(vr, SM(c, 256, 384), AF.Copy)
+            tt(ck("wm", c), vr, AC(c, 128, 256), OP.mult)
+
+    def stage_full(t):
+        ts(fu("dr"), fu("tot"), 2.2e6 - 2.5 * S17, 2048.0, OP.is_gt, OP.mult)
+        group(F1(0, 16), [(cb("lt"), fu("fl"))]
+              + [(cb("on"), A("fl", 0, 16 - 2 * d), F1(2 * d, 16)) for d in range(1, 8)]
+              + [(cb("i1k"), fu("fl")), (cb("i1"), fu("dr"))])
+        ts(fu("iah"), F1(0, 16), 1024.0 + CAP + 0.5, 16384.0, OP.is_gt, OP.mult)
+        vprev = "wfl%d" % ((t + 1) & 1)
+
+        def node(lo):
+            return [(cb("i1"), cb("c13"))] + [(cb("i1"), A(vprev, 16 * c, 16 * c + 8), F1(lo + 8 * c, lo + 8 * c + 8))
+                                              for c in range(NC)] + l2p(("ps1", 384 + lo, 400 + lo), ("iah", 0, 16))
+        group(F1(64, 80), [(A("u1f", 15 - q, 143 - q), A("pz", q, L, 16)) for q in range(16)])
+        zs = 1.0 if t == 0 else 2.0
+        big = 1.5 * 2 ** 34 * zs
+        ts(fu("hH"), F1(64, 80), big, -big, OP.add, OP.add)
+        tt(fu("h2"), F1(64, 80), fu("hH"), OP.subtract)
+        ts(fu("sl2"), fu("h2"), 1.0 / zs, 1024.0, OP.mult, OP.add)
+        tab = "tab%d" % (t + 1)
+        act(A("src", 0, L), ind(A("rem%d" % t, 0, H + 1), fu("sl2")))
+        if t < NR - 1:
+            ones = [(cb("ones"), A("fl", j, j + 1)) for j in range(16)]
+            group(F1(16, 17), ones)
+            group(F1(17, 18), ones + [(cb("i1"), cb("c75", 0, 1))])
+            b27 = 1.5 * 2 ** 27
+            ts(A("fs", 2, 3), F1(17, 18), b27, -b27, OP.add, OP.add)
+            tt(A("fs", 3, 4), F1(16, 17), A("fs", 2, 3), OP.subtract)
+        if t > 0:
+            group(F1(48, 64), node(48))
+            act(fu("vb"), F1(48, 64), bias=-1344.0)
+            ts(fu("vah"), F1(48, 64), -1344.0, None, OP.add)
+            vr = "wrp%d" % ((t - 1) & 1)
+            group(KA(0, 0, 256), [(cb("i1"), cb("tri"))]
+                  + [(cb("i1"), fu("vah"), KA(0, q, 256, 16)) for q in range(16)])
+            o = 0
+            prs = [(cb("bo1"), A("ed", 0, L))]
+            for c1 in range(15):
+                n = L - 16 * (c1 + 1)
+                if c1 < E3S:
+                    act(A("e3", o, o + n), A(vr, L - n, L), scale=-1.0, bias=A("vb", c1, c1 + 1))
+                    oe = o + n
+                else:
+                    ts(A("e3", o, o + n), A(vr, L - n, L), A("vb", c1, c1 + 1), None, OP.is_equal)
+                prs.append((cb("bo1"), A("e3", o, o + n), KA(1, 256 - n, 256)))
+                o += n
+            tt(A("ed", 0, L), A(vr, 0, L), KA(0, 0, 256), OP.is_equal)
+            if E3S:
+                ts(A("e3", 0, oe), A("e3", 0, oe), 0.0, None, OP.is_equal)
+            group(KA(1, 0, 256), prs)
+            act(A("cnb", 0, L), KA(1, 0, 256), AF.Copy)
+            group(F1(80, 96), node(80) + [(U("u17", q), A("cnb", q, L, 16)) for q in range(16)])
+        else:
+            group(F1(80, 96), node(80))
+        tt(fu("sy"), fu("dum"), F1(80, 96), OP.min)
+        cp(fu("sl"), fu("sy"))
+        for c in range(NC):
+            o = SM(c, 256, 384)
+            for x in ("kwc", "src"):
+                mm(o, cb("i1"), ck(x, c), True, False)
+                if x == "src" and t >= 1:
+                    ts(ck("sa", c), ck("src", c), A("rc%d" % (t - 1), 0, 1), A("rc%d" % (t - 1), 0, 1), OP.is_equal, OP.mult)
+                    mm(o, cb("im"), ck("sa", c), False, False)
+                if x == "src" and t >= 2:
+                    ts(ck("sb", c), ck("src", c), A("ra0", 0, 1), A("ra0", 0, 1), OP.is_equal, OP.mult)
+                    mm(o, cb("im"), ck("sb", c), False, False)
+                if x == "src":
+                    mm(o, cb("i1"), cb("m512"), False, False)
+                mm(o, cb("i1" if x == "kwc" else "im"), ck("flr", c), False, False)
+                mm(o, cb("i256"), ck("kvr", c), False, True)
+                tt(ck("f1" if x == "kwc" else "fi", c), ck("kvr" if x == "kwc" else "f1", c), o, OP.max)
+        cp(ind(A(tab, 0, REM), fu("sl")), A("fi", 0, L))
+        if t < NR - 1:
+            group(KA(0, 256, 512), [(cb("i1"), A("bv", 0, L)), (cb("im"), A("nm", 0, L)), (cb("i1"), A("wm", 0, L))])
+            act(A("bn", 0, L), KA(0, 256, 512), bias=1344.0)
+            cp(ind(A("nb", 0, REM), fu("sl")), A("bn", 0, L))
+            pushes(t + 1)
+            dma("y", A("tab%d" % (t + 2), 0, V), A(tab, 0, V), 2 * 128 * V)
+
+    def stage_d(t, c):
+        a = NL * c
+        z = ck(zbuf(t), c)
+        out = AC(c, 256, 384)
+        xc = "xc%d" % c
+        mm(out, cb("i1"), cb("pt"), True, False)
+        if NSB < 16:
+            mm(KA(c, 256, 384), cb("i1" if t == 0 else "ih"), z, True, True)
+            mm(out, cb("bv32" if t == 0 else "bv16"), z, False, False)
+        for b in range(NSB // 4):
+            bk = nb_[0] % 2
+            nb_[0] += 1
+            for j in range(4):
+                o = DB(bk, 128 * j, 128 * j + 128)
+                mm(o, cb("i1"), A(xc, 4 * b + j, 2048, 16), True, False)
+                mm(o, cb("im" if t == 0 else "imh"), z, False, True)
+            act(A("mx%d" % c, 512 * b, 512 * b + 512), DB(bk, 0, 512), AF.Abs)
+        for p in range(15, -1, -1):
+            mxp = A("mx%d" % c, 128 * p, 128 * p + 128)
+            if p >= NSB:
+                x = A(xc, p, 2048, 16)
+                mm(out, U("um32", p), x, False, False)
+                tt(mxp, x, KA(c, 256, 384), OP.max)
+            mm(out, U("u32" if p < NSB else "u64", p), mxp, False, p == 0)
+        tr(ck("dt", c), out)
+        scan(ck("ds", c), A("mnm", 0, 128), ck("dt", c), OP.max, OP.min)
+        b28 = 1.5 * 2 ** 28
+        last = A("ds", a + 15, a + NL, 16)
+        ts(cw("pH", c), last, b28, -b28, OP.add, OP.add)
+        tt(cw("p16", c), last, cw("pH", c), OP.subtract)
+        group(SM(c, 152, 160), [(cb("i1"), A("pc", 0, 8))] + l2p(("ps%d" % (4 + c), 152, 160), ("p16", 8 * c, 8 * c + 8)))
+        cp(cw("pw", c), SM(c, 152, 160))
+        tt(ck("sz", c), ind(A(xc, 0, 2048), cw("pw", c)), ck("zs", c), OP.add)
+        b24 = 1.5 * 2 ** 24
+        if t < NR - 1:
+            ts(ck("zb", c), ck("sz", c), b24, -b24, OP.add, OP.add)
+        else:
+            ts(ck("xm", c), ck("sz", c), b24, -b24, OP.add, OP.add)
+            act(ck("yzf", c), ck("xm", c), AF.Copy, scale=0.5)
+            dma("y", hbm("yz", a, a + NL), ck("yzf", c), 512 * NL)
+        tc = col(23) if t == 0 else A("fs", 4 + t, 5 + t)
+        act(ck("ug", c), out, AF.Relu, scale=BIG, bias=tc)
+        group(SM(c, 0, 128), [(cb("i1"), ck("kwc", c)), (cb("i1"), cb("io", a, NL)), (cb("i1"), ck("hb", c)),
+                              (cb("i1"), ck("ug", c))])
+        red(A("rr", c, c + 1), SM(c, 0, 128), OP.min)
+
+    BL = ((0, H), (H, V))
+
+    def clean(tab, frm, nm, acc):
+        bon[0] = -CLB
+        for lo, hi in BL:
+            ts(A(nm, lo, hi), A(frm, lo, hi), acc[0], acc[1], OP.is_equal, OP.mult)
+        for lo, hi in BL:
+            dma("g", A(tab, lo, hi), A(nm, lo, hi), 2 * 128 * (hi - lo) * 2, add=True)
+        bon[0] = 0.0
+
+    def stage_rv(t):
+        ra = "ra%d" % t
+        tt(A("rr", 2, 3), A("rr", 0, 1), A("rr", 1, 2), OP.min)
+        ts(A("rr", 2, 3), A("rr", 2, 3), BIG, None, OP.min)
+        b32 = 1.5 * 2 ** 32
+        ts(A("rr", 3, 4), A("rr", 2, 3), b32, -b32, OP.add, OP.add)
+        tt(A(ra, 0, 1), A("rr", 2, 3), A("rr", 3, 4), OP.subtract)
+        if t < NR - 1:
+            ts(A(ra, 1, 2), A(ra, 0, 1), 1.0, None, OP.add)
+            rb = "rb%d" % t
+            if t == 1:
+                tt(A("rr", 4, 5), A(ra, 0, 1), A("rb0", 0, 1), OP.not_equal)
+                tt(A(ra, 3, 4), A("rr", 4, 5), A(ra, 0, 1), OP.mult)
+            else:
+                cp(A(ra, 3, 4), A(ra, 0, 1))
+            ts(A(ra, 2, 3), A(ra, 3, 4), -1.0, None, OP.mult)
+            clean("tab%d" % (t + 2), "tab%d" % (t + 1), "cln", (A(ra, 3, 4), A(ra, 2, 3)))
+            remote(nxt, A(ra, 0, 2), A(rb, 0, 2), prv, "rvs%d" % t, "rvl%d" % t, 1024)
+            remote(prv, A(ra, 0, 2), A("rc%d" % t, 0, 2), nxt, "rws%d" % t, "rwl%d" % t, 1024)
+            ts(A(rb, 2, 3), A(rb, 0, 1), -1.0, None, OP.mult)
+        else:
+            tt(A("rr", 4, 5), A(ra, 0, 1), A("rb1", 0, 1), OP.not_equal)
+            tt(A("rr", 5, 6), A("rr", 4, 5), A(ra, 0, 1), OP.mult)
+            ts(A("rr", 6, 7), A("rr", 5, 6), -1.0, None, OP.mult)
+            for i in range(7):
+                lo, hi = 384 * i, 384 * i + 384
+                ts(A("cln", lo, hi), A("tab3", lo, hi), A("rr", 5, 6), A("rr", 6, 7), OP.is_equal, OP.mult)
+                o = A("ps%d" % (6, 7, 2, 3)[i % 4], 0, 384)
+                group(o, [(cb("i1"), A("tab3", lo, hi)), (cb("i1"), A("clb", lo, hi)), (cb("i1"), A("cln", lo, hi))])
+                if i % 2:
+                    cp(A("fin", lo, hi), o)
+                else:
+                    act(A("fin", lo, hi), o, AF.Copy)
+            for q, lo, hi in (("y", 0, 768), ("s", 768, 1536), ("y", 1536, 2304), ("s", 2304, V)):
+                dma(q, hbm("yk", lo, hi), A("fin", lo, hi), 256 * (hi - lo))
+
+    stages = {"v": stage_v, "n": stage_n, "c": stage_cmp, "w": stage_w, "d": stage_d}
+
+    def st(f, t, c):
+        bon[0] = BT[f][c]
+        stages[f](t, c)
+        bon[0] = 0.0
+
+    for t in range(NR):
+        for c in range(NC):
+            st("v", t, c)
+            st("n", t, c)
+        for c in range(NC):
+            st("c", t, c)
+            st("w", t, c)
+        bon[0] = BT["f"][0]
+        stage_full(t)
+        bon[0] = 0.0
+        if t == 1:
+            clean("tab3", "tab2", "clb", (A("rb0", 0, 1), A("rb0", 2, 3)))
+        if t == 2:
+            bon[0] = -CLB
+            for lo, hi in BL:
+                ts(A("clb", lo, hi), A("tab3", lo, hi), A("rb1", 0, 1), A("rb1", 2, 3), OP.is_equal, OP.mult)
+            bon[0] = 0.0
+        for c in range(NC):
+            st("d", t, c)
+        if t < NR - 1:
+            ts(A("fs", 5 + t, 6 + t), A("fs", 3, 4), -32.0 * BIG, col(23), OP.mult, OP.add)
+        stage_rv(t)
+    _emit(g, T, ops)
+
+
+def _emit(g, T, ops):
+    n = len(ops)
+    succ = [[] for _ in range(n)]
+    for i, o in enumerate(ops):
+        if "after" in o:
+            o["deps"][o["after"]] = False
+        for j in o["deps"]:
+            succ[j].append(i)
+    prio = [0.0] * n
+    for i in range(n - 1, -1, -1):
+        o = ops[i]
+        prio[i] = o["dur"] + o["lat"] + max([prio[s] for s in succ[i]], default=0.0)
+    prio = [p + o["bon"] for p, o in zip(prio, ops)]
+    left = [len(o["deps"]) for o in ops]
+    fin = [0.0] * n
+    qfree, ready, order = {}, {}, []
+    est = [0.0] * n
+
+    def push(i):
+        o = ops[i]
+        e = 0.0
+        for j, hard in o["deps"].items():
+            if "after" in o and j == o["after"]:
+                e = max(e, fin[j])
+            elif hard:
+                e = max(e, fin[j] + WK)
+        est[i] = e
+        ready.setdefault(o["q"], []).append(i)
+    for i in range(n):
+        if left[i] == 0:
+            push(i)
+    while len(order) < n:
+        best = None
+        for q, rs in ready.items():
+            if not rs:
+                continue
+            f = 0.0 if q == "ext" else qfree.get(q, 0.0)
+            t0 = max(f, min(est[i] for i in rs))
+            if best is None or t0 < best[0]:
+                best = (t0, q)
+        t0, q = best
+        rs = ready[q]
+        i = max([i for i in rs if est[i] <= t0 + 30.0], key=lambda k: (prio[k], -k))
+        rs.remove(i)
+        o = ops[i]
+        st = max(t0, est[i])
+        qfree[q] = st + o["dur"]
+        fin[i] = st + o["dur"] + o["lat"]
+        order.append(i)
+        for s in succ[i]:
+            left[s] -= 1
+            if left[s] == 0:
+                push(s)
+    eng = {"v": g.vector, "s": g.scalar, "p": g.tensor, "g": g, "y": g.sync}
+    known = {q: {} for q in eng}
+    count, semof, clock = {}, {}, {}
+    pos = {i: k for k, i in enumerate(order)}
+    for i in order:
+        o = ops[i]
+        q = o["q"]
+        if q == "ext":
+            semof[i] = (o["sem"], o["val"])
+            count[o["sem"]] = o["val"]
+            clock[i] = {o["sem"]: o["val"]}
+            continue
+        kn = known[q]
+        need = {}
+        for j in sorted([j for j, hard in o["deps"].items() if hard], key=lambda j: -pos[j]):
+            s, v = semof[j]
+            if kn.get(s, 0) >= v:
+                continue
+            need[s] = max(need.get(s, 0), v)
+            for s2, v2 in clock[j].items():
+                if kn.get(s2, 0) < v2:
+                    kn[s2] = v2
+        for s, v in need.items():
+            eng[q].wait_ge(T.sem[s], v)
+        r = o["call"]()
+        s = "q" + q if o["sem"] is None else o["sem"]
+        count[s] = count.get(s, 0) + o["val"]
+        if "remote" not in o:
+            r.then_inc(T.sem[s], o["val"])
+        semof[i] = (s, count[s])
+        clock[i] = dict(kn)
+        clock[i][s] = count[s]
+    for s, v in count.items():
+        if known["g"].get(s, 0) < v:
+            g.wait_ge(T.sem[s], v)

@@ -5,32 +5,28 @@ AF = ActivationFunctionType
 V, PL, L, NR, H = 2688, 4096, 256, 3, 2048
 REM = V + L
 NC, NL = 2, 128
+MID = 1344.0
 S17 = float(2 ** 17)
 BIG = float(2 ** 20)
-CYC, PEC, VF, SF, WK, GA, SCA = 0.83, 0.42, 80.0, 100.0, 60.0, 1.5, 3.0
-CLB = 15000.0
-BT = {"v": (0.0, 0.0), "n": (1700.0, 0.0), "c": (2000.0, 0.0), "w": (8800.0, 600.0), "d": (3800.0, 700.0), "f": (0.0,)}
+TINY = 2.0 ** -60
 CAP = 64
-NSB, E3S = 16, 0
-NSV, NSN, EQB, SUBK, SUBX = 0, 16, 1, 2, 2
+REP = 4
+CYC, PEC, VF, SF, PF, WK, GA, SCA = 0.9, 0.46, 60.0, 60.0, 8.0, 70.0, 1.55, 3.0
+LZ, LN, LR, LX = 4000.0, 10000.0, 12000.0, 6000.0
+BT = {"k": 200000.0, "v": (0.0, 0.0), "n": (1500.0, 0.0), "h": (0.0, 0.0), "c": (2000.0, 0.0), "w": (2000.0, 0.0),
+      "f": (0.0, 0.0), "d": (2000.0, 0.0), "e": -3000.0, "cl": 0.0}
+ENG = {"kn": "v", "kw": "s", "kv": "s", "fl": "s"}
+SUBK, SUBX, CLP = 2, 2, 3
 CBN = {}
 ALIAS = {}
 SCRATCH = {}
 
 
-def _lay(d, names):
+def _pack(big, dtype, names):
     o = 0
     for nm, w in names:
-        d[nm] = (o, o + w)
-        o += w
-    return o
-
-
-def _small(big, dtype, names):
-    o = 0
-    for nm in names:
         ALIAS[nm] = (big, o)
-        o += 32 if nm[:3] == "wfl" else 16
+        o += w
     SCRATCH[big] = ("sbuf", [128, o], dtype)
 
 
@@ -39,36 +35,38 @@ def _bufs(dtype, width, names):
         SCRATCH[nm] = ("sbuf", [128, width], dtype)
 
 
-CBW = _lay(CBN, [("u17", 144), ("u32", 144), ("u1", 144), ("bo1", 128), ("boh", 128), ("i1", 128),
-                 ("im", 128), ("imh", 128), ("i256", 128), ("i1k", 128), ("kb", 128), ("pt", 128), ("io", 256), ("tri", 256),
-                 ("on", 128), ("lt", 128), ("ones", 128), ("sl", 512), ("rq", 2048), ("c13", 16), ("c75", 2),
-                 ("m512", 128), ("ih", 128), ("u64", 144), ("um32", 144), ("bv16", 128), ("bv32", 128)])
-_bufs("bfloat16", REM, ("tab0", "tab1", "tab2", "tab3"))
+_pack("cb", "bfloat16", [(x, 128) for x in ("i1", "im", "ih", "iq", "bo1", "i1k", "lt", "ones", "i3", "im69", "i256",
+                                            "i512", "pt", "yc0", "yc1", "yc2")]
+      + [("u1", 144), ("i18", 144), ("ksc", 288), ("tiny", 512), ("io", 256), ("rx", 1024), ("rxi", 1024), ("axc", 64),
+         ("sv", 8), ("se", 8), ("sd", 16), ("c69", 8), ("c75", 8)])
+_pack("cf", "float32", [("row", 256), ("jr", 128), ("j18", 144), ("m16", 128), ("mxm", 144), ("mnm", 128), ("pw2", 176),
+                        ("half", 176), ("zero", 176), ("wt", 64), ("g8", 64), ("b8f", 8), ("ew", 128), ("efn", 128), ("efp", 128),
+                        ("on32", 128), ("tmp", 128), ("col", 48)])
+_pack("ch", "float16", [("thrb", 128), ("dumc", 16), ("pc", 8)])
+PADW = 272 + 3 * 144
+_pack("pad", "float16", [(x + str(c), w) for c in range(NC) for x, w in (("padw", 272), ("padh", 144), ("padn", 144), ("padp", 144))])
+_pack("padb", "bfloat16", [("pada0", 144), ("pada1", 144), ("fl0", 16), ("fl1", 16)])
+_bufs("bfloat16", REM, ("tab0", "tab2", "tab3"))
 _bufs("bfloat16", H + 16, ("rem0", "rem1", "rem2"))
-_bufs("bfloat16", H, ("kc0", "kc1", "e10", "e11", "e20", "e21", "xc0", "xc1", "mx0", "mx1", "da0",
-                      "da1", "db0", "db1"))
-_bufs("bfloat16", V, ("cln", "clb", "fin"))
-_bufs("bfloat16", L, ("zi", "zb", "kv", "kn", "q0", "qa", "qb", "e0", "kw", "kwc", "src", "sa", "sb", "f1", "hb", "ug",
-                      "flr", "nfr", "kvr", "knp", "kvp", "fi", "ed", "cnb"))
-_bufs("float16", L, ("bv", "nm", "cdh", "wm"))
-_bufs("float16", 8, ("pc",))
-_bufs("float32", L, ("wrp0", "wrp1", "row", "jr", "tmpc", "av", "val", "vt", "sc", "v2", "pz", "dt", "ds", "xm", "sz", "zs", "bn", "yzf"))
-_bufs("float32", 128, ("m32", "mxm", "mnm"))
-_bufs("int32", L, ("yi", "yj", "pi", "pj", "pk"))
+_bufs("bfloat16", H, ("e10", "e11", "e20", "e21", "xc0", "xc1", "mx0", "mx1", "kc0", "kc1"))
+_bufs("bfloat16", V, ("cln", "clc", "fin"))
+_bufs("bfloat16", L, ("zi", "zb", "e0", "kw", "kwc", "qw", "qx", "src", "sa", "sb", "f1", "r2", "qc", "hb", "ug", "kvr", "xs"))
+_bufs("bfloat16", 2 * L, ("kvn", "qa", "qb"))
+_bufs("float16", L, ("bv", "nm", "cdh", "wm", "vr0", "vr1"))
+_bufs("float32", L, ("r16", "pz", "v2", "ds", "bn", "yzf", "wT"))
+_bufs("float32", 288, ("sc", "ad", "val"))
+_bufs("int32", L, ("pi", "pj", "pk"))
 _bufs("uint16", L, ("cd", "pl"))
 _bufs("float32", 4, ("ra0", "ra1", "ra2", "rb0", "rb1", "rc0", "rc1"))
-_bufs("float32", 8, ("fs", "rr"))
+_bufs("float32", 16, ("fs", "rr"))
 _bufs("int32", 8, ("ipc",))
-_small("smu", "uint16", ("nl", "pw", "sl2", "sl", "wl0", "wl1", "wl2"))
-_small("sm32", "float32", ("dk", "nk16", "tot", "th", "hH", "h2", "vb", "sy", "pH", "dum", "v0w"))
-_small("sm16", "float16", ("w16", "fl", "dr", "iah", "vah", "p16", "wfl0", "wfl1"))
+_pack("smu", "uint16", [(x, 16) for x in ("nl", "pw", "hl", "sl", "wl0", "wl1", "wl2")])
+_pack("sm32", "float32", [(x, 16) for x in ("hH", "sy", "pH", "v320", "v321")])
+_pack("smb", "bfloat16", [("th", 16), ("rw", 128), ("rw2", 64)])
 SCRATCH["nb"] = ("sbuf", [128, REM], "int32")
-SCRATCH["X"] = ("sbuf", [128, PL], "bfloat16")
+SCRATCH["X"] = ("sbuf", [128, 2 * PL], "bfloat16")
 SCRATCH["thi"] = ("sbuf", [128, 1], "int32")
-SCRATCH["cb"] = ("sbuf", [128, CBW], "bfloat16")
-SCRATCH["u1f"] = ("sbuf", [128, 144], "float32")
-SCRATCH["col"] = ("sbuf", [128, 64], "float32")
-SCRATCH["e3"] = ("sbuf", [128, 1920], "bfloat16")
+SCRATCH["e3"] = ("sbuf", [128, 3072], "bfloat16")
 for _b in range(8):
     SCRATCH["ps%d" % _b] = ("psum", [128, 512], "float32")
 SEMAPHORES = ["qv", "qs", "qp", "qg"] + ["d%d" % i for i in range(40)] \
@@ -83,19 +81,18 @@ def rank_program(g, core, T, topo):
     nxt, prv = T.cores[(rank + 1) % nranks], T.cores[(rank - 1) % nranks]
     ops, hist, ndma, bon, nb_ = [], {}, [0], [0.0], [0]
 
-    def A(name, lo, hi, st=1):
+    def A(name, lo=0, hi=None, st=1, parts=None):
         if name in ALIAS:
-            name, o = ALIAS[name]
-            lo, hi = lo + o, hi + o
-        ap = T[name][:, lo:hi] if st == 1 else T[name][:, lo:hi:st]
+            big, o = ALIAS[name]
+            if hi is None:
+                later = [x[1] for x in ALIAS.values() if x[0] == big and x[1] > o]
+                hi = min(later + [SCRATCH[big][1][1]]) - o
+            name, lo, hi = big, lo + o, hi + o
+        elif hi is None:
+            hi = SCRATCH[name][1][1]
+        rows = slice(0, 128 if parts is None else parts)
+        ap = T[name][rows, lo:hi] if st == 1 else T[name][rows, lo:hi:st]
         return ([(name, lo, hi)], ap, (hi - lo + st - 1) // st)
-
-    def cb(nm, lo=0, w=None):
-        o, e = CBN[nm]
-        return A("cb", o + lo, e if w is None else o + lo + w)
-
-    def U(nm, q):
-        return cb(nm, 15 - q, 128)
 
     def ind(win, lst):
         return (win[0] + lst[0], win[1].indirect(lst[1]), 16 * lst[2], 1)
@@ -105,31 +102,30 @@ def rank_program(g, core, T, topo):
         deps = {}
         for regs, w in ((rd, 0), (wr, 1)):
             for nm, lo, hi in regs:
-                if nm[:2] == "ps":
-                    for q2, j in hist.get(nm, {}).items():
-                        if j != i:
-                            deps[j] = deps.get(j, False) or q2 != q or q != "p"
-                else:
-                    for j, l2, h2, w2 in hist.get(nm, []):
-                        if j != i and l2 < hi and lo < h2 and (w or w2):
-                            deps[j] = True
+                for j, l2, h2, w2 in hist.get(nm, []):
+                    if j != i and l2 < hi and lo < h2 and (w or w2):
+                        own = ops[j]["q"] == q and sem is None and ops[j]["sem"] is None
+                        soft = own and q == "p"
+                        deps[j] = deps.get(j, False) or not soft
         for regs, w in ((rd, 0), (wr, 1)):
             for nm, lo, hi in regs:
-                if nm[:2] == "ps":
-                    hist.setdefault(nm, {})[q] = i
-                else:
-                    a = hist.setdefault(nm, [])
-                    if w:
-                        a[:] = [e for e in a if e[0] == i or not (lo <= e[1] and e[2] <= hi)]
-                    a.append((i, lo, hi, w))
-        ops.append({"q": q, "dur": dur, "deps": deps, "call": call, "sem": sem, "val": val, "lat": lat, "bon": bon[0]})
+                a = hist.setdefault(nm, [])
+                if w:
+                    a[:] = [e for e in a if e[0] == i or not (lo <= e[1] and e[2] <= hi)]
+                a.append((i, lo, hi, w))
+        banks = sorted(set(x[0] for x in rd + wr if x[0][:2] == "ps"))
+        ops.append({"q": q, "dur": dur, "deps": deps, "call": call, "sem": sem, "val": val, "lat": lat, "bon": bon[0],
+                    "banks": banks})
         return i
+
+    def dt(x):
+        return SCRATCH[x[0][0][0]][2]
 
     def vdur(n, f):
         return max(64.0, n * f) * CYC + VF
 
     def two(*xs):
-        return all(SCRATCH[x[0][0][0]][2] in ("bfloat16", "float16", "uint16") for x in xs)
+        return all(dt(x) in ("bfloat16", "float16", "uint16") for x in xs)
 
     def sc_(x):
         return (x[1], x[0]) if isinstance(x, tuple) else (x, [])
@@ -146,48 +142,62 @@ def rank_program(g, core, T, topo):
                 return g.vector.tensor_scalar(out[1], a[1], x1, x2, o0, o1)
         return op("v", vdur(a[2], f), a[0] + r1 + r2, out[0], call)
 
+    def rnd(out, a, m):
+        big = 1.5 * 2.0 ** (23 + m)
+        return ts(out, a, big, -big, OP.add, OP.add)
+
     def tt(out, a, b, o):
         ps = a[0][0][0][:2] == "ps" or b[0][0][0][:2] == "ps"
-        return op("v", vdur(b[2], GA if len(a) > 3 else 1.0 if ps else 2.0), a[0] + b[0], out[0],
+        f = SCA if len(out) > 3 else GA if len(a) > 3 else 1.0 if ps else 2.0
+        return op("v", vdur(b[2], f), a[0] + b[0] + out[0][1:], out[0][:1],
                   lambda: g.vector.tensor_tensor(out[1], a[1], b[1], o))
 
     def cp(out, a):
         f = SCA if len(out) > 3 else GA if len(a) > 3 else (0.5 if two(out, a) else 1.0)
-        wr = out[0][:1] if len(out) > 3 else out[0]
-        rd = a[0] + (out[0][1:] if len(out) > 3 else [])
-        return op("v", vdur(a[2], f), rd, wr, lambda: g.vector.tensor_copy(out[1], a[1]))
+        return op("v", vdur(a[2], f), a[0] + out[0][1:], out[0][:1], lambda: g.vector.tensor_copy(out[1], a[1]))
 
     def red(out, a, o):
         return op("v", vdur(a[2], 1.0), a[0], out[0], lambda: g.vector.tensor_reduce(out[1], a[1], AxisListType.X, o))
 
-    def scan(out, d0, d1, o0, o1):
+    def scan(out, d0, d1, o0, o1, init=0.0):
         return op("v", vdur(d1[2], 1.0), d0[0] + d1[0], out[0],
-                  lambda: g.vector.tensor_tensor_scan(out[1], d0[1], d1[1], 0.0, o0, o1))
-
-    def tr(out, a):
-        return op("v", vdur(a[2], 1.0), a[0], out[0], lambda: g.vector.transpose(out[1], a[1]))
+                  lambda: g.vector.tensor_tensor_scan(out[1], d0[1], d1[1], init, o0, o1))
 
     def fill(out, c):
         return op("v", vdur(out[2], 0.5), [], out[0], lambda: g.vector.memset(out[1], c))
 
-    def act(out, a, func=None, scale=1.0, bias=0.0):
+    def act(out, a, func=None, scale=1.0, bias=0.0, acc=None):
         x, r = sc_(bias)
         y, r2 = sc_(scale)
         fn = AF.Identity if func is None else func
-        return op("s", a[2] * (GA if len(a) > 3 else 1.0) * CYC + SF, a[0] + r + r2, out[0],
-                  lambda: g.scalar.activation(out[1], a[1], fn, bias=x, scale=y))
+        if acc is None:
+            def call():
+                return g.scalar.activation(out[1], a[1], fn, bias=x, scale=y)
+        else:
+            def call():
+                return g.scalar.activation(out[1], a[1], fn, bias=x, scale=y, accum_out=acc[1])
+        return op("s", a[2] * (GA if len(a) > 3 else 1.0) * CYC + SF, a[0] + r + r2, out[0] + (acc[0] if acc else []), call)
 
-    def mm(out, lhsT, rhs, start, stop):
-        f = 4 if SCRATCH[rhs[0][0][0]][2] == "float32" else 1
-        return op("p", max(min(64.0, lhsT[2]), rhs[2]) * f * PEC, lhsT[0] + rhs[0], out[0],
-                  lambda: g.tensor.matmul(out[1], lhsT[1], rhs[1], start, stop))
+    def take(who, out, a):
+        return cp(out, a) if ENG[who] == "v" else act(out, a)
 
-    def group(out, pairs):
-        for i, pr in enumerate(pairs):
-            mm(pr[2] if len(pr) > 2 else out, pr[0], pr[1], i == 0, i == len(pairs) - 1)
+    def mms(out, pairs, start=True, stop=True, tok=None):
+        prs = [(p[2] if len(p) > 2 else out, p[0], p[1]) for p in pairs]
+        dur = sum(max(min(64.0, a[2]), b[2]) * (4 if dt(b) == "float32" else 1) * PEC + PF for o, a, b in prs)
+        rd = [r for o, a, b in prs for r in a[0] + b[0]]
+        wr = [r for o, a, b in prs for r in o[0]]
+        if tok is not None:
+            (rd if tok[0] == "r" else wr).append(("tok%d" % tok[1], 0, 1))
+
+        def call():
+            r = None
+            for i, (o, a, b) in enumerate(prs):
+                r = g.tensor.matmul(o[1], a[1], b[1], start and i == 0, stop and i == len(prs) - 1)
+            return r
+        return op("p", dur, rd, wr, call)
 
     def iota(out, pat, base, mul):
-        if SCRATCH[out[0][0][0]][2] != "int32":
+        if dt(out) != "int32":
             def call():
                 return g.iota(out[1], pat, base, mul, allow_small_or_imprecise_dtypes=True)
         else:
@@ -195,18 +205,18 @@ def rank_program(g, core, T, topo):
                 return g.iota(out[1], pat, base, mul)
         return op("g", 130 + 2 * out[2] * CYC, [], out[0], call)
 
-    def dma(q, out, a, nbytes, add=False, after=()):
+    def dma(q, out, a, nbytes, add=False, after=(), lat=None):
         s = "d%d" % ndma[0]
         ndma[0] += 1
         eng = {"y": g.sync, "s": g.scalar, "g": g}[q]
         if add:
             def call():
-                return eng.dma_start(out[1], a[1], accum_op=OP.add)
+                return eng.dma_start(out[1], a[1], accum_op=OP.add, max_dma_last_dim=4096)
         else:
             def call():
                 return eng.dma_start(out[1], a[1])
-        return op(q, 1000 if q == "g" else 60, a[0] + (out[0] if add else []) + [(x, 0, 1) for x in after], out[0], call, sem=s, val=16,
-                  lat=1900 + nbytes / 180.0)
+        return op(q, 1000 if q == "g" else 60, a[0] + (out[0] if add else []) + [(x, 0, 1) for x in after], out[0], call,
+                  sem=s, val=16, lat=1900 + nbytes / 200.0 if lat is None else lat)
 
     def hbm(name, lo, hi):
         return ([("hbm_" + name, lo, hi)], T[name][:, lo:hi], hi - lo)
@@ -221,426 +231,383 @@ def rank_program(g, core, T, topo):
         op("ext", 0, [], out[0], None, sem=rsem, val=len(topo.engines(frm, core)))
         ops[-1]["after"] = len(ops) - 2
 
-    def KA(c, lo, hi, st=1): return A("ps%d" % c, lo, hi, st)
-    def AC(c, lo, hi): return A("ps%d" % (2 + c), lo, hi)
-    def SM(c, lo, hi, st=1): return A("ps%d" % (4 + c), lo, hi, st)
-    def DB(b, lo, hi): return A("ps%d" % (6 + b), lo, hi)
-    def F1(lo, hi): return A("ps1", 384 + lo, 384 + hi)
-    def col(i): return A("col", i, i + 1)
+    def P(b, lo, hi, st=1, parts=None): return A("ps%d" % b, lo, hi, st, parts)
+    def SU(c, lo, hi, st=1, parts=None): return P(2 + c, lo, hi, st, parts)
+    def MI(c, lo, hi, st=1): return P(6 + c, lo, hi, st)
+    def col(i, w=1): return A("col", i, i + w)
     def ck(name, c): return A(name, NL * c, NL * c + NL)
     def cw(name, c): return A(name, 8 * c, 8 * c + 8)
-    def fu(name): return A(name, 0, 16)
-    def tabw(t): return A("tab%d" % t, 0, V)
+    TAB = ("tab0", "tab0", "tab2", "tab3")
+    def tabw(t): return A(TAB[t], 0, V)
     def zbuf(t): return "zi" if t == 0 else "zb"
+    def pad(nm, c): return A(nm + str(c), 15, 143, 16)
+    I1, IM = A("i1"), A("im")
+    B8 = A("bo1", 0, 128, 16)
 
-    dma("s", A("zi", 0, L), hbm("z0", 0, L), 2 * 128 * L)
-    dma("y", A("nb", 0, V), hbm("nbr", 0, V), 4 * 128 * V)
-    dma("s", A("tab0", 0, V), hbm("ring", 0, V), 2 * 128 * V)
-    dma("s", A("thi", 0, 1), hbm("thr", 0, 1), 512)
-    dma("y", A("X", 0, PL), hbm("mat", 0, PL), 2 * 128 * PL, after=("nb", "tab0"))
-    dma("y", A("tab1", 0, V), hbm("ring", 0, V), 2 * 128 * V, after=("X",))
+    def wrap(nm, c, sel="i1", n=8):
+        if n == 8:
+            return [(A(nm + str(c), 15 - q, 143 - q), A(sel, q, 128, 16)) for q in range(16)]
+        return [(A(nm + str(c), 15 - q, 143 - q), A(sel, n * q, n * q + n)) for q in range(16)]
 
+    dma("s", A("zi"), hbm("z0", 0, L), 0, lat=LZ)
+    dma("y", A("nb", 0, V), hbm("nbr", 0, V), 0, lat=LN)
+    dma("s", A("tab0", 0, V), hbm("ring", 0, V), 0, lat=LR)
+    dma("s", A("thi"), hbm("thr", 0, 1), 0, lat=LR)
+    dma("y", A("X", 0, PL), hbm("mat", 0, PL), 0, after=("nb", "tab0"), lat=LX)
+    dma("y", A("X", PL, 2 * PL), hbm("mat", 0, PL), 0, after=("X",), lat=LX)
+
+    bon[0] = BT["k"]
     iota(A("ipc", 0, 1), [[0, 1]], 0, 1)
-    iota(A("row", 0, 256), [[1, 256]], 0, 0)
-    iota(A("jr", 0, 256), [[0, 16], [1, 16]], 0, 0)
-    iota(A("m32", 0, 128), [[32, 4], [0, 32]], 0, 0)
-    iota(fu("dum"), [[16, 16]], V, 1)
-    iota(fu("v0w"), [[160, 16]], 0, 10)
-    iota(A("v2", 0, 256), [[20, 256]], 1, 0)
-    ip = A("ipc", 0, 1)
-    ts(A("ipc", 1, 2), ip, 15, None, OP.bitwise_and)
-    ts(A("ipc", 2, 3), ip, 96, None, OP.bitwise_and)
-    ts(A("ipc", 3, 4), ip, 4, 1, OP.logical_shift_right, OP.bitwise_and)
-    cp(A("col", 0, 2), A("ipc", 0, 2))
-    cp(A("col", 4, 6), A("ipc", 2, 4))
+    iota(A("row"), [[1, 256]], 0, 0)
+    iota(A("jr"), [[0, 8], [1, 16]], 0, 0)
+    iota(A("j18"), [[0, 8], [1, 18]], 0, 0)
+    iota(A("v320"), [[160, 16]], -int(MID), 10)
+    iota(A("v2"), [[20, 256]], 1, 0)
+    iota(A("g8"), [[0, 8], [16, 8]], 0, 0)
+    iota(A("io"), [[512, 256]], 0, 0)
+    iota(A("rxi"), [[1, 16], [16, 8], [0, 8]], 0, 0)
+    row128, row144, j128 = A("row", 0, 128), A("row", 0, 144), A("jr")
+    ts(A("ipc", 1, 2), A("ipc", 0, 1), 15, None, OP.bitwise_and)
+    cp(col(0, 2), A("ipc", 0, 2))
     tt(col(2), col(0), col(1), OP.subtract)
     ts(col(3), col(2), 15.0, None, OP.add)
-    ts(col(36), col(1), -1.0, 16.0, OP.mult, OP.add)
-    ts(col(8), col(1), 3244.0, None, OP.mult)
-    row128 = A("row", 0, 128)
-    row144 = A("row", 0, 144)
-    j128 = A("jr", 0, 128)
-    tt(A("tmpc", 0, 256), A("row", 0, 256), A("jr", 0, 256), OP.subtract)
-    m16 = A("tmpc", 0, 128)
-    ts(cb("i1"), row128, col(0), None, OP.is_equal)
-    act(cb("im"), cb("i1"), AF.Copy, scale=-1.0)
-    ts(cb("bo1"), m16, col(2), None, OP.is_equal)
-    ts(cb("u1"), row144, col(3), None, OP.is_equal)
-    act(cb("u17"), cb("u1"), AF.Copy, scale=S17)
-    ts(col(7), col(1), -4096.0, 61440.0 - 2.5 * S17, OP.mult, OP.add)
-    act(cb("kb"), row128, scale=0.0, bias=col(7))
-    ts(A("mxm", 0, 128), j128, 0.5, 2e9, OP.is_ge, OP.mult)
-    ts(A("mxm", 0, 128), A("mxm", 0, 128), -1e9, None, OP.add)
-    ts(col(12), col(5), 10000.0, col(0), OP.mult, OP.add)
-    ts(col(13), col(5), -10000.0, col(0), OP.mult, OP.add)
-    for g2 in range(2):
-        for c2 in range(2):
-            ts(cb("sl", 128 * (2 * g2 + c2), 128), row128, float(-16 * g2 if c2 == 0 else 16 * (1 - g2) - 10000), col(12 + c2),
-               OP.add, OP.is_equal)
-    act(cb("u32"), cb("u1"), AF.Copy, scale=32.0)
-    ts(col(6), col(1), -8.0, None, OP.add)
-    act(cb("pt"), row128, scale=0.0, bias=col(6))
-    act(A("mnm", 0, 128), A("mxm", 0, 128), AF.Copy, scale=-1.0)
-    iota(cb("io"), [[512, 256]], 0, 0)
-    fill(col(16), BIG)
-    ts(fu("dum"), fu("dum"), col(2), None, OP.subtract)
-    ts(col(17), col(2), -10.0, None, OP.mult)
-    ts(fu("v0w"), fu("v0w"), col(17), None, OP.add)
-    ts(A("pc", 0, 8), A("dum", 0, 8), 16.0, float(8 - 16 * V), OP.mult, OP.add)
-    act(A("u1f", 0, 144), cb("u1"), AF.Copy)
-    ts(cb("on"), A("m32", 0, 128), col(4), None, OP.is_equal)
-    ts(cb("lt"), row128, col(0), None, OP.is_ge)
-    tt(cb("lt"), cb("lt"), cb("on"), OP.mult)
-    act(cb("ones"), row128, scale=0.0, bias=1.0)
-    act(cb("c13"), A("row", 0, 16), scale=0.0, bias=1344.0)
-    if NSB < 16:
-        act(cb("ih"), cb("i1"), AF.Copy, scale=0.5)
-        act(cb("u64"), cb("u1"), AF.Copy, scale=64.0)
-        act(cb("um32"), cb("u1"), AF.Copy, scale=-32.0)
-        ts(cb("bv16"), j128, float(NSB), -16.0, OP.is_ge, OP.mult)
-        tt(cb("bv16"), cb("bv16"), cb("bo1"), OP.mult)
-        act(cb("bv32"), cb("bv16"), AF.Copy, scale=2.0)
-    act(cb("m512"), row128, scale=0.0, bias=-512.0)
-    act(cb("c75"), A("row", 0, 2), scale=0.0, bias=-7.5)
-    ts(A("col", 40, 56), A("jr", 0, 16), col(1), None, OP.is_equal)
-    for q in range(16):
-        act(cb("rq", 128 * q, 128), cb("bo1"), AF.Copy, scale=col(40 + q))
-    for c in range(NC):
-        ts(A("wfl1", 16 * c, 16 * c + 8), cw("v0w", c), -1344.0, None, OP.add)
-    act(A("wrp1", 0, L), A("v2", 0, L), scale=0.5, bias=-1344.5)
-    cp(col(18), A("thi", 0, 1))
-    ts(col(22), col(18), 32.0, col(6), OP.mult, OP.add)
-    ts(col(23), col(22), -BIG, BIG, OP.mult, OP.add)
-    act(cb("i1k"), cb("i1"), AF.Copy, scale=1024.0)
-    act(cb("imh"), cb("i1"), AF.Copy, scale=-0.5)
-    act(cb("i256"), cb("i1"), AF.Copy, scale=-256.0)
-    act(cb("boh"), cb("bo1"), AF.Copy, scale=0.5)
-    ts(cb("tri"), A("jr", 0, 256), col(1), 32768.0, OP.is_le, OP.mult)
+    ts(col(4), col(2), 0.125, col(0), OP.mult, OP.add)
+    tt(A("m16"), row128, j128, OP.subtract)
+    ts(I1, row128, col(0), None, OP.is_equal)
+    ts(A("bo1"), A("m16"), col(2), None, OP.is_equal)
+    ts(A("u1"), row144, col(3), None, OP.is_equal)
+    ts(A("i18"), row144, col(4), None, OP.is_equal)
+    for nm, s in (("im", -1.0), ("ih", 0.5), ("iq", -0.25), ("i1k", 1024.0), ("i3", 3.0 / 4096),
+                  ("im69", -2.0 ** 69), ("i256", -256.0), ("i512", -512.0)):
+        act(A(nm), I1, AF.Copy, scale=s)
+    for t in range(NR):
+        ts(col(5 + t), col(1), -1.0, float(16 + t), OP.mult, OP.add)
+        act(A("yc%d" % t), row128, scale=0.0, bias=col(5 + t))
+        ts(A("ipc", 2 + t, 3 + t), col(1), 811.0, float(t), OP.mult, OP.add)
+    ts(A("ipc", 5, 8), A("ipc", 2, 5), PL - 1, None, OP.bitwise_and)
+    cp(col(8, 3), A("ipc", 5, 8))
+    ts(col(11), col(8), 4.0, None, OP.mult)
+    for nm, lo, x in (("sv", 0, S17), ("se", 0, 17 * S17), ("sd", 0, 32.0), ("sd", 8, 1.0), ("b8f", 0, 1.0)):
+        act(A(nm, lo, lo + 8), B8, AF.Copy, scale=x)
+    for lo in (0, 144):
+        ts(A("ksc", lo, lo + 144), A("j18"), -4096.0, 15 * 4096 - 2.5 * S17, OP.mult, OP.add)
+    for lo, x in ((16, 0.0), (17, -35 * S17), (160, 0.0), (161, 16 * S17)):
+        ts(A("ksc", lo, lo + 127, 18), A("row", 0, 8), 0.0, x, OP.mult, OP.add)
+    ts(A("mxm"), A("j18"), 0.5, 2e9, OP.is_ge, OP.mult)
+    act(A("mxm"), A("mxm"), bias=-1e9)
+    ts(A("mnm"), j128, 0.5, -2e9, OP.is_ge, OP.mult)
+    act(A("mnm"), A("mnm"), bias=1e9)
+    fill(A("tiny"), TINY)
+    fill(A("pad"), 0.0)
+    fill(A("padb"), 0.0)
+    fill(SU(0, 416, 417), BIG)
+    act(A("ones"), row128, scale=0.0, bias=1.0)
+    act(A("on32"), row128, scale=0.0, bias=1.0)
+    act(A("c69"), A("row", 0, 8), scale=0.0, bias=2.0 ** 69)
+    act(A("c75"), A("row", 0, 8), scale=0.0, bias=-7.5)
+    act(A("pt"), j128, bias=-8.0)
+    ts(A("lt"), row128, col(0), None, OP.is_ge)
+    ts(col(12), col(2), -10.0, None, OP.mult)
+    ts(A("v320"), A("v320"), col(12), None, OP.add)
+    ts(col(13), col(1), MID, None, OP.add)
+    ts(A("dumc"), A("row", 0, 16), 16.0, col(13), OP.mult, OP.add)
+    ts(col(14), col(1), 16.0, 8.0, OP.mult, OP.add)
+    ts(A("pc"), A("row", 0, 8), 256.0, col(14), OP.mult, OP.add)
+    ts(col(15), col(0), 16.0, None, OP.mult)
+    ts(col(16), col(0), 16.0, -128.0, OP.mult, OP.add)
+    ts(A("ew"), A("m16"), col(15), None, OP.is_equal)
+    ts(A("efn"), A("m16"), col(16), -512.0, OP.is_equal, OP.mult)
+    act(A("efp"), A("efn"), AF.Copy, scale=-1.0)
+    bon[0] = 0.0
+    cp(col(17), A("thi"))
+    ts(col(18), col(17), -2048.0, None, OP.add)
+    ts(A("thrb"), A("ones"), col(18), None, OP.mult)
+    bon[0] = BT["k"] / 2
+    fill(A("e3"), 0.0)
+    ts(A("rx"), A("rxi"), col(0), 0.5, OP.is_equal, OP.mult)
+    ts(A("axc"), A("g8"), col(2), -0.5, OP.is_equal, OP.add)
+    fill(A("half"), 0.5)
+    fill(A("zero"), 0.0)
+    scan(A("pw2"), A("half"), A("zero"), OP.mult, OP.add, 2.0 ** 64)
+    tt(A("tmp"), A("pw2", 0, 128), I1, OP.mult)
+    red(col(19), A("tmp"), OP.add)
+    ts(col(20), col(19), 2.0, None, OP.mult)
+    ts(A("tmp", 0, 16), A("jr", 0, 16), col(1), None, OP.is_equal)
+    tt(A("tmp", 16, 32), A("tmp", 0, 16), A("pw2", 0, 16), OP.mult)
+    red(col(21), A("tmp", 16, 32), OP.add)
+    ts(col(24, 8), A("b8f"), col(21), None, OP.mult)
+    for g2 in range(8):
+        ts(A("wt", g2, 64, 8), A("pw2", 63, 176, 16), col(24 + g2), None, OP.mult)
+    bon[0] = 0.0
+
     def pushes(t):
         for x, lo, hi, to in (("a", 1024, 2048, 0), ("b", 0, 1026, 1024)):
-            remote(prv, A("tab%d" % t, lo, hi), A("rem%d" % t, to, to + hi - lo), nxt, "push%s%d" % (x, t), "pl%s%d" % (x, t),
+            remote(prv, A(TAB[t], lo, hi), A("rem%d" % t, to, to + hi - lo), nxt, "push%s%d" % (x, t), "pl%s%d" % (x, t),
                    256 * (hi - lo))
 
     pushes(0)
 
-    def l2p(out, src):
-        (nm, lo, hi), (sn, slo, shi) = out, src
-        return [(cb("sl", 128 * (2 * g2 + c2), 128), A(sn, slo + g2, shi, 2), A(nm, lo + c2, hi, 2))
-                for c2 in range(2) for g2 in range(2)]
+    def kv(nm, c, x): return A(nm, 256 * c + 128 * x, 256 * c + 128 * x + 128)
+    def kone(x): return P(x, 0, 128 * REP, REP)
 
-    def l2wrap(out, src):
-        prs = l2p(out, src)
-        group(None, prs[:2])
-        group(None, prs[2:])
-
-    def l2direct(c, o, nm):
-        a = NL * c
-        lo = CBN["bo1"][0]
-        bank = "ps%d" % (4 + c)
-        for pa in range(4):
-            for ib in range(4):
-                out = ([(bank, 0, 1)], T[bank][32 * pa:32 * pa + 32, o + 2 * ib:o + 2 * ib + 2], 2)
-                mm(out, A(nm, a + 32 * ib, a + 32 * ib + 32), A("cb", lo + 32 * pa, lo + 32 * pa + 32, 16), True, True)
-
-    def clean_q(t, c, nm):
-        x = ck(nm, c)
-        prs = [(cb("i1"), x)]
-        ts(ck("q0", c), x, 0.0, None, OP.is_equal)
-        prs.append((cb("im"), ck("q0", c)))
-        if t >= 2:
-            ts(ck("qb", c), x, A("rb0", 0, 1), A("rb0", 1, 2), OP.is_equal, OP.mult)
-            prs.append((cb("im"), ck("qb", c)))
-        if t >= 1:
-            ra = "ra%d" % (t - 1)
-            ts(ck("qa", c), x, A(ra, 0, 1), A(ra, 1, 2), OP.is_equal, OP.mult)
-            prs.append((cb("im"), ck("qa", c)))
-        return prs
+    def dead(t):
+        return [A("ra%d" % max(t - 1, 0), 0, 1), A("rr", 4, 5)][:t]
 
     def stage_v(t, c):
         a = NL * c
         if t == 0:
-            cp(ck("kv", c), A("tab0", 10 * a, 10 * (a + NL), 10))
-            ts(ck("bv", c), A("nb", 10 * a, 10 * (a + NL), 10), -1344.0, None, OP.add)
+            take("kv", kv("kvn", c, 0), A("tab0", 10 * a, 10 * (a + NL), 10))
+            ts(ck("bv", c), A("nb", 10 * a, 10 * (a + NL), 10), -MID, None, OP.add)
         else:
             vl = cw("wl%d" % (t - 1), c)
-            act(ck("kv", c), ind(tabw(t), vl))
-            ts(ck("bv", c), ind(A("nb", 0, V), vl), -1344.0, None, OP.add)
-        group(KA(c, 0, 128), clean_q(t, c, "kv"))
+            take("kv", kv("kvn", c, 0), ind(tabw(t), vl))
+            ts(ck("bv", c), ind(A("nb", 0, V), vl), -MID, None, OP.add)
 
     def stage_n(t, c):
         a = NL * c
-        z = ck(zbuf(t), c)
-        m = AC(c, 128, 256)
-        mm(SM(c, 0, 128), cb("bo1" if t == 0 else "boh"), z, True, True)
-        act(ck("zs", c), z, scale=1.0 if t == 0 else 0.5, bias=-0.5)
-        ts(ck("yi", c), SM(c, 0, 128), col(36), float(t), OP.add, OP.add)
-        ts(ck("yj", c), ck("yi", c), 15, None, OP.bitwise_and)
-        ts(m, ck("yj", c), 0.0, None, OP.is_equal)
+        y, m = MI(c, 128, 256), MI(c, 0, 128)
+        mms(y, [(A("bo1"), ck(zbuf(t), c)), (I1, A("yc%d" % t))])
+        rnd(ck("r16", c), y, 4)
+        tt(m, y, ck("r16", c), OP.is_equal)
         tt(ck("nm", c), ck("bv", c), m, OP.mult)
-        group(SM(c, 128, 136), [(U("u1", q), A("nm", a + q, a + NL, 16)) for q in range(16)])
-        ts(cw("nl", c), SM(c, 128, 136), 1344.0, None, OP.add)
+        mms(MI(c, 384, 392), [(A("u1", 15 - q, 143 - q), A("nm", a + q, a + NL, 16)) for q in range(16)])
+        ts(cw("nl", c), MI(c, 384, 392), MID, None, OP.add)
         cp(ck("cd", c), ind(A("nb", 0, V), cw("nl", c)))
         kc = "kc%d" % c
+        w = NL // SUBK
         for s in range(SUBK):
-            act(A(kc, 2048 // SUBK * s, 2048 // SUBK * (s + 1)),
-                ind(tabw(t), A("cd", a + 128 // SUBK * s, a + 128 // SUBK * (s + 1))))
-        cp(ck("kn", c), ind(tabw(t), cw("nl", c)))
-        l2direct(c, 160, "nm")
-        tt(ck("e0", c), ck("kn", c), KA(c, 0, 128), OP.is_equal)
-        l2direct(c, 168, "e0")
-        ts(ck("cdh", c), ck("cd", c), -1344.0, None, OP.add)
-        group(KA(c, 128, 256), clean_q(t, c, "kn"))
-        if NSV:
-            act(ck("kvp", c), KA(c, 0, 128), AF.Copy)
-        if NSN:
-            act(ck("knp", c), KA(c, 128, 256), AF.Copy)
-        ts(cw("dk", c), SM(c, 168, 176), 2.5, 15 * S17, OP.is_ge, OP.mult)
-        tt(cw("nk16", c), cw("dk", c), SM(c, 160, 168), OP.add)
+            act(A(kc, 16 * w * s, 16 * w * (s + 1)), ind(tabw(t), A("cd", a + w * s, a + w * s + w)))
+        take("kn", kv("kvn", c, 1), ind(tabw(t), cw("nl", c)))
+        ts(ck("cdh", c), ck("cd", c), -MID, None, OP.add)
+        for nm, r in zip(("qa", "qb"), dead(t)):
+            ts(A(nm, 256 * c, 256 * c + 256), A("kvn", 256 * c, 256 * c + 256), r, r, OP.is_equal, OP.mult)
+
+    def keys(t, c, x):
+        prs = []
+        for lhs, nm in [(I1, "kvn"), (IM, "qa"), (IM, "qb")][:1 + t]:
+            prs += [(lhs, kv(nm, c, x), P(x, j, 128 * REP, REP)) for j in range(REP)]
+        mms(P(x, 0, 128 * REP), prs + [(I1, A("tiny", 0, 128 * REP))])
+
+    def stage_h(t, c):
+        tt(ck("pz", c), ck(zbuf(t), c), kone(1), OP.mult)
+        mms(MI(c, 392, 400), [(ck("pz", c), A("b8f"))])
+        rnd(cw("hH", c), MI(c, 392, 400), 11)
+        tt(pad("padh", c), MI(c, 392, 400), cw("hH", c), OP.subtract)
+        mms(MI(c, 400, 408), wrap("padh", c))
+        ts(cw("hl", c), MI(c, 400, 408), 1024.0, None, OP.add)
+        act(ck("src", c), ind(A("rem%d" % t, 0, H + 1), cw("hl", c)))
+        for nm, r in [("sa", A("rc%d" % max(t - 1, 0), 0, 1)), ("sb", A("ra0", 0, 1))][:t]:
+            ts(ck(nm, c), ck("src", c), r, None, OP.is_equal)
 
     def stage_cmp(t, c):
         kc = "kc%d" % c
-        a = NL * c
-        for e, db, ns, neg, lo in (("e1%d" % c, "da%d" % c, NSV, "kvp", 0), ("e2%d" % c, "db%d" % c, NSN, "knp", 128)):
-            out = SM(c, 384, 512) if lo == 0 else AC(c, 0, 128)
-            for b in range(ns // 4):
-                hi = 512 * (4 - b)
-                bk = nb_[0] % 2
-                nb_[0] += 1
-                for j in range(4):
-                    o = DB(bk, 128 * j, 128 * j + 128)
-                    mm(o, cb("i1"), A(kc, 12 - 4 * b + j, 2048, 16), True, False)
-                    mm(o, cb("im"), ck(neg, c), False, True)
-                act(A(db, hi - 512, hi), DB(bk, 0, 512), AF.Copy)
-                if b % EQB == EQB - 1:
-                    w = 512 * EQB
-                    ts(A(e, hi - 512, hi - 512 + w), A(db, hi - 512, hi - 512 + w), 0.0, None, OP.is_equal)
-            mm(out, cb("i1"), ck("cdh", c), True, False)
-            mm(out, cb("i1"), cb("kb"), False, False)
-            for k in range(16):
-                ek = A(e, 128 * k, 128 * k + 128)
-                if k < 16 - ns:
-                    tt(ek, A(kc, k, 2048, 16), KA(c, lo, lo + 128), OP.is_equal)
-                mm(out, U("u17", k), ek, False, k == 15)
-            if lo == 0:
-                cp(ck("av", c), out)
-        act(ck("kvr", c), KA(c, 0, 128), AF.Relu)
-        tt(ck("val", c), ck("av", c), AC(c, 0, 128), OP.min)
-        tr(ck("vt", c), ck("val", c))
-        scan(ck("sc", c), A("mxm", 0, 128), ck("vt", c), OP.min, OP.max)
-        tt(cw("tot", c), A("sc", a + 15, a + NL, 16), cw("nk16", c), OP.max)
-        big = 1.5 * 2 ** 35
-        ts(cw("th", c), cw("tot", c), big, -big, OP.add, OP.add)
-        tt(cw("w16", c), cw("tot", c), cw("th", c), OP.subtract)
-        ts(cw("fl", c), cw("tot", c), 350000.0 - 2.5 * S17, None, OP.is_lt)
-        sm = "ps%d" % (4 + c)
-        l2wrap((sm, 136, 144), ("w16", 8 * c, 8 * c + 8))
-        l2wrap((sm, 144, 152), ("fl", 8 * c, 8 * c + 8))
-        ts(cw("wl%d" % t, c), SM(c, 136, 144), 1344.0, None, OP.add)
-        cp(A("wfl%d" % (t & 1), 16 * c, 16 * c + 16), SM(c, 136, 152))
+        tk = ("w", 2 + c)
+        keys(t, c, 0)
+
+        def low(o, x):
+            return [(I1, A("ksc", 144 * x, 144 * x + 144), o(0, 1)), (ck("cdh", c), A("i18"), o(0, 1)),
+                    (ck("nm", c), B8, o(16, 18)), (ck("nm", c), B8, o(17, 18))]
+
+        def ov(lo, st): return MI(c, 128 + lo, 272, st)
+        def on(lo, st): return SU(c, lo, 144, st)
+        def ek(x, b, j): return A("e%d%d" % (x + 1, c), 128 * REP * b + j, 128 * REP * (b + 1), REP)
+        ad, sc = A("ad", 144 * c, 144 * c + 144), A("sc", 144 * c, 144 * c + 144)
+        mms(None, low(on, 1), True, False, tk)
+        for x in range(2):
+            e = "e%d%d" % (x + 1, c)
+            if x == 1:
+                keys(t, c, 1)
+                bon[0] += BT["h"][c]
+                stage_h(t, c)
+                bon[0] -= BT["h"][c]
+            for b in range(16 // REP):
+                lo, hi = 128 * REP * b, 128 * REP * (b + 1)
+                tt(A(e, lo, hi), A(kc, b, H, 16 // REP), P(x, 0, 128 * REP), OP.is_equal)
+                if x == 1:
+                    mms(None, [(ek(1, b, j), A("sv"), on(b + 16 // REP * j, 18)) for j in range(REP)], False, hi == H, tk)
+            if x == 0:
+                tt(ck("e0", c), kv("kvn", c, 1), kone(0), OP.is_equal)
+                mms(None, low(ov, 0) + [(ck("e0", c), A("se"), ov(17, 18))]
+                    + [(ek(0, b, j), A("sv"), ov(b + 16 // REP * j, 18)) for b in range(16 // REP) for j in range(REP)])
+                act(ad, ov(0, 1), AF.Copy)
+                act(ck("kvr", c), kone(0), AF.Relu, bias=-TINY)
+        val = A("val", 144 * c, 144 * c + 144)
+        tt(val, ad, on(0, 1), OP.min)
+        scan(sc, A("mxm"), val, OP.min, OP.max)
+        tot = A("sc", 144 * c + 17, 144 * c + 144, 18)
+        rnd(cw("th", c), tot, 12)
+        tt(pad("padw", c), tot, cw("th", c), OP.subtract)
+        fl = A("fl%d" % c, 8, 16)
+        if t < NR - 1 or ENG["fl"] == "s":
+            act(fl, cw("th", c), AF.Relu, scale=-2.0 ** -16, bias=1.0, acc=A("fs", c, c + 1))
+        else:
+            ts(fl, tot, 32768.0, None, OP.is_lt)
+        mms(SU(c, 420, 428), wrap("padw", c), tok=("r", 2 + c))
+        ts(cw("wl%d" % t, c), SU(c, 420, 428), MID, None, OP.add)
 
     def stage_w(t, c):
         a = NL * c
-        cp(ck("kw", c), ind(tabw(t), cw("wl%d" % t, c)))
-        prs = [(cb("i1"), ck("kw", c))]
-        if t >= 1:
-            ra = A("ra%d" % (t - 1), 3, 4)
-            ts(ck("qa", c), ck("kw", c), ra, ra, OP.is_equal, OP.mult)
-            prs.append((cb("im"), ck("qa", c)))
-        if t >= 2:
-            rb = A("rb0", 0, 1)
-            ts(ck("qb", c), ck("kw", c), rb, rb, OP.is_equal, OP.mult)
-            prs.append((cb("im"), ck("qb", c)))
-        kw = SM(c, 0, 128)
-        group(kw, prs)
-        tt(ck("pi", c), ck("v2", c), kw, OP.mult)
-        ts(ck("pj", c), ck("pi", c), col(8), float(4 * t), OP.add, OP.add)
-        ts(ck("pk", c), ck("pj", c), 2, PL - 1, OP.arith_shift_right, OP.bitwise_and)
-        cp(ck("pl", c), ck("pk", c))
-        for s in range(SUBX):
-            act(A("xc%d" % c, 2048 // SUBX * s, 2048 // SUBX * (s + 1)),
-                ind(A("X", 0, PL), A("pl", a + 128 // SUBX * s, a + 128 // SUBX * (s + 1))))
-        tt(ck("pz", c), ck(zbuf(t), c), kw, OP.mult)
-        act(ck("kwc", c), kw, AF.Copy)
-        act(ck("hb", c), ck("kwc", c), AF.Relu, scale=-BIG, bias=col(16))
-        for q in range(16):
-            mm(SM(c, 256 + q, 512, 16), cb("rq", 128 * q, 128), A("wfl%d" % (t & 1), 16 * c, 16 * c + 16), True, True)
-        act(ck("flr", c), SM(c, 384, 512), scale=-512.0)
-        if t < NR - 1:
-            act(ck("v2", c), SM(c, 256, 384), scale=2.0, bias=2689.0)
-            vr = ck("wrp%d" % (t & 1), c)
-            act(vr, SM(c, 256, 384), AF.Copy)
-            tt(ck("wm", c), vr, AC(c, 128, 256), OP.mult)
-
-    def stage_full(t):
-        ts(fu("dr"), fu("tot"), 2.2e6 - 2.5 * S17, 2048.0, OP.is_gt, OP.mult)
-        group(F1(0, 16), [(cb("lt"), fu("fl"))]
-              + [(cb("on"), A("fl", 0, 16 - 2 * d), F1(2 * d, 16)) for d in range(1, 8)]
-              + [(cb("i1k"), fu("fl")), (cb("i1"), fu("dr"))])
-        ts(fu("iah"), F1(0, 16), 1024.0 + CAP + 0.5, 16384.0, OP.is_gt, OP.mult)
-        vprev = "wfl%d" % ((t + 1) & 1)
-
-        def node(lo):
-            return [(cb("i1"), cb("c13"))] + [(cb("i1"), A(vprev, 16 * c, 16 * c + 8), F1(lo + 8 * c, lo + 8 * c + 8))
-                                              for c in range(NC)] + l2p(("ps1", 384 + lo, 400 + lo), ("iah", 0, 16))
-        group(F1(64, 80), [(A("u1f", 15 - q, 143 - q), A("pz", q, L, 16)) for q in range(16)])
-        zs = 1.0 if t == 0 else 2.0
-        big = 1.5 * 2 ** 34 * zs
-        ts(fu("hH"), F1(64, 80), big, -big, OP.add, OP.add)
-        tt(fu("h2"), F1(64, 80), fu("hH"), OP.subtract)
-        ts(fu("sl2"), fu("h2"), 1.0 / zs, 1024.0, OP.mult, OP.add)
-        tab = "tab%d" % (t + 1)
-        act(A("src", 0, L), ind(A("rem%d" % t, 0, H + 1), fu("sl2")))
-        if t < NR - 1:
-            ones = [(cb("ones"), A("fl", j, j + 1)) for j in range(16)]
-            group(F1(16, 17), ones)
-            group(F1(17, 18), ones + [(cb("i1"), cb("c75", 0, 1))])
-            b27 = 1.5 * 2 ** 27
-            ts(A("fs", 2, 3), F1(17, 18), b27, -b27, OP.add, OP.add)
-            tt(A("fs", 3, 4), F1(16, 17), A("fs", 2, 3), OP.subtract)
-        if t > 0:
-            group(F1(48, 64), node(48))
-            act(fu("vb"), F1(48, 64), bias=-1344.0)
-            ts(fu("vah"), F1(48, 64), -1344.0, None, OP.add)
-            vr = "wrp%d" % ((t - 1) & 1)
-            group(KA(0, 0, 256), [(cb("i1"), cb("tri"))]
-                  + [(cb("i1"), fu("vah"), KA(0, q, 256, 16)) for q in range(16)])
-            o = 0
-            prs = [(cb("bo1"), A("ed", 0, L))]
-            for c1 in range(15):
-                n = L - 16 * (c1 + 1)
-                if c1 < E3S:
-                    act(A("e3", o, o + n), A(vr, L - n, L), scale=-1.0, bias=A("vb", c1, c1 + 1))
-                    oe = o + n
-                else:
-                    ts(A("e3", o, o + n), A(vr, L - n, L), A("vb", c1, c1 + 1), None, OP.is_equal)
-                prs.append((cb("bo1"), A("e3", o, o + n), KA(1, 256 - n, 256)))
-                o += n
-            tt(A("ed", 0, L), A(vr, 0, L), KA(0, 0, 256), OP.is_equal)
-            if E3S:
-                ts(A("e3", 0, oe), A("e3", 0, oe), 0.0, None, OP.is_equal)
-            group(KA(1, 0, 256), prs)
-            act(A("cnb", 0, L), KA(1, 0, 256), AF.Copy)
-            group(F1(80, 96), node(80) + [(U("u17", q), A("cnb", q, L, 16)) for q in range(16)])
+        tk = ("r", 2 + c)
+        src = ind(tabw(t), cw("wl%d" % t, c))
+        if t == 0:
+            tt(ck("pi", c), src, ck("v2", c), OP.mult)
+            act(ck("kwc", c), src)
+            ts(ck("pj", c), ck("pi", c), col(11), None, OP.add)
+            ts(ck("pk", c), ck("pj", c), 2, PL - 1, OP.arith_shift_right, OP.bitwise_and)
+            cp(ck("pl", c), ck("pk", c))
         else:
-            group(F1(80, 96), node(80))
-        tt(fu("sy"), fu("dum"), F1(80, 96), OP.min)
-        cp(fu("sl"), fu("sy"))
-        for c in range(NC):
-            o = SM(c, 256, 384)
-            for x in ("kwc", "src"):
-                mm(o, cb("i1"), ck(x, c), True, False)
-                if x == "src" and t >= 1:
-                    ts(ck("sa", c), ck("src", c), A("rc%d" % (t - 1), 0, 1), A("rc%d" % (t - 1), 0, 1), OP.is_equal, OP.mult)
-                    mm(o, cb("im"), ck("sa", c), False, False)
-                if x == "src" and t >= 2:
-                    ts(ck("sb", c), ck("src", c), A("ra0", 0, 1), A("ra0", 0, 1), OP.is_equal, OP.mult)
-                    mm(o, cb("im"), ck("sb", c), False, False)
-                if x == "src":
-                    mm(o, cb("i1"), cb("m512"), False, False)
-                mm(o, cb("i1" if x == "kwc" else "im"), ck("flr", c), False, False)
-                mm(o, cb("i256"), ck("kvr", c), False, True)
-                tt(ck("f1" if x == "kwc" else "fi", c), ck("kvr" if x == "kwc" else "f1", c), o, OP.max)
-        cp(ind(A(tab, 0, REM), fu("sl")), A("fi", 0, L))
+            take("kw", ck("kw", c), src)
+            prs = [(I1, ck("kw", c))]
+            for nm, r in zip(("qw", "qx"), dead(t)):
+                ts(ck(nm, c), ck("kw", c), r, r, OP.is_equal, OP.mult)
+                prs.append((IM, ck(nm, c)))
+            mms(SU(c, 0, 128), prs, tok=tk)
+            tt(ck("pi", c), ck("v2", c), SU(c, 0, 128), OP.mult)
+            ts(ck("pk", c), ck("pi", c), 2, PL - 1, OP.arith_shift_right, OP.bitwise_and)
+            ts(ck("pl", c), ck("pk", c), col(8 + t), None, OP.add)
+            act(ck("kwc", c), SU(c, 0, 128), AF.Copy)
+        w = NL // SUBX
+        for s in range(SUBX):
+            act(A("xc%d" % c, 16 * w * s, 16 * w * (s + 1)),
+                ind(A("X", 0, PL if t == 0 else 2 * PL), A("pl", a + w * s, a + w * s + w)))
+        act(ck("hb", c), ck("kwc", c), AF.Relu, scale=-BIG, bias=BIG)
+        mms(SU(c, 288, 416, parts=16), [(A("padw%d" % c, 15, 271, 16), I1), (A("fl%d" % c), I1)], tok=tk)
+        act(A("wT", a, a + NL, parts=16), SU(c, 288, 416, parts=16), AF.Copy)
         if t < NR - 1:
-            group(KA(0, 256, 512), [(cb("i1"), A("bv", 0, L)), (cb("im"), A("nm", 0, L)), (cb("i1"), A("wm", 0, L))])
-            act(A("bn", 0, L), KA(0, 256, 512), bias=1344.0)
-            cp(ind(A("nb", 0, REM), fu("sl")), A("bn", 0, L))
-            pushes(t + 1)
-            dma("y", A("tab%d" % (t + 2), 0, V), A(tab, 0, V), 2 * 128 * V)
+            act(cw("v32%d" % ((t + 1) & 1), c), SU(c, 420, 428), AF.Copy)
+            wb = SU(c, 128, 256)
+            mms(wb, [(A("ew", parts=16), A("wT", a, a + NL, parts=16))], tok=tk)
+            act(ck("v2", c), wb, scale=2.0, bias=2 * MID + 1)
+            cp(ck("vr%d" % ((t + 1) & 1), c), wb)
+            tt(ck("wm", c), ck("vr%d" % ((t + 1) & 1), c), MI(c, 0, 128), OP.mult)
+
+    def e3(c1, c):
+        o = 256 * c1 + NL * c if c1 < 8 else 2048 + NL * (c1 - 8)
+        return A("e3", o, o + NL)
+
+    def stage_e(t):
+        for c1 in range(16):
+            o = 256 * c1 if c1 < 8 else 2048 + NL * (c1 - 9)
+            ts(A("e3", o + 16 * c1, o + L), A("vr%d" % (t & 1), 16 * c1, L), A("v32%d" % (t & 1), c1, c1 + 1), None, OP.is_equal)
+
+    def stage_f(t, c):
+        a = NL * c
+        wT = A("wT", a, a + NL, parts=16)
+        pr = MI(c, 408, 416)
+        mms(pr, [(A("lt"), A("fl%d" % c, 8, 16)), (A("i1k"), A("fl%d" % c, 8, 16)), (A("i3"), cw("th", c))]
+            + [(A("ones"), A("fl0", 8, 16))] * c)
+        if t == 0:
+            ts(pad("padn", c), pr, 1024.0 + CAP + 0.5, -4096.0, OP.is_lt, OP.mult)
+        else:
+            act(pad("pada", c), pr, AF.Sign, scale=-1.0, bias=1024.0 + CAP + 0.5)
+            ax = MI(c, 448, 512)
+            mms(ax, wrap("pada", c, "rx", 64) + [(I1, A("axc"))])
+            tt(A("rw", 64 * c, 64 * c + 64), ax, A("wt"), OP.mult)
+            if c == 0:
+                act(A("rw2"), ax, AF.Relu, scale=2.0 ** 70)
+            mms(MI(c, 416, 424), [(I1, A("c69")), (A("im69"), pad("pada", c))]
+                + [(e3(c1, 1), A("rw2", 8 * c1, 8 * c1 + 8)) for c1 in range(8 * c)]
+                + [(e3(8 * c + c1, c), A("rw", 64 * c + 8 * c1, 64 * c + 8 * c1 + 8)) for c1 in range(8)])
+            ts(pad("padn", c), MI(c, 416, 424), col(20), -4096.0, OP.is_lt, OP.mult)
+        mms(MI(c, 424, 432), wrap("padn", c) + [(I1, cw("dumc", c))])
+        tt(cw("sy", c), MI(c, 424, 432), cw("v32%d" % (t & 1), c), OP.max)
+        ts(cw("sl", c), cw("sy", c), MID, None, OP.add)
+        o1, o2 = MI(c, 128, 256), MI(c, 256, 384)
+        mms(o1, [(I1, ck("kwc", c)), (A("i256"), ck("kvr", c)), (A("efn", parts=16), wT)])
+        tt(ck("f1", c), ck("kvr", c), o1, OP.max)
+        prs = [(I1, ck("src", c)), (A("i256"), ck("kvr", c))] + [(A("i512"), ck(x, c)) for x in ("sa", "sb")[:t]]
+        out = ind(A(TAB[t + 1], 0, REM), cw("sl", c))
+        if t < NR - 1:
+            mms(o2, prs + [(A("efp", parts=16), wT)])
+            act(ck("r2", c), o2, AF.Relu, bias=-512.0)
+            tt(out, ck("f1", c), ck("r2", c), OP.add)
+            mms(o1, [(I1, ck("bv", c)), (IM, ck("nm", c)), (I1, ck("wm", c))])
+            act(ck("bn", c), o1, bias=MID)
+            cp(ind(A("nb", 0, REM), cw("sl", c)), ck("bn", c))
+        else:
+            mms(o2, prs + [(A("i512"), A("ones")), (A("efp", parts=16), wT)])
+            tt(ck("r2", c), ck("f1", c), o2, OP.max)
+            ts(ck("qc", c), ck("r2", c), A("rb1", 0, 1), A("rr", 9, 10), OP.is_equal, OP.mult)
+            tt(out, ck("r2", c), ck("qc", c), OP.add)
 
     def stage_d(t, c):
         a = NL * c
         z = ck(zbuf(t), c)
-        out = AC(c, 256, 384)
-        xc = "xc%d" % c
-        mm(out, cb("i1"), cb("pt"), True, False)
-        if NSB < 16:
-            mm(KA(c, 256, 384), cb("i1" if t == 0 else "ih"), z, True, True)
-            mm(out, cb("bv32" if t == 0 else "bv16"), z, False, False)
-        for b in range(NSB // 4):
-            bk = nb_[0] % 2
+        xc, mx = "xc%d" % c, "mx%d" % c
+        tk = ("w", 2 + c)
+        for b in range(4):
+            bk = 4 + nb_[0] % 2
             nb_[0] += 1
-            for j in range(4):
-                o = DB(bk, 128 * j, 128 * j + 128)
-                mm(o, cb("i1"), A(xc, 4 * b + j, 2048, 16), True, False)
-                mm(o, cb("im" if t == 0 else "imh"), z, False, True)
-            act(A("mx%d" % c, 512 * b, 512 * b + 512), DB(bk, 0, 512), AF.Abs)
-        for p in range(15, -1, -1):
-            mxp = A("mx%d" % c, 128 * p, 128 * p + 128)
-            if p >= NSB:
-                x = A(xc, p, 2048, 16)
-                mm(out, U("um32", p), x, False, False)
-                tt(mxp, x, KA(c, 256, 384), OP.max)
-            mm(out, U("u32" if p < NSB else "u64", p), mxp, False, p == 0)
-        tr(ck("dt", c), out)
-        scan(ck("ds", c), A("mnm", 0, 128), ck("dt", c), OP.max, OP.min)
-        b28 = 1.5 * 2 ** 28
+            mms(None, [(I1, A(xc, 4 * b + j, H, 16), P(bk, 128 * j, 128 * j + 128)) for j in range(4)]
+                + [(IM, z, P(bk, 128 * j, 128 * j + 128)) for j in range(4)])
+            act(A(mx, 512 * b, 512 * b + 512), P(bk, 0, 512), AF.Abs)
+            prs = [(I1, A("pt"), SU(c, 0, 128)), (A("thrb"), IM, SU(c, 128, 256))] if b == 0 else []
+            mms(None, prs + [(A(mx, 128 * p, 128 * p + 128), A("sd"), SU(c, p, 256, 16)) for p in range(4 * b, 4 * b + 4)],
+                b == 0, b == 3, tk)
+        tk = ("r", 2 + c)
+        scan(ck("ds", c), A("mnm"), SU(c, 0, 128), OP.max, OP.min)
         last = A("ds", a + 15, a + NL, 16)
-        ts(cw("pH", c), last, b28, -b28, OP.add, OP.add)
-        tt(cw("p16", c), last, cw("pH", c), OP.subtract)
-        group(SM(c, 152, 160), [(cb("i1"), A("pc", 0, 8))] + l2p(("ps%d" % (4 + c), 152, 160), ("p16", 8 * c, 8 * c + 8)))
-        cp(cw("pw", c), SM(c, 152, 160))
-        tt(ck("sz", c), ind(A(xc, 0, 2048), cw("pw", c)), ck("zs", c), OP.add)
-        b24 = 1.5 * 2 ** 24
+        rnd(cw("pH", c), last, 5)
+        tt(pad("padp", c), last, cw("pH", c), OP.subtract)
+        act(ck("ug", c), SU(c, 128, 256), AF.Relu, scale=BIG, bias=-2047 * BIG if t == 0 else A("fs", 4 + t, 5 + t))
+        mms(SU(c, 288, 416), [(I1, ck("kwc", c)), (I1, ck("io", c)), (I1, ck("hb", c)), (ck("ug", c), I1)], tok=tk)
+        red(SU(1, 416, 417) if c == 0 else A("rr", 0, 1), SU(c, 288, 417), OP.min)
+        mms(SU(c, 428, 436), wrap("padp", c) + [(I1, A("pc"))], tok=tk)
+        cp(cw("pw", c), SU(c, 428, 436))
+        act(ck("xs", c), ind(A(xc), cw("pw", c)))
+        xz = MI(c, 256, 384)
+        mms(xz, [(A("ih"), z), (A("iq"), A("ones")), (A("ih"), ck("xs", c))])
         if t < NR - 1:
-            ts(ck("zb", c), ck("sz", c), b24, -b24, OP.add, OP.add)
+            rnd(ck("zb", c), xz, 0)
         else:
-            ts(ck("xm", c), ck("sz", c), b24, -b24, OP.add, OP.add)
-            act(ck("yzf", c), ck("xm", c), AF.Copy, scale=0.5)
+            rnd(ck("yzf", c), xz, 0)
             dma("y", hbm("yz", a, a + NL), ck("yzf", c), 512 * NL)
-        tc = col(23) if t == 0 else A("fs", 4 + t, 5 + t)
-        act(ck("ug", c), out, AF.Relu, scale=BIG, bias=tc)
-        group(SM(c, 0, 128), [(cb("i1"), ck("kwc", c)), (cb("i1"), cb("io", a, NL)), (cb("i1"), ck("hb", c)),
-                              (cb("i1"), ck("ug", c))])
-        red(A("rr", c, c + 1), SM(c, 0, 128), OP.min)
 
-    BL = ((0, H), (H, V))
+    def failures(t):
+        on = [(A("on32"), A("fs", c, c + 1)) for c in range(NC)]
+        mms(MI(1, 432, 433), on)
+        mms(MI(1, 433, 434), on + [(I1, A("c75", 0, 1))])
+        rnd(A("fs", 2, 3), MI(1, 433, 434), 4)
+        tt(A("fs", 3, 4), MI(1, 432, 433), A("fs", 2, 3), OP.subtract)
+        act(A("fs", 5 + t, 6 + t), A("fs", 3, 4), scale=-BIG, bias=-2047 * BIG)
 
-    def clean(tab, frm, nm, acc):
-        bon[0] = -CLB
-        for lo, hi in BL:
-            ts(A(nm, lo, hi), A(frm, lo, hi), acc[0], acc[1], OP.is_equal, OP.mult)
-        for lo, hi in BL:
-            dma("g", A(tab, lo, hi), A(nm, lo, hi), 2 * 128 * (hi - lo) * 2, add=True)
+    def clean(tab, frm, nm, key, neg):
+        bon[0] = BT["cl"]
+        act(A("rr", neg, neg + 1), key, AF.Copy, scale=-1.0)
+        w = V // CLP
+        for lo in range(0, V, w):
+            ts(A(nm, lo, lo + w), A(frm, lo, lo + w), key, A("rr", neg, neg + 1), OP.is_equal, OP.mult)
+        dma("g", A(tab, 0, V), A(frm if nm == tab else nm, 0, V), 2 * 128 * V * 2, add=True)
         bon[0] = 0.0
 
     def stage_rv(t):
-        ra = "ra%d" % t
-        tt(A("rr", 2, 3), A("rr", 0, 1), A("rr", 1, 2), OP.min)
-        ts(A("rr", 2, 3), A("rr", 2, 3), BIG, None, OP.min)
-        b32 = 1.5 * 2 ** 32
-        ts(A("rr", 3, 4), A("rr", 2, 3), b32, -b32, OP.add, OP.add)
-        tt(A(ra, 0, 1), A("rr", 2, 3), A("rr", 3, 4), OP.subtract)
+        ra = A("ra%d" % t, 0, 1)
+        rnd(A("rr", 1, 2), A("rr", 0, 1), 9)
+        tt(ra, A("rr", 0, 1), A("rr", 1, 2), OP.subtract)
         if t < NR - 1:
-            ts(A(ra, 1, 2), A(ra, 0, 1), 1.0, None, OP.add)
-            rb = "rb%d" % t
-            if t == 1:
-                tt(A("rr", 4, 5), A(ra, 0, 1), A("rb0", 0, 1), OP.not_equal)
-                tt(A(ra, 3, 4), A("rr", 4, 5), A(ra, 0, 1), OP.mult)
-            else:
-                cp(A(ra, 3, 4), A(ra, 0, 1))
-            ts(A(ra, 2, 3), A(ra, 3, 4), -1.0, None, OP.mult)
-            clean("tab%d" % (t + 2), "tab%d" % (t + 1), "cln", (A(ra, 3, 4), A(ra, 2, 3)))
-            remote(nxt, A(ra, 0, 2), A(rb, 0, 2), prv, "rvs%d" % t, "rvl%d" % t, 1024)
-            remote(prv, A(ra, 0, 2), A("rc%d" % t, 0, 2), nxt, "rws%d" % t, "rwl%d" % t, 1024)
-            ts(A(rb, 2, 3), A(rb, 0, 1), -1.0, None, OP.mult)
+            remote(prv, ra, A("rc%d" % t, 0, 1), nxt, "rws%d" % t, "rwl%d" % t, 512)
+            remote(nxt, ra, A("rb%d" % t, 0, 1), prv, "rvs%d" % t, "rvl%d" % t, 512)
+        if t == 0:
+            clean("tab2", "tab0", "tab2", ra, 6)
+        elif t == 1:
+            tt(A("rr", 3, 4), ra, A("rb0", 0, 1), OP.not_equal)
+            tt(A("rr", 4, 5), A("rr", 3, 4), A("rb0", 0, 1), OP.mult)
+            clean("tab3", "tab2", "cln", ra, 8)
+            clean("tab3", "tab2", "clc", A("rb1", 0, 1), 9)
         else:
-            tt(A("rr", 4, 5), A(ra, 0, 1), A("rb1", 0, 1), OP.not_equal)
-            tt(A("rr", 5, 6), A("rr", 4, 5), A(ra, 0, 1), OP.mult)
-            ts(A("rr", 6, 7), A("rr", 5, 6), -1.0, None, OP.mult)
             for i in range(7):
                 lo, hi = 384 * i, 384 * i + 384
-                ts(A("cln", lo, hi), A("tab3", lo, hi), A("rr", 5, 6), A("rr", 6, 7), OP.is_equal, OP.mult)
-                o = A("ps%d" % (6, 7, 2, 3)[i % 4], 0, 384)
-                group(o, [(cb("i1"), A("tab3", lo, hi)), (cb("i1"), A("clb", lo, hi)), (cb("i1"), A("cln", lo, hi))])
-                if i % 2:
-                    cp(A("fin", lo, hi), o)
+                ts(A("cln", lo, hi), A("tab3", lo, hi), ra, ra, OP.is_equal, OP.mult)
+                o = P((4, 5, 0, 1)[i % 4], 0, 384)
+                mms(o, [(I1, A("tab3", lo, hi)), (IM, A("cln", lo, hi))])
+                if i in (3, 6):
+                    ts(A("fin", lo, hi), o, 0.0, None, OP.max)
                 else:
-                    act(A("fin", lo, hi), o, AF.Copy)
-            for q, lo, hi in (("y", 0, 768), ("s", 768, 1536), ("y", 1536, 2304), ("s", 2304, V)):
+                    act(A("fin", lo, hi), o, AF.Relu)
+            for q, lo, hi in (("y", 0, 768), ("y", 768, 1536), ("y", 1536, 2304), ("y", 2304, V)):
                 dma(q, hbm("yk", lo, hi), A("fin", lo, hi), 256 * (hi - lo))
 
-    stages = {"v": stage_v, "n": stage_n, "c": stage_cmp, "w": stage_w, "d": stage_d}
+    stages = {"v": stage_v, "n": stage_n, "c": stage_cmp, "w": stage_w, "d": stage_d, "f": stage_f}
 
     def st(f, t, c):
         bon[0] = BT[f][c]
@@ -648,26 +615,24 @@ def rank_program(g, core, T, topo):
         bon[0] = 0.0
 
     for t in range(NR):
+        if t > 0:
+            bon[0] = BT["e"]
+            stage_e(t)
         for c in range(NC):
             st("v", t, c)
             st("n", t, c)
         for c in range(NC):
             st("c", t, c)
             st("w", t, c)
-        bon[0] = BT["f"][0]
-        stage_full(t)
-        bon[0] = 0.0
+        for c in range(NC):
+            st("f", t, c)
+        if t < NR - 1:
+            pushes(t + 1)
+            failures(t)
         if t == 1:
-            clean("tab3", "tab2", "clb", (A("rb0", 0, 1), A("rb0", 2, 3)))
-        if t == 2:
-            bon[0] = -CLB
-            for lo, hi in BL:
-                ts(A("clb", lo, hi), A("tab3", lo, hi), A("rb1", 0, 1), A("rb1", 2, 3), OP.is_equal, OP.mult)
-            bon[0] = 0.0
+            clean("tab3", "tab2", "tab3", A("rb0", 0, 1), 7)
         for c in range(NC):
             st("d", t, c)
-        if t < NR - 1:
-            ts(A("fs", 5 + t, 6 + t), A("fs", 3, 4), -32.0 * BIG, col(23), OP.mult, OP.add)
         stage_rv(t)
     _emit(g, T, ops)
 
@@ -683,11 +648,11 @@ def _emit(g, T, ops):
     prio = [0.0] * n
     for i in range(n - 1, -1, -1):
         o = ops[i]
-        prio[i] = o["dur"] + o["lat"] + max([prio[s] for s in succ[i]], default=0.0)
+        prio[i] = o["dur"] + o["lat"] + max([prio[s] + WK for s in succ[i]], default=0.0)
     prio = [p + o["bon"] for p, o in zip(prio, ops)]
     left = [len(o["deps"]) for o in ops]
     fin = [0.0] * n
-    qfree, ready, order = {}, {}, []
+    qfree, ready, order, bank = {}, {}, [], {}
     est = [0.0] * n
 
     def push(i):
@@ -700,6 +665,10 @@ def _emit(g, T, ops):
                 e = max(e, fin[j] + WK)
         est[i] = e
         ready.setdefault(o["q"], []).append(i)
+
+    def start(i):
+        o = ops[i]
+        return max([est[i]] + [fin[j] + WK for b in o["banks"] for q2, j in bank.get(b, {}).items() if q2 != o["q"]])
     for i in range(n):
         if left[i] == 0:
             push(i)
@@ -709,15 +678,20 @@ def _emit(g, T, ops):
             if not rs:
                 continue
             f = 0.0 if q == "ext" else qfree.get(q, 0.0)
-            t0 = max(f, min(est[i] for i in rs))
+            t0 = max(f, min(start(i) for i in rs))
             if best is None or t0 < best[0]:
                 best = (t0, q)
         t0, q = best
         rs = ready[q]
-        i = max([i for i in rs if est[i] <= t0 + 30.0], key=lambda k: (prio[k], -k))
+        i = max([i for i in rs if start(i) <= t0 + 30.0], key=lambda k: (prio[k], -k))
         rs.remove(i)
         o = ops[i]
-        st = max(t0, est[i])
+        st = max(t0, start(i))
+        for b in o["banks"]:
+            for q2, j in bank.setdefault(b, {}).items():
+                if q2 != q:
+                    o["deps"][j] = True
+            bank[b][q] = i
         qfree[q] = st + o["dur"]
         fin[i] = st + o["dur"] + o["lat"]
         order.append(i)

@@ -1,3 +1,5 @@
+import numpy as np
+from concourse.bass import DstId, RemoteDMATransfer
 from concourse.mybir import AluOpType, AxisListType, ActivationFunctionType
 
 OP = AluOpType
@@ -12,12 +14,15 @@ TINY = 2.0 ** -60
 CAP = 64
 REP = 4
 CYC, PEC, VF, SF, PF, WK, GA, SCA = 0.9, 0.46, 60.0, 60.0, 8.0, 70.0, 1.55, 3.0
-LZ, LN, LR, LX = 4000.0, 10000.0, 12000.0, 6000.0
-BT = {"k": 200000.0, "v": (0.0, 0.0), "n": (1500.0, 0.0), "h": (0.0, 0.0), "c": (2000.0, 0.0), "w": (2000.0, 0.0),
-      "f": (0.0, 0.0), "d": (2000.0, 0.0), "e": -3000.0, "cl": 0.0}
-ENG = {"kn": "v", "kw": "s", "kv": "s", "fl": "s"}
+LZ, LN, LR, LX = 3000.0, 8000.0, 10500.0, 6000.0
+LP, LV = 12000.0, 5000.0
+BT = {"k": 0.0, "v": (0.0, 0.0), "n": (0.0, 0.0), "h": (0.0, 0.0), "c": (0.0, 0.0), "w": (0.0, 0.0),
+      "f": (0.0, 0.0), "d": (0.0, 0.0), "e": 0.0, "cl": 0.0}
+ENG = {"kn": "s", "kw": "s", "kv": "s", "fl": "s", "bv": "s", "cdh": "v", "vr": "s", "r16": "s"}
+HV, HX = 1, 1
 SUBK, SUBX, CLP = 2, 2, 3
-CBN = {}
+SLACK, HOLD, PASSES, JIT, SEED = 30.0, 0.3, 40, 200.0, 1
+PLAN = []
 ALIAS = {}
 SCRATCH = {}
 
@@ -36,24 +41,24 @@ def _bufs(dtype, width, names):
 
 
 _pack("cb", "bfloat16", [(x, 128) for x in ("i1", "im", "ih", "iq", "bo1", "i1k", "lt", "ones", "i3", "im69", "i256",
-                                            "i512", "pt", "yc0", "yc1", "yc2")]
+                                            "i512", "pt", "yc0", "yc1", "yc2", "bo16", "ew", "efn", "efp")]
       + [("u1", 144), ("i18", 144), ("ksc", 288), ("tiny", 512), ("io", 256), ("rx", 1024), ("rxi", 1024), ("axc", 64),
          ("sv", 8), ("se", 8), ("sd", 16), ("c69", 8), ("c75", 8)])
 _pack("cf", "float32", [("row", 256), ("jr", 128), ("j18", 144), ("m16", 128), ("mxm", 144), ("mnm", 128), ("pw2", 176),
-                        ("half", 176), ("zero", 176), ("wt", 64), ("g8", 64), ("b8f", 8), ("ew", 128), ("efn", 128), ("efp", 128),
+                        ("half", 176), ("zero", 176), ("wt", 64), ("g8", 64), ("b8f", 16),
                         ("on32", 128), ("tmp", 128), ("col", 48)])
-_pack("ch", "float16", [("thrb", 128), ("dumc", 16), ("pc", 8)])
+_pack("ch", "float16", [("thrb", 128), ("dumc", 16), ("pc", 8), ("ch1k", 8)])
 PADW = 272 + 3 * 144
 _pack("pad", "float16", [(x + str(c), w) for c in range(NC) for x, w in (("padw", 272), ("padh", 144), ("padn", 144), ("padp", 144))])
 _pack("padb", "bfloat16", [("pada0", 144), ("pada1", 144), ("fl0", 16), ("fl1", 16)])
 _bufs("bfloat16", REM, ("tab0", "tab2", "tab3"))
-_bufs("bfloat16", H + 16, ("rem0", "rem1", "rem2"))
+_bufs("bfloat16", H, ("rem0", "rem1", "rem2"))
 _bufs("bfloat16", H, ("e10", "e11", "e20", "e21", "xc0", "xc1", "mx0", "mx1", "kc0", "kc1"))
 _bufs("bfloat16", V, ("cln", "clc", "fin"))
 _bufs("bfloat16", L, ("zi", "zb", "e0", "kw", "kwc", "qw", "qx", "src", "sa", "sb", "f1", "r2", "qc", "hb", "ug", "kvr", "xs"))
 _bufs("bfloat16", 2 * L, ("kvn", "qa", "qb"))
-_bufs("float16", L, ("bv", "nm", "cdh", "wm", "vr0", "vr1"))
-_bufs("float32", L, ("r16", "pz", "v2", "ds", "bn", "yzf", "wT"))
+_bufs("float16", L, ("bv", "nm", "cdh", "wm", "vr0", "vr1", "r16", "wT"))
+_bufs("float32", L, ("pz", "v2", "ds", "bn", "yzf"))
 _bufs("float32", 288, ("sc", "ad", "val"))
 _bufs("int32", L, ("pi", "pj", "pk"))
 _bufs("uint16", L, ("cd", "pl"))
@@ -70,7 +75,7 @@ SCRATCH["e3"] = ("sbuf", [128, 3072], "bfloat16")
 for _b in range(8):
     SCRATCH["ps%d" % _b] = ("psum", [128, 512], "float32")
 SEMAPHORES = ["qv", "qs", "qp", "qg"] + ["d%d" % i for i in range(40)] \
-    + [a + str(i) for a in ("pusha", "pushb", "pla", "plb", "rvs", "rvl", "rws", "rwl") for i in range(3)]
+    + [a + str(i) for a in ("push", "pl", "rvs", "rvl", "rws") for i in range(3)]
 
 
 def rank_program(g, core, T, topo):
@@ -178,8 +183,10 @@ def rank_program(g, core, T, topo):
                 return g.scalar.activation(out[1], a[1], fn, bias=x, scale=y, accum_out=acc[1])
         return op("s", a[2] * (GA if len(a) > 3 else 1.0) * CYC + SF, a[0] + r + r2, out[0] + (acc[0] if acc else []), call)
 
-    def take(who, out, a):
-        return cp(out, a) if ENG[who] == "v" else act(out, a)
+    def take(who, out, a, add=None):
+        if ENG[who] == "s":
+            return act(out, a, bias=add or 0.0)
+        return cp(out, a) if add is None else ts(out, a, add, None, OP.add)
 
     def mms(out, pairs, start=True, stop=True, tok=None):
         prs = [(p[2] if len(p) > 2 else out, p[0], p[1]) for p in pairs]
@@ -221,15 +228,19 @@ def rank_program(g, core, T, topo):
     def hbm(name, lo, hi):
         return ([("hbm_" + name, lo, hi)], T[name][:, lo:hi], hi - lo)
 
-    def remote(dst, src, out, frm, rsem, lsem, nbytes):
-        rid, pid, _se = topo.addr(dst)
-        msk = topo.mask(core, dst)
-        ne = len(topo.engines(core, dst))
-        op("g", 1000, src[0], [], lambda: g.remote_dma(out[1], src[1], T.sem[rsem], T.sem[lsem], pid, rid, msk),
-           sem=lsem, val=ne, lat=2000 + nbytes / 60.0)
-        ops[-1]["remote"] = True
-        op("ext", 0, [], out[0], None, sem=rsem, val=len(topo.engines(frm, core)))
-        ops[-1]["after"] = len(ops) - 2
+    def remote(src, parts, lsem, lat, after=()):
+        trs, ne = [], 0
+        for k, (dst, out, frm, rsem) in enumerate(parts):
+            rid, pid, _se = topo.addr(dst)
+            es = topo.engines(core, dst)[k::len(parts)]
+            ne += len(es)
+            trs.append(RemoteDMATransfer(dst_ids=[DstId(rid=rid, pnc=pid)], dma_engine_mask=sum(1 << e for e in es),
+                                         remote_sem=T.sem[rsem], src=src[1], dst=out[1]))
+        i = op("g", 1000, src[0] + list(after), [], lambda: g.remote_dma_fused(trs, local_sem=T.sem[lsem]), sem=lsem, val=ne, lat=lat)
+        ops[i]["remote"] = True
+        for k, (dst, out, frm, rsem) in enumerate(parts):
+            j = op("ext", 0, [], out[0], None, sem=rsem, val=len(topo.engines(frm, core)[k::len(parts)]))
+            ops[j]["after"] = i
 
     def P(b, lo, hi, st=1, parts=None): return A("ps%d" % b, lo, hi, st, parts)
     def SU(c, lo, hi, st=1, parts=None): return P(2 + c, lo, hi, st, parts)
@@ -249,10 +260,10 @@ def rank_program(g, core, T, topo):
             return [(A(nm + str(c), 15 - q, 143 - q), A(sel, q, 128, 16)) for q in range(16)]
         return [(A(nm + str(c), 15 - q, 143 - q), A(sel, n * q, n * q + n)) for q in range(16)]
 
-    dma("s", A("zi"), hbm("z0", 0, L), 0, lat=LZ)
-    dma("y", A("nb", 0, V), hbm("nbr", 0, V), 0, lat=LN)
-    dma("s", A("tab0", 0, V), hbm("ring", 0, V), 0, lat=LR)
-    dma("s", A("thi"), hbm("thr", 0, 1), 0, lat=LR)
+    for k, (nm, src, w, lat) in enumerate((("zi", "z0", L, LZ), ("nb", "nbr", V, LN), ("tab0", "ring", V, LR), ("thi", "thr", 1, LR))):
+        bon[0] = 1e6 * (4 - k)
+        dma("y", A(nm, 0, w), hbm(src, 0, w), 0, lat=lat)
+    bon[0] = 0.0
     dma("y", A("X", 0, PL), hbm("mat", 0, PL), 0, after=("nb", "tab0"), lat=LX)
     dma("y", A("X", PL, 2 * PL), hbm("mat", 0, PL), 0, after=("X",), lat=LX)
 
@@ -280,15 +291,17 @@ def rank_program(g, core, T, topo):
     for nm, s in (("im", -1.0), ("ih", 0.5), ("iq", -0.25), ("i1k", 1024.0), ("i3", 3.0 / 4096),
                   ("im69", -2.0 ** 69), ("i256", -256.0), ("i512", -512.0)):
         act(A(nm), I1, AF.Copy, scale=s)
+    act(A("bo16"), A("bo1"), AF.Copy, scale=0.0625)
     for t in range(NR):
-        ts(col(5 + t), col(1), -1.0, float(16 + t), OP.mult, OP.add)
+        ts(col(5 + t), col(1), -0.0625, 1 + t / 16, OP.mult, OP.add)
         act(A("yc%d" % t), row128, scale=0.0, bias=col(5 + t))
         ts(A("ipc", 2 + t, 3 + t), col(1), 811.0, float(t), OP.mult, OP.add)
     ts(A("ipc", 5, 8), A("ipc", 2, 5), PL - 1, None, OP.bitwise_and)
     cp(col(8, 3), A("ipc", 5, 8))
     ts(col(11), col(8), 4.0, None, OP.mult)
-    for nm, lo, x in (("sv", 0, S17), ("se", 0, 17 * S17), ("sd", 0, 32.0), ("sd", 8, 1.0), ("b8f", 0, 1.0)):
+    for nm, lo, x in (("sv", 0, S17), ("se", 0, 17 * S17), ("sd", 0, 32.0), ("sd", 8, 1.0), ("b8f", 0, 1.0), ("b8f", 8, 1.0)):
         act(A(nm, lo, lo + 8), B8, AF.Copy, scale=x)
+    act(A("ch1k"), A("row", 0, 8), scale=0.0, bias=-1023.5)
     for lo in (0, 144):
         ts(A("ksc", lo, lo + 144), A("j18"), -4096.0, 15 * 4096 - 2.5 * S17, OP.mult, OP.add)
     for lo, x in ((16, 0.0), (17, -35 * S17), (160, 0.0), (161, 16 * S17)):
@@ -335,15 +348,14 @@ def rank_program(g, core, T, topo):
     ts(A("tmp", 0, 16), A("jr", 0, 16), col(1), None, OP.is_equal)
     tt(A("tmp", 16, 32), A("tmp", 0, 16), A("pw2", 0, 16), OP.mult)
     red(col(21), A("tmp", 16, 32), OP.add)
-    ts(col(24, 8), A("b8f"), col(21), None, OP.mult)
+    ts(col(24, 8), A("b8f", 0, 8), col(21), None, OP.mult)
     for g2 in range(8):
         ts(A("wt", g2, 64, 8), A("pw2", 63, 176, 16), col(24 + g2), None, OP.mult)
     bon[0] = 0.0
 
     def pushes(t):
-        for x, lo, hi, to in (("a", 1024, 2048, 0), ("b", 0, 1026, 1024)):
-            remote(prv, A(TAB[t], lo, hi), A("rem%d" % t, to, to + hi - lo), nxt, "push%s%d" % (x, t), "pl%s%d" % (x, t),
-                   256 * (hi - lo))
+        remote(A(TAB[t], 0, H), [(prv, A("rem%d" % t), nxt, "push%d" % t)], "pl%d" % t, LP,
+               A("ra%d" % (t - 1), 0, 1)[0] if t else ())
 
     pushes(0)
 
@@ -357,17 +369,17 @@ def rank_program(g, core, T, topo):
         a = NL * c
         if t == 0:
             take("kv", kv("kvn", c, 0), A("tab0", 10 * a, 10 * (a + NL), 10))
-            ts(ck("bv", c), A("nb", 10 * a, 10 * (a + NL), 10), -MID, None, OP.add)
+            take("bv", ck("bv", c), A("nb", 10 * a, 10 * (a + NL), 10), -MID)
         else:
             vl = cw("wl%d" % (t - 1), c)
             take("kv", kv("kvn", c, 0), ind(tabw(t), vl))
-            ts(ck("bv", c), ind(A("nb", 0, V), vl), -MID, None, OP.add)
+            take("bv", ck("bv", c), ind(A("nb", 0, V), vl), -MID)
 
     def stage_n(t, c):
         a = NL * c
         y, m = MI(c, 128, 256), MI(c, 0, 128)
-        mms(y, [(A("bo1"), ck(zbuf(t), c)), (I1, A("yc%d" % t))])
-        rnd(ck("r16", c), y, 4)
+        mms(y, [(A("bo16"), ck(zbuf(t), c)), (I1, A("yc%d" % t)), (A("i1k"), A("ones"))])
+        take("r16", ck("r16", c), y)
         tt(m, y, ck("r16", c), OP.is_equal)
         tt(ck("nm", c), ck("bv", c), m, OP.mult)
         mms(MI(c, 384, 392), [(A("u1", 15 - q, 143 - q), A("nm", a + q, a + NL, 16)) for q in range(16)])
@@ -378,7 +390,7 @@ def rank_program(g, core, T, topo):
         for s in range(SUBK):
             act(A(kc, 16 * w * s, 16 * w * (s + 1)), ind(tabw(t), A("cd", a + w * s, a + w * s + w)))
         take("kn", kv("kvn", c, 1), ind(tabw(t), cw("nl", c)))
-        ts(ck("cdh", c), ck("cd", c), -MID, None, OP.add)
+        take("cdh", ck("cdh", c), ck("cd", c) if ENG["cdh"] == "v" else ind(A("nb", 0, V), cw("nl", c)), -MID)
         for nm, r in zip(("qa", "qb"), dead(t)):
             ts(A(nm, 256 * c, 256 * c + 256), A("kvn", 256 * c, 256 * c + 256), r, r, OP.is_equal, OP.mult)
 
@@ -390,12 +402,12 @@ def rank_program(g, core, T, topo):
 
     def stage_h(t, c):
         tt(ck("pz", c), ck(zbuf(t), c), kone(1), OP.mult)
-        mms(MI(c, 392, 400), [(ck("pz", c), A("b8f"))])
-        rnd(cw("hH", c), MI(c, 392, 400), 11)
+        mms(MI(c, 392, 408), [(ck("pz", c), A("b8f")), (I1, A("ch1k"), MI(c, 400, 408))])
+        rnd(cw("hH", c), MI(c, 400, 408), 11)
         tt(pad("padh", c), MI(c, 392, 400), cw("hH", c), OP.subtract)
-        mms(MI(c, 400, 408), wrap("padh", c))
-        ts(cw("hl", c), MI(c, 400, 408), 1024.0, None, OP.add)
-        act(ck("src", c), ind(A("rem%d" % t, 0, H + 1), cw("hl", c)))
+        mms(MI(c, 436, 444), wrap("padh", c))
+        cp(cw("hl", c), MI(c, 436, 444))
+        act(ck("src", c), ind(A("rem%d" % t), cw("hl", c)))
         for nm, r in [("sa", A("rc%d" % max(t - 1, 0), 0, 1)), ("sb", A("ra0", 0, 1))][:t]:
             ts(ck(nm, c), ck("src", c), r, None, OP.is_equal)
 
@@ -422,7 +434,11 @@ def rank_program(g, core, T, topo):
                 bon[0] -= BT["h"][c]
             for b in range(16 // REP):
                 lo, hi = 128 * REP * b, 128 * REP * (b + 1)
-                tt(A(e, lo, hi), A(kc, b, H, 16 // REP), P(x, 0, 128 * REP), OP.is_equal)
+                nh = 2 if x < HV else 1
+                for h in range(nh):
+                    w = 128 * REP // nh
+                    tt(A(e, lo + w * h, lo + w * h + w), A(kc, H // nh * h + b, H // nh * (h + 1), 16 // REP),
+                       P(x, w * h, w * h + w), OP.is_equal)
                 if x == 1:
                     mms(None, [(ek(1, b, j), A("sv"), on(b + 16 // REP * j, 18)) for j in range(REP)], False, hi == H, tk)
             if x == 0:
@@ -478,7 +494,7 @@ def rank_program(g, core, T, topo):
             wb = SU(c, 128, 256)
             mms(wb, [(A("ew", parts=16), A("wT", a, a + NL, parts=16))], tok=tk)
             act(ck("v2", c), wb, scale=2.0, bias=2 * MID + 1)
-            cp(ck("vr%d" % ((t + 1) & 1), c), wb)
+            take("vr", ck("vr%d" % ((t + 1) & 1), c), wb)
             tt(ck("wm", c), ck("vr%d" % ((t + 1) & 1), c), MI(c, 0, 128), OP.mult)
 
     def e3(c1, c):
@@ -538,12 +554,15 @@ def rank_program(g, core, T, topo):
         for b in range(4):
             bk = 4 + nb_[0] % 2
             nb_[0] += 1
-            mms(None, [(I1, A(xc, 4 * b + j, H, 16), P(bk, 128 * j, 128 * j + 128)) for j in range(4)]
-                + [(IM, z, P(bk, 128 * j, 128 * j + 128)) for j in range(4)])
-            act(A(mx, 512 * b, 512 * b + 512), P(bk, 0, 512), AF.Abs)
-            prs = [(I1, A("pt"), SU(c, 0, 128)), (A("thrb"), IM, SU(c, 128, 256))] if b == 0 else []
-            mms(None, prs + [(A(mx, 128 * p, 128 * p + 128), A("sd"), SU(c, p, 256, 16)) for p in range(4 * b, 4 * b + 4)],
-                b == 0, b == 3, tk)
+            h, r = b // 2, b % 2
+            mms(P(bk, 0, 512), [(I1, A(xc, 1024 * h + r, 1024 * h + 1024, 2))]
+                + [(IM, A(zbuf(t), a + 64 * h, a + 64 * h + 64), P(bk, j, 512, 8)) for j in range(8)])
+            act(A(mx, 1024 * r + 512 * h, 1024 * r + 512 * h + 512), P(bk, 0, 512), AF.Abs)
+            if b == 0:
+                mms(None, [(I1, A("pt"), SU(c, 0, 128)), (A("thrb"), IM, SU(c, 128, 256))], True, False, tk)
+            if h == 1:
+                mms(None, [(A(mx, 1024 * r + j, 1024 * r + 1024, 8), A("sd"), SU(c, r + 2 * j, 256, 16)) for j in range(8)],
+                    False, r == 1, tk)
         tk = ("r", 2 + c)
         scan(ck("ds", c), A("mnm"), SU(c, 0, 128), OP.max, OP.min)
         last = A("ds", a + 15, a + NL, 16)
@@ -585,8 +604,10 @@ def rank_program(g, core, T, topo):
         rnd(A("rr", 1, 2), A("rr", 0, 1), 9)
         tt(ra, A("rr", 0, 1), A("rr", 1, 2), OP.subtract)
         if t < NR - 1:
-            remote(prv, ra, A("rc%d" % t, 0, 1), nxt, "rws%d" % t, "rwl%d" % t, 512)
-            remote(nxt, ra, A("rb%d" % t, 0, 1), prv, "rvs%d" % t, "rvl%d" % t, 512)
+            bon[0] = 1e5
+            remote(ra, [(prv, A("rc%d" % t, 0, 1), nxt, "rws%d" % t), (nxt, A("rb%d" % t, 0, 1), prv, "rvs%d" % t)], "rvl%d" % t, LV)
+            bon[0] = 0.0
+            pushes(t + 1)
         if t == 0:
             clean("tab2", "tab0", "tab2", ra, 6)
         elif t == 1:
@@ -627,7 +648,6 @@ def rank_program(g, core, T, topo):
         for c in range(NC):
             st("f", t, c)
         if t < NR - 1:
-            pushes(t + 1)
             failures(t)
         if t == 1:
             clean("tab3", "tab2", "tab3", A("rb0", 0, 1), 7)
@@ -637,34 +657,15 @@ def rank_program(g, core, T, topo):
     _emit(g, T, ops)
 
 
-def _emit(g, T, ops):
+def _plan(ops, pred, succ, prio, back):
     n = len(ops)
-    succ = [[] for _ in range(n)]
-    for i, o in enumerate(ops):
-        if "after" in o:
-            o["deps"][o["after"]] = False
-        for j in o["deps"]:
-            succ[j].append(i)
-    prio = [0.0] * n
-    for i in range(n - 1, -1, -1):
-        o = ops[i]
-        prio[i] = o["dur"] + o["lat"] + max([prio[s] + WK for s in succ[i]], default=0.0)
-    prio = [p + o["bon"] for p, o in zip(prio, ops)]
-    left = [len(o["deps"]) for o in ops]
-    fin = [0.0] * n
-    qfree, ready, order, bank = {}, {}, [], {}
-    est = [0.0] * n
+    left = [len(p) for p in pred]
+    fin, est = [0.0] * n, [0.0] * n
+    qfree, ready, order, bank, turns = {}, {}, [], {}, [[] for _ in range(n)]
 
     def push(i):
-        o = ops[i]
-        e = 0.0
-        for j, hard in o["deps"].items():
-            if "after" in o and j == o["after"]:
-                e = max(e, fin[j])
-            elif hard:
-                e = max(e, fin[j] + WK)
-        est[i] = e
-        ready.setdefault(o["q"], []).append(i)
+        est[i] = max([fin[j] + w for j, w in pred[i]], default=0.0) + (ops[i]["lat"] if back else 0.0)
+        ready.setdefault(ops[i]["q"], []).append(i)
 
     def start(i):
         o = ops[i]
@@ -675,30 +676,58 @@ def _emit(g, T, ops):
     while len(order) < n:
         best = None
         for q, rs in ready.items():
-            if not rs:
-                continue
-            f = 0.0 if q == "ext" else qfree.get(q, 0.0)
-            t0 = max(f, min(start(i) for i in rs))
-            if best is None or t0 < best[0]:
-                best = (t0, q)
-        t0, q = best
-        rs = ready[q]
-        i = max([i for i in rs if start(i) <= t0 + 30.0], key=lambda k: (prio[k], -k))
-        rs.remove(i)
+            if rs:
+                ss = [(start(i), i) for i in rs]
+                t0 = max(0.0 if q == "ext" else qfree.get(q, 0.0), min(ss)[0])
+                if best is None or t0 < best[0]:
+                    best = (t0, q, ss)
+        t0, q, ss = best
+        i = max([i for s, i in ss if s <= t0 + SLACK], key=lambda k: (prio[k], -k))
+        soon = [k for s, k in ss if s <= t0 + HOLD * ops[i]["dur"] and prio[k] > prio[i] + ops[i]["dur"]]
+        if soon:
+            i = max(soon, key=lambda k: (prio[k], -k))
+        ready[q].remove(i)
         o = ops[i]
         st = max(t0, start(i))
         for b in o["banks"]:
-            for q2, j in bank.setdefault(b, {}).items():
-                if q2 != q:
-                    o["deps"][j] = True
+            turns[i] += [j for q2, j in bank.setdefault(b, {}).items() if q2 != q]
             bank[b][q] = i
         qfree[q] = st + o["dur"]
-        fin[i] = st + o["dur"] + o["lat"]
+        fin[i] = st + o["dur"] + (0.0 if back else o["lat"])
         order.append(i)
-        for s in succ[i]:
+        for s, w in succ[i]:
             left[s] -= 1
             if left[s] == 0:
                 push(s)
+    return max(fin), fin, order, turns
+
+
+def _emit(g, T, ops):
+    n = len(ops)
+    pred, succ = [[] for _ in range(n)], [[] for _ in range(n)]
+    for i, o in enumerate(ops):
+        if "after" in o:
+            o["deps"][o["after"]] = False
+        for j, hard in o["deps"].items():
+            pred[i].append((j, WK if hard else 0.0))
+            succ[j].append((i, WK if hard else 0.0))
+    if not PLAN:
+        prio = [0.0] * n
+        for i in range(n - 1, -1, -1):
+            prio[i] = ops[i]["dur"] + ops[i]["lat"] + max([prio[s] + w for s, w in succ[i]], default=0.0)
+        best = None
+        rng = np.random.default_rng(SEED)
+        for k in range(PASSES):
+            r = _plan(ops, pred, succ, [p + o["bon"] for p, o in zip(prio, ops)], False)
+            if best is None or r[0] < best[0]:
+                best = r
+            ends = r[1] if k % 4 < 3 else best[1]
+            prio = _plan(ops, succ, pred, [e + x for e, x in zip(ends, rng.random(n) * JIT)], True)[1]
+        PLAN.append(best)
+    order = PLAN[0][2]
+    for i in range(n):
+        for j in PLAN[0][3][i]:
+            ops[i]["deps"][j] = True
     eng = {"v": g.vector, "s": g.scalar, "p": g.tensor, "g": g, "y": g.sync}
     known = {q: {} for q in eng}
     count, semof, clock = {}, {}, {}

@@ -8,20 +8,23 @@ V, PL, L, NR, H = 2688, 4096, 256, 3, 2048
 REM = V + L
 NC, NL = 2, 128
 MID = 1344.0
-S17 = float(2 ** 17)
+OFF = 1088.0
 BIG = float(2 ** 20)
 TINY = 2.0 ** -60
 CAP = 64
 REP = 4
-CYC, PEC, VF, SF, PF, WK, GA, SCA = 0.9, 0.46, 60.0, 60.0, 8.0, 70.0, 1.55, 3.0
+CYC, PEC, VF, SF, PF, WK, GA, SCA = 0.9, 0.46, 60.0, 150.0, 5.0, 70.0, 1.4, 3.0
 LZ, LN, LR, LX = 3000.0, 8000.0, 10500.0, 6000.0
-LP, LV = 12000.0, 5000.0
+LP, LV = 17000.0, 15000.0
 BT = {"k": 0.0, "v": (0.0, 0.0), "n": (0.0, 0.0), "h": (0.0, 0.0), "c": (0.0, 0.0), "w": (0.0, 0.0),
       "f": (0.0, 0.0), "d": (0.0, 0.0), "e": 0.0, "cl": 0.0}
-ENG = {"kn": "s", "kw": "s", "kv": "s", "fl": "s", "bv": "s", "cdh": "v", "vr": "s", "r16": "s"}
-HV, HX = 1, 1
+ENG = {"k01": "s", "k10": "s", "k11": "s", "k20": "s", "k21": "s"}
+DV = ((), (), ())
+NS = (0, 0)
+HV = (1, 1)
 SUBK, SUBX, CLP = 2, 2, 3
-SLACK, HOLD, PASSES, JIT, SEED = 30.0, 0.3, 40, 200.0, 1
+SLACK, HOLD, PASSES, JIT, SEED = 30.0, 0.3, 250, 1000.0, 1
+TEMP, WIN, LEAN = 1500.0, 20000.0, 150.0
 PLAN = []
 ALIAS = {}
 SCRATCH = {}
@@ -40,14 +43,14 @@ def _bufs(dtype, width, names):
         SCRATCH[nm] = ("sbuf", [128, width], dtype)
 
 
-_pack("cb", "bfloat16", [(x, 128) for x in ("i1", "im", "ih", "iq", "bo1", "i1k", "lt", "ones", "i3", "im69", "i256",
+_pack("cb", "bfloat16", [(x, 128) for x in ("i1", "im", "ih", "bo1", "i1k", "lt", "ones", "i3", "im69", "i256",
                                             "i512", "pt", "yc0", "yc1", "yc2", "bo16", "ew", "efn", "efp")]
-      + [("u1", 144), ("i18", 144), ("ksc", 288), ("tiny", 512), ("io", 256), ("rx", 1024), ("rxi", 1024), ("axc", 64),
-         ("sv", 8), ("se", 8), ("sd", 16), ("c69", 8), ("c75", 8)])
+      + [("u1", 144), ("i18", 144), ("sn", 8), ("b8", 8), ("coff", 16), ("io", 256), ("rx", 1024), ("rxi", 1024), ("axc", 64),
+         ("sv", 8), ("se", 8), ("sd", 16), ("sd2", 16), ("sdm", 16), ("zm", 128), ("c69", 8), ("c75", 8)])
 _pack("cf", "float32", [("row", 256), ("jr", 128), ("j18", 144), ("m16", 128), ("mxm", 144), ("mnm", 128), ("pw2", 176),
                         ("half", 176), ("zero", 176), ("wt", 64), ("g8", 64), ("b8f", 16),
                         ("on32", 128), ("tmp", 128), ("col", 48)])
-_pack("ch", "float16", [("thrb", 128), ("dumc", 16), ("pc", 8), ("ch1k", 8)])
+_pack("ch", "float16", [("thrb", 128), ("dumc", 16), ("pc", 8), ("ch1k", 8), ("ksc", 288), ("th", 16), ("hH", 16)])
 PADW = 272 + 3 * 144
 _pack("pad", "float16", [(x + str(c), w) for c in range(NC) for x, w in (("padw", 272), ("padh", 144), ("padn", 144), ("padp", 144))])
 _pack("padb", "bfloat16", [("pada0", 144), ("pada1", 144), ("fl0", 16), ("fl1", 16)])
@@ -55,9 +58,9 @@ _bufs("bfloat16", REM, ("tab0", "tab2", "tab3"))
 _bufs("bfloat16", H, ("rem0", "rem1", "rem2"))
 _bufs("bfloat16", H, ("e10", "e11", "e20", "e21", "xc0", "xc1", "mx0", "mx1", "kc0", "kc1"))
 _bufs("bfloat16", V, ("cln", "clc", "fin"))
-_bufs("bfloat16", L, ("zi", "zb", "e0", "kw", "kwc", "qw", "qx", "src", "sa", "sb", "f1", "r2", "qc", "hb", "ug", "kvr", "xs"))
+_bufs("bfloat16", L, ("zi", "zb", "e0", "kw", "kwc", "qw", "qx", "src", "sa", "sb", "f1", "r2", "qc", "hb", "ug", "kvr", "knp"))
 _bufs("bfloat16", 2 * L, ("kvn", "qa", "qb"))
-_bufs("float16", L, ("bv", "nm", "cdh", "wm", "vr0", "vr1", "r16", "wT"))
+_bufs("float16", L, ("bv", "nm", "cdh", "wm", "vr0", "vr1", "r16", "wT", "xs"))
 _bufs("float32", L, ("pz", "v2", "ds", "bn", "yzf"))
 _bufs("float32", 288, ("sc", "ad", "val"))
 _bufs("int32", L, ("pi", "pj", "pk"))
@@ -66,8 +69,8 @@ _bufs("float32", 4, ("ra0", "ra1", "ra2", "rb0", "rb1", "rc0", "rc1"))
 _bufs("float32", 16, ("fs", "rr"))
 _bufs("int32", 8, ("ipc",))
 _pack("smu", "uint16", [(x, 16) for x in ("nl", "pw", "hl", "sl", "wl0", "wl1", "wl2")])
-_pack("sm32", "float32", [(x, 16) for x in ("hH", "sy", "pH", "v320", "v321")])
-_pack("smb", "bfloat16", [("th", 16), ("rw", 128), ("rw2", 64)])
+_pack("sm32", "float32", [(x, 16) for x in ("sy", "pH", "v320", "v321")])
+_pack("smb", "bfloat16", [("rw", 128), ("rw2", 64)])
 SCRATCH["nb"] = ("sbuf", [128, REM], "int32")
 SCRATCH["X"] = ("sbuf", [128, 2 * PL], "bfloat16")
 SCRATCH["thi"] = ("sbuf", [128, 1], "int32")
@@ -84,7 +87,7 @@ def rank_program(g, core, T, topo):
         return
     nranks = len(T.cores)
     nxt, prv = T.cores[(rank + 1) % nranks], T.cores[(rank - 1) % nranks]
-    ops, hist, ndma, bon, nb_ = [], {}, [0], [0.0], [0]
+    ops, hist, ndma, bon, nb_, dry = [], {}, [0], [0.0], [0], []
 
     def A(name, lo=0, hi=None, st=1, parts=None):
         if name in ALIAS:
@@ -103,6 +106,10 @@ def rank_program(g, core, T, topo):
         return (win[0] + lst[0], win[1].indirect(lst[1]), 16 * lst[2], 1)
 
     def op(q, dur, rd, wr, call, sem=None, val=1, lat=0.0):
+        if dry:
+            if dry[0] == 1:
+                return dur, rd, call
+            rd = rd + dry.pop()
         i = len(ops)
         deps = {}
         for regs, w in ((rd, 0), (wr, 1)):
@@ -183,10 +190,26 @@ def rank_program(g, core, T, topo):
                 return g.scalar.activation(out[1], a[1], fn, bias=x, scale=y, accum_out=acc[1])
         return op("s", a[2] * (GA if len(a) > 3 else 1.0) * CYC + SF, a[0] + r + r2, out[0] + (acc[0] if acc else []), call)
 
-    def take(who, out, a, add=None):
-        if ENG[who] == "s":
-            return act(out, a, bias=add or 0.0)
-        return cp(out, a) if add is None else ts(out, a, add, None, OP.add)
+    def either(who, vec, sca):
+        e = ENG.get(who, "a")
+        if e != "a":
+            return vec() if e == "v" else sca()
+        dry.append(1)
+        dur, rd, call = sca()
+        dry[0] = rd
+        i = vec()
+        ops[i]["alt"] = {"v": (ops[i]["dur"], ops[i]["call"]), "s": (dur, call)}
+        return i
+
+    def take(who, out, a, add=None, mul=None):
+        def vec():
+            if mul is not None:
+                return ts(out, a, mul, add or 0.0, OP.mult, OP.add)
+            return cp(out, a) if add is None else ts(out, a, add, None, OP.add)
+        return either(who, vec, lambda: act(out, a, bias=add or 0.0, scale=mul or 1.0))
+
+    def relu(who, out, a, add):
+        return either(who, lambda: ts(out, a, add, 0.0, OP.add, OP.max), lambda: act(out, a, AF.Relu, bias=add))
 
     def mms(out, pairs, start=True, stop=True, tok=None):
         prs = [(p[2] if len(p) > 2 else out, p[0], p[1]) for p in pairs]
@@ -265,7 +288,6 @@ def rank_program(g, core, T, topo):
         dma("y", A(nm, 0, w), hbm(src, 0, w), 0, lat=lat)
     bon[0] = 0.0
     dma("y", A("X", 0, PL), hbm("mat", 0, PL), 0, after=("nb", "tab0"), lat=LX)
-    dma("y", A("X", PL, 2 * PL), hbm("mat", 0, PL), 0, after=("X",), lat=LX)
 
     bon[0] = BT["k"]
     iota(A("ipc", 0, 1), [[0, 1]], 0, 1)
@@ -287,8 +309,8 @@ def rank_program(g, core, T, topo):
     ts(I1, row128, col(0), None, OP.is_equal)
     ts(A("bo1"), A("m16"), col(2), None, OP.is_equal)
     ts(A("u1"), row144, col(3), None, OP.is_equal)
-    ts(A("i18"), row144, col(4), None, OP.is_equal)
-    for nm, s in (("im", -1.0), ("ih", 0.5), ("iq", -0.25), ("i1k", 1024.0), ("i3", 3.0 / 4096),
+    ts(A("i18"), row144, col(4), 1 / 4096, OP.is_equal, OP.mult)
+    for nm, s in (("im", -1.0), ("ih", 0.5), ("i1k", 1024.0), ("i3", 3.0),
                   ("im69", -2.0 ** 69), ("i256", -256.0), ("i512", -512.0)):
         act(A(nm), I1, AF.Copy, scale=s)
     act(A("bo16"), A("bo1"), AF.Copy, scale=0.0625)
@@ -299,18 +321,24 @@ def rank_program(g, core, T, topo):
     ts(A("ipc", 5, 8), A("ipc", 2, 5), PL - 1, None, OP.bitwise_and)
     cp(col(8, 3), A("ipc", 5, 8))
     ts(col(11), col(8), 4.0, None, OP.mult)
-    for nm, lo, x in (("sv", 0, S17), ("se", 0, 17 * S17), ("sd", 0, 32.0), ("sd", 8, 1.0), ("b8f", 0, 1.0), ("b8f", 8, 1.0)):
+    for nm, lo, x in (("sv", 0, 32.0), ("se", 0, 17 * 32.0), ("sd", 0, 32.0), ("sd", 8, 1.0), ("b8f", 0, 1 / 2048), ("b8f", 8, 1 / 2048),
+                      ("sn", 0, 1 / 4096), ("b8", 0, 1.0)):
         act(A(nm, lo, lo + 8), B8, AF.Copy, scale=x)
-    act(A("ch1k"), A("row", 0, 8), scale=0.0, bias=-1023.5)
+    if any(DV):
+        act(A("sd2"), A("sd"), AF.Copy, scale=2.0)
+        act(A("sdm"), A("sd"), AF.Copy, scale=-1.0)
+        act(A("zm", 0, 64), A("bo1", 0, 128, 2), AF.Copy, scale=-32.0)
+        act(A("zm", 64, 128), A("bo1", 0, 128, 2), AF.Copy, scale=-1.0)
+    act(A("ch1k"), A("row", 0, 8), scale=0.0, bias=-1023.5 / 2048)
+    act(A("coff"), A("row", 0, 16), scale=0.0, bias=OFF)
     for lo in (0, 144):
-        ts(A("ksc", lo, lo + 144), A("j18"), -4096.0, 15 * 4096 - 2.5 * S17, OP.mult, OP.add)
-    for lo, x in ((16, 0.0), (17, -35 * S17), (160, 0.0), (161, 16 * S17)):
-        ts(A("ksc", lo, lo + 127, 18), A("row", 0, 8), 0.0, x, OP.mult, OP.add)
+        act(A("ksc", lo, lo + 144), A("j18"), scale=-1.0, bias=OFF + 15 - 2.5 * 32)
+    for lo, x in ((16, 0.0), (17, -35 * 32.0), (160, 0.0), (161, 16 * 32.0)):
+        act(A("ksc", lo, lo + 127, 18), A("row", 0, 8), scale=0.0, bias=OFF + x)
     ts(A("mxm"), A("j18"), 0.5, 2e9, OP.is_ge, OP.mult)
     act(A("mxm"), A("mxm"), bias=-1e9)
     ts(A("mnm"), j128, 0.5, -2e9, OP.is_ge, OP.mult)
     act(A("mnm"), A("mnm"), bias=1e9)
-    fill(A("tiny"), TINY)
     fill(A("pad"), 0.0)
     fill(A("padb"), 0.0)
     fill(SU(0, 416, 417), BIG)
@@ -328,7 +356,7 @@ def rank_program(g, core, T, topo):
     ts(A("pc"), A("row", 0, 8), 256.0, col(14), OP.mult, OP.add)
     ts(col(15), col(0), 16.0, None, OP.mult)
     ts(col(16), col(0), 16.0, -128.0, OP.mult, OP.add)
-    ts(A("ew"), A("m16"), col(15), None, OP.is_equal)
+    ts(A("ew"), A("m16"), col(15), 4096.0, OP.is_equal, OP.mult)
     ts(A("efn"), A("m16"), col(16), -512.0, OP.is_equal, OP.mult)
     act(A("efp"), A("efn"), AF.Copy, scale=-1.0)
     bon[0] = 0.0
@@ -348,16 +376,18 @@ def rank_program(g, core, T, topo):
     ts(A("tmp", 0, 16), A("jr", 0, 16), col(1), None, OP.is_equal)
     tt(A("tmp", 16, 32), A("tmp", 0, 16), A("pw2", 0, 16), OP.mult)
     red(col(21), A("tmp", 16, 32), OP.add)
-    ts(col(24, 8), A("b8f", 0, 8), col(21), None, OP.mult)
+    ts(col(24, 8), A("b8"), col(21), None, OP.mult)
     for g2 in range(8):
         ts(A("wt", g2, 64, 8), A("pw2", 63, 176, 16), col(24 + g2), None, OP.mult)
     bon[0] = 0.0
 
     def pushes(t):
-        remote(A(TAB[t], 0, H), [(prv, A("rem%d" % t), nxt, "push%d" % t)], "pl%d" % t, LP,
-               A("ra%d" % (t - 1), 0, 1)[0] if t else ())
+        bon[0] = 1e5
+        remote(A(TAB[t], 0, H), [(prv, A("rem%d" % t), nxt, "push%d" % t)], "pl%d" % t, LP)
+        bon[0] = 0.0
 
     pushes(0)
+    dma("y", A("X", PL, 2 * PL), hbm("mat", 0, PL), 0, after=("X", "rem0"), lat=LX)
 
     def kv(nm, c, x): return A(nm, 256 * c + 128 * x, 256 * c + 128 * x + 128)
     def kone(x): return P(x, 0, 128 * REP, REP)
@@ -383,14 +413,14 @@ def rank_program(g, core, T, topo):
         tt(m, y, ck("r16", c), OP.is_equal)
         tt(ck("nm", c), ck("bv", c), m, OP.mult)
         mms(MI(c, 384, 392), [(A("u1", 15 - q, 143 - q), A("nm", a + q, a + NL, 16)) for q in range(16)])
-        ts(cw("nl", c), MI(c, 384, 392), MID, None, OP.add)
-        cp(ck("cd", c), ind(A("nb", 0, V), cw("nl", c)))
+        take("nl", cw("nl", c), MI(c, 384, 392), MID)
+        take("cd", ck("cd", c), ind(A("nb", 0, V), cw("nl", c)))
         kc = "kc%d" % c
         w = NL // SUBK
         for s in range(SUBK):
-            act(A(kc, 16 * w * s, 16 * w * (s + 1)), ind(tabw(t), A("cd", a + w * s, a + w * s + w)))
-        take("kn", kv("kvn", c, 1), ind(tabw(t), cw("nl", c)))
-        take("cdh", ck("cdh", c), ck("cd", c) if ENG["cdh"] == "v" else ind(A("nb", 0, V), cw("nl", c)), -MID)
+            take("k%d%d" % (t, c), A(kc, 16 * w * s, 16 * w * (s + 1)), ind(tabw(t), A("cd", a + w * s, a + w * s + w)), 4 * TINY)
+        take("kn", kv("kvn", c, 1), ind(tabw(t), cw("nl", c)), TINY)
+        take("cdh", ck("cdh", c), ck("cd", c), -MID)
         for nm, r in zip(("qa", "qb"), dead(t)):
             ts(A(nm, 256 * c, 256 * c + 256), A("kvn", 256 * c, 256 * c + 256), r, r, OP.is_equal, OP.mult)
 
@@ -398,16 +428,16 @@ def rank_program(g, core, T, topo):
         prs = []
         for lhs, nm in [(I1, "kvn"), (IM, "qa"), (IM, "qb")][:1 + t]:
             prs += [(lhs, kv(nm, c, x), P(x, j, 128 * REP, REP)) for j in range(REP)]
-        mms(P(x, 0, 128 * REP), prs + [(I1, A("tiny", 0, 128 * REP))])
+        mms(None, prs)
 
     def stage_h(t, c):
         tt(ck("pz", c), ck(zbuf(t), c), kone(1), OP.mult)
-        mms(MI(c, 392, 408), [(ck("pz", c), A("b8f")), (I1, A("ch1k"), MI(c, 400, 408))])
-        rnd(cw("hH", c), MI(c, 400, 408), 11)
+        mms(MI(c, 392, 408), [(ck("pz", c), A("b8f")), (I1, A("coff")), (I1, A("ch1k"), MI(c, 400, 408))])
+        take("hH", cw("hH", c), MI(c, 400, 408))
         tt(pad("padh", c), MI(c, 392, 400), cw("hH", c), OP.subtract)
         mms(MI(c, 436, 444), wrap("padh", c))
-        cp(cw("hl", c), MI(c, 436, 444))
-        act(ck("src", c), ind(A("rem%d" % t), cw("hl", c)))
+        take("hl", cw("hl", c), MI(c, 436, 444), None, 2048.0)
+        take("src", ck("src", c), ind(A("rem%d" % t), cw("hl", c)))
         for nm, r in [("sa", A("rc%d" % max(t - 1, 0), 0, 1)), ("sb", A("ra0", 0, 1))][:t]:
             ts(ck(nm, c), ck("src", c), r, None, OP.is_equal)
 
@@ -418,7 +448,7 @@ def rank_program(g, core, T, topo):
 
         def low(o, x):
             return [(I1, A("ksc", 144 * x, 144 * x + 144), o(0, 1)), (ck("cdh", c), A("i18"), o(0, 1)),
-                    (ck("nm", c), B8, o(16, 18)), (ck("nm", c), B8, o(17, 18))]
+                    (ck("nm", c), A("sn"), o(16, 18)), (ck("nm", c), A("sn"), o(17, 18))]
 
         def ov(lo, st): return MI(c, 128 + lo, 272, st)
         def on(lo, st): return SU(c, lo, 144, st)
@@ -434,7 +464,18 @@ def rank_program(g, core, T, topo):
                 bon[0] -= BT["h"][c]
             for b in range(16 // REP):
                 lo, hi = 128 * REP * b, 128 * REP * (b + 1)
-                nh = 2 if x < HV else 1
+                nh = 2 if x < HV[c] else 1
+                if x == 1 and b < NS[c]:
+                    if b == 0:
+                        take("knp", ck("knp", c), kone(1))
+                    bk = 4 + nb_[0] % 2
+                    nb_[0] += 1
+                    mms(P(bk, 0, 512), [(I1, A(kc, b, H, 4))] + [(IM, ck("knp", c), P(bk, j, 512, 4)) for j in range(4)])
+                    d = A("mx%d" % c, lo, hi)
+                    act(d, P(bk, 0, 512), AF.Abs)
+                    either("ez", lambda: ts(A(e, lo, hi), d, 0.0, None, OP.is_equal),
+                           lambda: act(A(e, lo, hi), d, AF.Relu, scale=-2 / TINY, bias=1.0))
+                    nh = 0
                 for h in range(nh):
                     w = 128 * REP // nh
                     tt(A(e, lo + w * h, lo + w * h + w), A(kc, H // nh * h + b, H // nh * (h + 1), 16 // REP),
@@ -445,21 +486,17 @@ def rank_program(g, core, T, topo):
                 tt(ck("e0", c), kv("kvn", c, 1), kone(0), OP.is_equal)
                 mms(None, low(ov, 0) + [(ck("e0", c), A("se"), ov(17, 18))]
                     + [(ek(0, b, j), A("sv"), ov(b + 16 // REP * j, 18)) for b in range(16 // REP) for j in range(REP)])
-                act(ad, ov(0, 1), AF.Copy)
-                act(ck("kvr", c), kone(0), AF.Relu, bias=-TINY)
+                take("ad", ad, ov(0, 1))
+                take("kvr", ck("kvr", c), kone(0))
         val = A("val", 144 * c, 144 * c + 144)
         tt(val, ad, on(0, 1), OP.min)
         scan(sc, A("mxm"), val, OP.min, OP.max)
         tot = A("sc", 144 * c + 17, 144 * c + 144, 18)
-        rnd(cw("th", c), tot, 12)
+        take("th", cw("th", c), tot)
         tt(pad("padw", c), tot, cw("th", c), OP.subtract)
-        fl = A("fl%d" % c, 8, 16)
-        if t < NR - 1 or ENG["fl"] == "s":
-            act(fl, cw("th", c), AF.Relu, scale=-2.0 ** -16, bias=1.0, acc=A("fs", c, c + 1))
-        else:
-            ts(fl, tot, 32768.0, None, OP.is_lt)
+        act(A("fl%d" % c, 8, 16), cw("th", c), AF.Relu, scale=-1.0, bias=OFF + 1, acc=A("fs", c, c + 1))
         mms(SU(c, 420, 428), wrap("padw", c), tok=("r", 2 + c))
-        ts(cw("wl%d" % t, c), SU(c, 420, 428), MID, None, OP.add)
+        take("wl", cw("wl%d" % t, c), SU(c, 420, 428), MID, 4096.0)
 
     def stage_w(t, c):
         a = NL * c
@@ -467,10 +504,10 @@ def rank_program(g, core, T, topo):
         src = ind(tabw(t), cw("wl%d" % t, c))
         if t == 0:
             tt(ck("pi", c), src, ck("v2", c), OP.mult)
-            act(ck("kwc", c), src)
+            take("kwc", ck("kwc", c), src)
             ts(ck("pj", c), ck("pi", c), col(11), None, OP.add)
             ts(ck("pk", c), ck("pj", c), 2, PL - 1, OP.arith_shift_right, OP.bitwise_and)
-            cp(ck("pl", c), ck("pk", c))
+            take("pl", ck("pl", c), ck("pk", c))
         else:
             take("kw", ck("kw", c), src)
             prs = [(I1, ck("kw", c))]
@@ -480,20 +517,21 @@ def rank_program(g, core, T, topo):
             mms(SU(c, 0, 128), prs, tok=tk)
             tt(ck("pi", c), ck("v2", c), SU(c, 0, 128), OP.mult)
             ts(ck("pk", c), ck("pi", c), 2, PL - 1, OP.arith_shift_right, OP.bitwise_and)
-            ts(ck("pl", c), ck("pk", c), col(8 + t), None, OP.add)
-            act(ck("kwc", c), SU(c, 0, 128), AF.Copy)
+            take("pl", ck("pl", c), ck("pk", c), col(8 + t))
+            take("kwc", ck("kwc", c), SU(c, 0, 128))
         w = NL // SUBX
         for s in range(SUBX):
-            act(A("xc%d" % c, 16 * w * s, 16 * w * (s + 1)),
-                ind(A("X", 0, PL if t == 0 else 2 * PL), A("pl", a + w * s, a + w * s + w)))
-        act(ck("hb", c), ck("kwc", c), AF.Relu, scale=-BIG, bias=BIG)
+            take("x%d%d" % (c, s), A("xc%d" % c, 16 * w * s, 16 * w * (s + 1)),
+                 ind(A("X", 0, PL if t == 0 else 2 * PL), A("pl", a + w * s, a + w * s + w)))
+        either("hb", lambda: ts(ck("hb", c), ck("kwc", c), 0.0, BIG, OP.is_equal, OP.mult),
+               lambda: act(ck("hb", c), ck("kwc", c), AF.Relu, scale=-BIG, bias=BIG))
         mms(SU(c, 288, 416, parts=16), [(A("padw%d" % c, 15, 271, 16), I1), (A("fl%d" % c), I1)], tok=tk)
-        act(A("wT", a, a + NL, parts=16), SU(c, 288, 416, parts=16), AF.Copy)
+        take("wT", A("wT", a, a + NL, parts=16), SU(c, 288, 416, parts=16))
         if t < NR - 1:
-            act(cw("v32%d" % ((t + 1) & 1), c), SU(c, 420, 428), AF.Copy)
+            take("v32", cw("v32%d" % ((t + 1) & 1), c), SU(c, 420, 428), None, 4096.0)
             wb = SU(c, 128, 256)
             mms(wb, [(A("ew", parts=16), A("wT", a, a + NL, parts=16))], tok=tk)
-            act(ck("v2", c), wb, scale=2.0, bias=2 * MID + 1)
+            take("v2", ck("v2", c), wb, 2 * MID + 1, 2.0)
             take("vr", ck("vr%d" % ((t + 1) & 1), c), wb)
             tt(ck("wm", c), ck("vr%d" % ((t + 1) & 1), c), MI(c, 0, 128), OP.mult)
 
@@ -513,9 +551,9 @@ def rank_program(g, core, T, topo):
         mms(pr, [(A("lt"), A("fl%d" % c, 8, 16)), (A("i1k"), A("fl%d" % c, 8, 16)), (A("i3"), cw("th", c))]
             + [(A("ones"), A("fl0", 8, 16))] * c)
         if t == 0:
-            ts(pad("padn", c), pr, 1024.0 + CAP + 0.5, -4096.0, OP.is_lt, OP.mult)
+            ts(pad("padn", c), pr, 3 * OFF + 1024.0 + CAP + 0.5, -4096.0, OP.is_lt, OP.mult)
         else:
-            act(pad("pada", c), pr, AF.Sign, scale=-1.0, bias=1024.0 + CAP + 0.5)
+            act(pad("pada", c), pr, AF.Sign, scale=-1.0, bias=3 * OFF + 1024.0 + CAP + 0.5)
             ax = MI(c, 448, 512)
             mms(ax, wrap("pada", c, "rx", 64) + [(I1, A("axc"))])
             tt(A("rw", 64 * c, 64 * c + 64), ax, A("wt"), OP.mult)
@@ -527,7 +565,7 @@ def rank_program(g, core, T, topo):
             ts(pad("padn", c), MI(c, 416, 424), col(20), -4096.0, OP.is_lt, OP.mult)
         mms(MI(c, 424, 432), wrap("padn", c) + [(I1, cw("dumc", c))])
         tt(cw("sy", c), MI(c, 424, 432), cw("v32%d" % (t & 1), c), OP.max)
-        ts(cw("sl", c), cw("sy", c), MID, None, OP.add)
+        take("sl", cw("sl", c), cw("sy", c), MID)
         o1, o2 = MI(c, 128, 256), MI(c, 256, 384)
         mms(o1, [(I1, ck("kwc", c)), (A("i256"), ck("kvr", c)), (A("efn", parts=16), wT)])
         tt(ck("f1", c), ck("kvr", c), o1, OP.max)
@@ -535,10 +573,10 @@ def rank_program(g, core, T, topo):
         out = ind(A(TAB[t + 1], 0, REM), cw("sl", c))
         if t < NR - 1:
             mms(o2, prs + [(A("efp", parts=16), wT)])
-            act(ck("r2", c), o2, AF.Relu, bias=-512.0)
+            relu("r2", ck("r2", c), o2, -512.0)
             tt(out, ck("f1", c), ck("r2", c), OP.add)
             mms(o1, [(I1, ck("bv", c)), (IM, ck("nm", c)), (I1, ck("wm", c))])
-            act(ck("bn", c), o1, bias=MID)
+            take("bn", ck("bn", c), o1, MID)
             cp(ind(A("nb", 0, REM), cw("sl", c)), ck("bn", c))
         else:
             mms(o2, prs + [(A("i512"), A("ones")), (A("efp", parts=16), wT)])
@@ -551,31 +589,41 @@ def rank_program(g, core, T, topo):
         z = ck(zbuf(t), c)
         xc, mx = "xc%d" % c, "mx%d" % c
         tk = ("w", 2 + c)
+        byv = [(c, r) in DV[t] for r in range(2)]
         for b in range(4):
-            bk = 4 + nb_[0] % 2
-            nb_[0] += 1
             h, r = b // 2, b % 2
-            mms(P(bk, 0, 512), [(I1, A(xc, 1024 * h + r, 1024 * h + 1024, 2))]
-                + [(IM, A(zbuf(t), a + 64 * h, a + 64 * h + 64), P(bk, j, 512, 8)) for j in range(8)])
-            act(A(mx, 1024 * r + 512 * h, 1024 * r + 512 * h + 512), P(bk, 0, 512), AF.Abs)
+            x, o = A(xc, 1024 * h + r, 1024 * h + 1024, 2), A(mx, 1024 * r + 512 * h, 1024 * r + 512 * h + 512)
+            if not (r == 1 and byv[0] and byv[1]):
+                bk = 4 + nb_[0] % 2
+                nb_[0] += 1
+                mms(P(bk, 0, 512), [(I1, x)] * (1 - byv[r])
+                    + [(I1 if byv[r] else IM, A(zbuf(t), a + 64 * h, a + 64 * h + 64), P(bk, j, 512, 8)) for j in range(8)])
+            if byv[r]:
+                tt(o, x, P(bk, 0, 512), OP.max)
+            else:
+                act(o, P(bk, 0, 512), AF.Abs)
             if b == 0:
-                mms(None, [(I1, A("pt"), SU(c, 0, 128)), (A("thrb"), IM, SU(c, 128, 256))], True, False, tk)
+                mms(None, [(I1, A("pt"), SU(c, 0, 128)), (A("thrb"), IM, SU(c, 128, 256))]
+                    + [(z, A("zm"), SU(c, r2, 256, 2)) for r2 in range(2) if byv[r2]], True, False, tk)
             if h == 1:
-                mms(None, [(A(mx, 1024 * r + j, 1024 * r + 1024, 8), A("sd"), SU(c, r + 2 * j, 256, 16)) for j in range(8)],
-                    False, r == 1, tk)
+                if byv[r]:
+                    mms(None, [(A(xc, r + 2 * j, H, 16), A("sdm"), SU(c, r + 2 * j, 256, 16)) for j in range(8)], False, False, tk)
+                mms(None, [(A(mx, 1024 * r + j, 1024 * r + 1024, 8), A("sd2" if byv[r] else "sd"), SU(c, r + 2 * j, 256, 16))
+                           for j in range(8)], False, r == 1, tk)
         tk = ("r", 2 + c)
         scan(ck("ds", c), A("mnm"), SU(c, 0, 128), OP.max, OP.min)
         last = A("ds", a + 15, a + NL, 16)
         rnd(cw("pH", c), last, 5)
         tt(pad("padp", c), last, cw("pH", c), OP.subtract)
-        act(ck("ug", c), SU(c, 128, 256), AF.Relu, scale=BIG, bias=-2047 * BIG if t == 0 else A("fs", 4 + t, 5 + t))
+        either("ug", lambda: ts(ck("ug", c), SU(c, 128, 256), 2047.5 if t == 0 else A("fs", 8 + t, 9 + t), BIG, OP.is_gt, OP.mult),
+               lambda: act(ck("ug", c), SU(c, 128, 256), AF.Relu, scale=BIG, bias=-2047 * BIG if t == 0 else A("fs", 4 + t, 5 + t)))
         mms(SU(c, 288, 416), [(I1, ck("kwc", c)), (I1, ck("io", c)), (I1, ck("hb", c)), (ck("ug", c), I1)], tok=tk)
         red(SU(1, 416, 417) if c == 0 else A("rr", 0, 1), SU(c, 288, 417), OP.min)
         mms(SU(c, 428, 436), wrap("padp", c) + [(I1, A("pc"))], tok=tk)
-        cp(cw("pw", c), SU(c, 428, 436))
-        act(ck("xs", c), ind(A(xc), cw("pw", c)))
+        take("pw", cw("pw", c), SU(c, 428, 436))
+        take("xs", ck("xs", c), ind(A(xc), cw("pw", c)), -0.5)
         xz = MI(c, 256, 384)
-        mms(xz, [(A("ih"), z), (A("iq"), A("ones")), (A("ih"), ck("xs", c))])
+        mms(xz, [(A("ih"), z), (A("ih"), ck("xs", c))])
         if t < NR - 1:
             rnd(ck("zb", c), xz, 0)
         else:
@@ -588,11 +636,12 @@ def rank_program(g, core, T, topo):
         mms(MI(1, 433, 434), on + [(I1, A("c75", 0, 1))])
         rnd(A("fs", 2, 3), MI(1, 433, 434), 4)
         tt(A("fs", 3, 4), MI(1, 432, 433), A("fs", 2, 3), OP.subtract)
-        act(A("fs", 5 + t, 6 + t), A("fs", 3, 4), scale=-BIG, bias=-2047 * BIG)
+        take("fs", A("fs", 5 + t, 6 + t), A("fs", 3, 4), -2047 * BIG, -BIG)
+        take("fs", A("fs", 9 + t, 10 + t), A("fs", 3, 4), 2047.5)
 
     def clean(tab, frm, nm, key, neg):
         bon[0] = BT["cl"]
-        act(A("rr", neg, neg + 1), key, AF.Copy, scale=-1.0)
+        take("neg", A("rr", neg, neg + 1), key, None, -1.0)
         w = V // CLP
         for lo in range(0, V, w):
             ts(A(nm, lo, lo + w), A(frm, lo, lo + w), key, A("rr", neg, neg + 1), OP.is_equal, OP.mult)
@@ -607,7 +656,6 @@ def rank_program(g, core, T, topo):
             bon[0] = 1e5
             remote(ra, [(prv, A("rc%d" % t, 0, 1), nxt, "rws%d" % t), (nxt, A("rb%d" % t, 0, 1), prv, "rvs%d" % t)], "rvl%d" % t, LV)
             bon[0] = 0.0
-            pushes(t + 1)
         if t == 0:
             clean("tab2", "tab0", "tab2", ra, 6)
         elif t == 1:
@@ -621,10 +669,7 @@ def rank_program(g, core, T, topo):
                 ts(A("cln", lo, hi), A("tab3", lo, hi), ra, ra, OP.is_equal, OP.mult)
                 o = P((4, 5, 0, 1)[i % 4], 0, 384)
                 mms(o, [(I1, A("tab3", lo, hi)), (IM, A("cln", lo, hi))])
-                if i in (3, 6):
-                    ts(A("fin", lo, hi), o, 0.0, None, OP.max)
-                else:
-                    act(A("fin", lo, hi), o, AF.Relu)
+                relu("fin", A("fin", lo, hi), o, 0.0)
             for q, lo, hi in (("y", 0, 768), ("y", 768, 1536), ("y", 1536, 2304), ("y", 2304, V)):
                 dma(q, hbm("yk", lo, hi), A("fin", lo, hi), 256 * (hi - lo))
 
@@ -648,6 +693,7 @@ def rank_program(g, core, T, topo):
         for c in range(NC):
             st("f", t, c)
         if t < NR - 1:
+            pushes(t + 1)
             failures(t)
         if t == 1:
             clean("tab3", "tab2", "tab3", A("rb0", 0, 1), 7)
@@ -660,16 +706,19 @@ def rank_program(g, core, T, topo):
 def _plan(ops, pred, succ, prio, back):
     n = len(ops)
     left = [len(p) for p in pred]
-    fin, est = [0.0] * n, [0.0] * n
+    fin, est, who = [0.0] * n, [0.0] * n, [None] * n
     qfree, ready, order, bank, turns = {}, {}, [], {}, [[] for _ in range(n)]
 
     def push(i):
         est[i] = max([fin[j] + w for j, w in pred[i]], default=0.0) + (ops[i]["lat"] if back else 0.0)
-        ready.setdefault(ops[i]["q"], []).append(i)
+        for q in ops[i].get("alt", [ops[i]["q"]]):
+            ready.setdefault(q, []).append(i)
 
-    def start(i):
-        o = ops[i]
-        return max([est[i]] + [fin[j] + WK for b in o["banks"] for q2, j in bank.get(b, {}).items() if q2 != o["q"]])
+    def start(i, q):
+        return max([est[i]] + [fin[j] + WK for b in ops[i]["banks"] for q2, j in bank.get(b, {}).items() if q2 != q])
+
+    def dur(i, q):
+        return ops[i]["alt"][q][0] if "alt" in ops[i] else ops[i]["dur"]
     for i in range(n):
         if left[i] == 0:
             push(i)
@@ -677,29 +726,31 @@ def _plan(ops, pred, succ, prio, back):
         best = None
         for q, rs in ready.items():
             if rs:
-                ss = [(start(i), i) for i in rs]
+                ss = [(start(i, q) + (LEAN if q == "v" and "alt" in ops[i] else 0.0), i) for i in rs]
                 t0 = max(0.0 if q == "ext" else qfree.get(q, 0.0), min(ss)[0])
                 if best is None or t0 < best[0]:
                     best = (t0, q, ss)
         t0, q, ss = best
         i = max([i for s, i in ss if s <= t0 + SLACK], key=lambda k: (prio[k], -k))
-        soon = [k for s, k in ss if s <= t0 + HOLD * ops[i]["dur"] and prio[k] > prio[i] + ops[i]["dur"]]
+        soon = [k for s, k in ss if s <= t0 + HOLD * dur(i, q) and prio[k] > prio[i] + dur(i, q)]
         if soon:
             i = max(soon, key=lambda k: (prio[k], -k))
-        ready[q].remove(i)
         o = ops[i]
-        st = max(t0, start(i))
+        for q2 in o.get("alt", [q]):
+            ready[q2].remove(i)
+        st = max(0.0 if q == "ext" else qfree.get(q, 0.0), start(i, q))
         for b in o["banks"]:
             turns[i] += [j for q2, j in bank.setdefault(b, {}).items() if q2 != q]
             bank[b][q] = i
-        qfree[q] = st + o["dur"]
-        fin[i] = st + o["dur"] + (0.0 if back else o["lat"])
+        qfree[q] = st + dur(i, q)
+        fin[i] = qfree[q] + (0.0 if back else o["lat"])
         order.append(i)
+        who[i] = q
         for s, w in succ[i]:
             left[s] -= 1
             if left[s] == 0:
                 push(s)
-    return max(fin), fin, order, turns
+    return max(fin), fin, order, turns, who
 
 
 def _emit(g, T, ops):
@@ -721,13 +772,20 @@ def _emit(g, T, ops):
             r = _plan(ops, pred, succ, [p + o["bon"] for p, o in zip(prio, ops)], False)
             if best is None or r[0] < best[0]:
                 best = r
-            ends = r[1] if k % 4 < 3 else best[1]
-            prio = _plan(ops, succ, pred, [e + x for e, x in zip(ends, rng.random(n) * JIT)], True)[1]
+            if k == 0 or r[0] < cur[0] + TEMP * (1 - k / PASSES):
+                cur = r
+            ends = np.array(cur[1])
+            mid = rng.random() * cur[0]
+            ends = ends + rng.random(n) * JIT * (np.abs(ends - mid) < WIN)
+            prio = _plan(ops, succ, pred, list(ends), True)[1]
         PLAN.append(best)
     order = PLAN[0][2]
     for i in range(n):
         for j in PLAN[0][3][i]:
             ops[i]["deps"][j] = True
+        if "alt" in ops[i]:
+            ops[i]["q"] = PLAN[0][4][i]
+            ops[i]["dur"], ops[i]["call"] = ops[i]["alt"][ops[i]["q"]]
     eng = {"v": g.vector, "s": g.scalar, "p": g.tensor, "g": g, "y": g.sync}
     known = {q: {} for q in eng}
     count, semof, clock = {}, {}, {}

import numpy as np
from concourse.bass import DstId, RemoteDMATransfer
from concourse.mybir import AluOpType, AxisListType, ActivationFunctionType

OP = AluOpType
AF = ActivationFunctionType
V, PL, L, NR, H = 2688, 4096, 256, 3, 2048
REM = V + L
NC, NL = 2, 128
MID = 1344.0
OFF = 1088.0
BIG = float(2 ** 20)
TINY = 2.0 ** -60
CAP = 64
REP = 4
CYC, PEC, VF, SF, PF, WK, GA, SCA = 0.9, 0.46, 60.0, 150.0, 5.0, 70.0, 1.4, 3.0
LZ, LN, LR, LX = 3000.0, 8000.0, 10500.0, 6000.0
LP, LV = 17000.0, 15000.0
BT = {"k": 0.0, "v": (0.0, 0.0), "n": (0.0, 0.0), "h": (0.0, 0.0), "c": (0.0, 0.0), "w": (0.0, 0.0),
      "f": (0.0, 0.0), "d": (0.0, 0.0), "e": 0.0, "cl": 0.0}
ENG = {"k01": "s", "k10": "s", "k11": "s", "k20": "s", "k21": "s"}
DV = ((), (), ())
NS = (0, 0)
HV = (1, 1)
SUBK, SUBX, CLP = 2, 2, 3
SLACK, HOLD, PASSES, JIT, SEED = 30.0, 0.3, 250, 1000.0, 1
TEMP, WIN, LEAN = 1500.0, 20000.0, 150.0
PLAN = []
ALIAS = {}
SCRATCH = {}


def _pack(big, dtype, names):
    o = 0
    for nm, w in names:
        ALIAS[nm] = (big, o)
        o += w
    SCRATCH[big] = ("sbuf", [128, o], dtype)


def _bufs(dtype, width, names):
    for nm in names:
        SCRATCH[nm] = ("sbuf", [128, width], dtype)


_pack("cb", "bfloat16", [(x, 128) for x in ("i1", "im", "ih", "bo1", "i1k", "lt", "ones", "i3", "im69", "i256",
                                            "i512", "pt", "yc0", "yc1", "yc2", "bo16", "ew", "efn", "efp")]
      + [("u1", 144), ("i18", 144), ("sn", 8), ("b8", 8), ("coff", 16), ("io", 256), ("rx", 1024), ("rxi", 1024), ("axc", 64),
         ("sv", 8), ("se", 8), ("sd", 16), ("sd2", 16), ("sdm", 16), ("zm", 128), ("c69", 8), ("c75", 8)])
_pack("cf", "float32", [("row", 256), ("jr", 128), ("j18", 144), ("m16", 128), ("mxm", 144), ("mnm", 128), ("pw2", 176),
                        ("half", 176), ("zero", 176), ("wt", 64), ("g8", 64), ("b8f", 16),
                        ("on32", 128), ("tmp", 128), ("col", 48)])
_pack("ch", "float16", [("thrb", 128), ("dumc", 16), ("pc", 8), ("ch1k", 8), ("ksc", 288), ("th", 16), ("hH", 16)])
PADW = 272 + 3 * 144
_pack("pad", "float16", [(x + str(c), w) for c in range(NC) for x, w in (("padw", 272), ("padh", 144), ("padn", 144), ("padp", 144))])
_pack("padb", "bfloat16", [("pada0", 144), ("pada1", 144), ("fl0", 16), ("fl1", 16)])
_bufs("bfloat16", REM, ("tab0", "tab2", "tab3"))
_bufs("bfloat16", H, ("rem0", "rem1", "rem2"))
_bufs("bfloat16", H, ("e10", "e11", "e20", "e21", "xc0", "xc1", "mx0", "mx1", "kc0", "kc1"))
_bufs("bfloat16", V, ("cln", "clc", "fin"))
_bufs("bfloat16", L, ("zi", "zb", "e0", "kw", "kwc", "qw", "qx", "src", "sa", "sb", "f1", "r2", "qc", "hb", "ug", "kvr", "knp"))
_bufs("bfloat16", 2 * L, ("kvn", "qa", "qb"))
_bufs("float16", L, ("bv", "nm", "cdh", "wm", "vr0", "vr1", "r16", "wT", "xs"))
_bufs("float32", L, ("pz", "v2", "ds", "bn", "yzf"))
_bufs("float32", 288, ("sc", "ad", "val"))
_bufs("int32", L, ("pi", "pj", "pk"))
_bufs("uint16", L, ("cd", "pl"))
_bufs("float32", 4, ("ra0", "ra1", "ra2", "rb0", "rb1", "rc0", "rc1"))
_bufs("float32", 16, ("fs", "rr"))
_bufs("int32", 8, ("ipc",))
_pack("smu", "uint16", [(x, 16) for x in ("nl", "pw", "hl", "sl", "wl0", "wl1", "wl2")])
_pack("sm32", "float32", [(x, 16) for x in ("sy", "pH", "v320", "v321")])
_pack("smb", "bfloat16", [("rw", 128), ("rw2", 64)])
SCRATCH["nb"] = ("sbuf", [128, REM], "int32")
SCRATCH["X"] = ("sbuf", [128, 2 * PL], "bfloat16")
SCRATCH["thi"] = ("sbuf", [128, 1], "int32")
SCRATCH["e3"] = ("sbuf", [128, 3072], "bfloat16")
for _b in range(8):
    SCRATCH["ps%d" % _b] = ("psum", [128, 512], "float32")
SEMAPHORES = ["qv", "qs", "qp", "qg"] + ["d%d" % i for i in range(40)] \
    + [a + str(i) for a in ("push", "pl", "rvs", "rvl", "rws") for i in range(3)]


def rank_program(g, core, T, topo):
    rank = T.rank_of(core)
    if rank is None:
        return
    nranks = len(T.cores)
    nxt, prv = T.cores[(rank + 1) % nranks], T.cores[(rank - 1) % nranks]
    ops, hist, ndma, bon, nb_, dry = [], {}, [0], [0.0], [0], []

    def A(name, lo=0, hi=None, st=1, parts=None):
        if name in ALIAS:
            big, o = ALIAS[name]
            if hi is None:
                later = [x[1] for x in ALIAS.values() if x[0] == big and x[1] > o]
                hi = min(later + [SCRATCH[big][1][1]]) - o
            name, lo, hi = big, lo + o, hi + o
        elif hi is None:
            hi = SCRATCH[name][1][1]
        rows = slice(0, 128 if parts is None else parts)
        ap = T[name][rows, lo:hi] if st == 1 else T[name][rows, lo:hi:st]
        return ([(name, lo, hi)], ap, (hi - lo + st - 1) // st)

    def ind(win, lst):
        return (win[0] + lst[0], win[1].indirect(lst[1]), 16 * lst[2], 1)

    def op(q, dur, rd, wr, call, sem=None, val=1, lat=0.0):
        if dry:
            if dry[0] == 1:
                return dur, rd, call
            rd = rd + dry.pop()
        i = len(ops)
        deps = {}
        for regs, w in ((rd, 0), (wr, 1)):
            for nm, lo, hi in regs:
                for j, l2, h2, w2 in hist.get(nm, []):
                    if j != i and l2 < hi and lo < h2 and (w or w2):
                        own = ops[j]["q"] == q and sem is None and ops[j]["sem"] is None
                        soft = own and q == "p"
                        deps[j] = deps.get(j, False) or not soft
        for regs, w in ((rd, 0), (wr, 1)):
            for nm, lo, hi in regs:
                a = hist.setdefault(nm, [])
                if w:
                    a[:] = [e for e in a if e[0] == i or not (lo <= e[1] and e[2] <= hi)]
                a.append((i, lo, hi, w))
        banks = sorted(set(x[0] for x in rd + wr if x[0][:2] == "ps"))
        ops.append({"q": q, "dur": dur, "deps": deps, "call": call, "sem": sem, "val": val, "lat": lat, "bon": bon[0],
                    "banks": banks})
        return i

    def dt(x):
        return SCRATCH[x[0][0][0]][2]

    def vdur(n, f):
        return max(64.0, n * f) * CYC + VF

    def two(*xs):
        return all(dt(x) in ("bfloat16", "float16", "uint16") for x in xs)

    def sc_(x):
        return (x[1], x[0]) if isinstance(x, tuple) else (x, [])

    def ts(out, a, s1, s2, o0, o1=None):
        x1, r1 = sc_(s1)
        x2, r2 = sc_(s2)
        f = GA if len(a) > 3 else (0.5 if two(out, a) else 1.0)
        if o1 is None:
            def call():
                return g.vector.tensor_scalar(out[1], a[1], x1, None, o0)
        else:
            def call():
                return g.vector.tensor_scalar(out[1], a[1], x1, x2, o0, o1)
        return op("v", vdur(a[2], f), a[0] + r1 + r2, out[0], call)

    def rnd(out, a, m):
        big = 1.5 * 2.0 ** (23 + m)
        return ts(out, a, big, -big, OP.add, OP.add)

    def tt(out, a, b, o):
        ps = a[0][0][0][:2] == "ps" or b[0][0][0][:2] == "ps"
        f = SCA if len(out) > 3 else GA if len(a) > 3 else 1.0 if ps else 2.0
        return op("v", vdur(b[2], f), a[0] + b[0] + out[0][1:], out[0][:1],
                  lambda: g.vector.tensor_tensor(out[1], a[1], b[1], o))

    def cp(out, a):
        f = SCA if len(out) > 3 else GA if len(a) > 3 else (0.5 if two(out, a) else 1.0)
        return op("v", vdur(a[2], f), a[0] + out[0][1:], out[0][:1], lambda: g.vector.tensor_copy(out[1], a[1]))

    def red(out, a, o):
        return op("v", vdur(a[2], 1.0), a[0], out[0], lambda: g.vector.tensor_reduce(out[1], a[1], AxisListType.X, o))

    def scan(out, d0, d1, o0, o1, init=0.0):
        return op("v", vdur(d1[2], 1.0), d0[0] + d1[0], out[0],
                  lambda: g.vector.tensor_tensor_scan(out[1], d0[1], d1[1], init, o0, o1))

    def fill(out, c):
        return op("v", vdur(out[2], 0.5), [], out[0], lambda: g.vector.memset(out[1], c))

    def act(out, a, func=None, scale=1.0, bias=0.0, acc=None):
        x, r = sc_(bias)
        y, r2 = sc_(scale)
        fn = AF.Identity if func is None else func
        if acc is None:
            def call():
                return g.scalar.activation(out[1], a[1], fn, bias=x, scale=y)
        else:
            def call():
                return g.scalar.activation(out[1], a[1], fn, bias=x, scale=y, accum_out=acc[1])
        return op("s", a[2] * (GA if len(a) > 3 else 1.0) * CYC + SF, a[0] + r + r2, out[0] + (acc[0] if acc else []), call)

    def either(who, vec, sca):
        e = ENG.get(who, "a")
        if e != "a":
            return vec() if e == "v" else sca()
        dry.append(1)
        dur, rd, call = sca()
        dry[0] = rd
        i = vec()
        ops[i]["alt"] = {"v": (ops[i]["dur"], ops[i]["call"]), "s": (dur, call)}
        return i

    def take(who, out, a, add=None, mul=None):
        def vec():
            if mul is not None:
                return ts(out, a, mul, add or 0.0, OP.mult, OP.add)
            return cp(out, a) if add is None else ts(out, a, add, None, OP.add)
        return either(who, vec, lambda: act(out, a, bias=add or 0.0, scale=mul or 1.0))

    def relu(who, out, a, add):
        return either(who, lambda: ts(out, a, add, 0.0, OP.add, OP.max), lambda: act(out, a, AF.Relu, bias=add))

    def mms(out, pairs, start=True, stop=True, tok=None):
        prs = [(p[2] if len(p) > 2 else out, p[0], p[1]) for p in pairs]
        dur = sum(max(min(64.0, a[2]), b[2]) * (4 if dt(b) == "float32" else 1) * PEC + PF for o, a, b in prs)
        rd = [r for o, a, b in prs for r in a[0] + b[0]]
        wr = [r for o, a, b in prs for r in o[0]]
        if tok is not None:
            (rd if tok[0] == "r" else wr).append(("tok%d" % tok[1], 0, 1))

        def call():
            r = None
            for i, (o, a, b) in enumerate(prs):
                r = g.tensor.matmul(o[1], a[1], b[1], start and i == 0, stop and i == len(prs) - 1)
            return r
        return op("p", dur, rd, wr, call)

    def iota(out, pat, base, mul):
        if dt(out) != "int32":
            def call():
                return g.iota(out[1], pat, base, mul, allow_small_or_imprecise_dtypes=True)
        else:
            def call():
                return g.iota(out[1], pat, base, mul)
        return op("g", 130 + 2 * out[2] * CYC, [], out[0], call)

    def dma(q, out, a, nbytes, add=False, after=(), lat=None):
        s = "d%d" % ndma[0]
        ndma[0] += 1
        eng = {"y": g.sync, "s": g.scalar, "g": g}[q]
        if add:
            def call():
                return eng.dma_start(out[1], a[1], accum_op=OP.add, max_dma_last_dim=4096)
        else:
            def call():
                return eng.dma_start(out[1], a[1])
        return op(q, 1000 if q == "g" else 60, a[0] + (out[0] if add else []) + [(x, 0, 1) for x in after], out[0], call,
                  sem=s, val=16, lat=1900 + nbytes / 200.0 if lat is None else lat)

    def hbm(name, lo, hi):
        return ([("hbm_" + name, lo, hi)], T[name][:, lo:hi], hi - lo)

    def remote(src, parts, lsem, lat, after=()):
        trs, ne = [], 0
        for k, (dst, out, frm, rsem) in enumerate(parts):
            rid, pid, _se = topo.addr(dst)
            es = topo.engines(core, dst)[k::len(parts)]
            ne += len(es)
            trs.append(RemoteDMATransfer(dst_ids=[DstId(rid=rid, pnc=pid)], dma_engine_mask=sum(1 << e for e in es),
                                         remote_sem=T.sem[rsem], src=src[1], dst=out[1]))
        i = op("g", 1000, src[0] + list(after), [], lambda: g.remote_dma_fused(trs, local_sem=T.sem[lsem]), sem=lsem, val=ne, lat=lat)
        ops[i]["remote"] = True
        for k, (dst, out, frm, rsem) in enumerate(parts):
            j = op("ext", 0, [], out[0], None, sem=rsem, val=len(topo.engines(frm, core)[k::len(parts)]))
            ops[j]["after"] = i

    def P(b, lo, hi, st=1, parts=None): return A("ps%d" % b, lo, hi, st, parts)
    def SU(c, lo, hi, st=1, parts=None): return P(2 + c, lo, hi, st, parts)
    def MI(c, lo, hi, st=1): return P(6 + c, lo, hi, st)
    def col(i, w=1): return A("col", i, i + w)
    def ck(name, c): return A(name, NL * c, NL * c + NL)
    def cw(name, c): return A(name, 8 * c, 8 * c + 8)
    TAB = ("tab0", "tab0", "tab2", "tab3")
    def tabw(t): return A(TAB[t], 0, V)
    def zbuf(t): return "zi" if t == 0 else "zb"
    def pad(nm, c): return A(nm + str(c), 15, 143, 16)
    I1, IM = A("i1"), A("im")
    B8 = A("bo1", 0, 128, 16)

    def wrap(nm, c, sel="i1", n=8):
        if n == 8:
            return [(A(nm + str(c), 15 - q, 143 - q), A(sel, q, 128, 16)) for q in range(16)]
        return [(A(nm + str(c), 15 - q, 143 - q), A(sel, n * q, n * q + n)) for q in range(16)]

    for k, (nm, src, w, lat) in enumerate((("zi", "z0", L, LZ), ("nb", "nbr", V, LN), ("tab0", "ring", V, LR), ("thi", "thr", 1, LR))):
        bon[0] = 1e6 * (4 - k)
        dma("y", A(nm, 0, w), hbm(src, 0, w), 0, lat=lat)
    bon[0] = 0.0
    dma("y", A("X", 0, PL), hbm("mat", 0, PL), 0, after=("nb", "tab0"), lat=LX)

    bon[0] = BT["k"]
    iota(A("ipc", 0, 1), [[0, 1]], 0, 1)
    iota(A("row"), [[1, 256]], 0, 0)
    iota(A("jr"), [[0, 8], [1, 16]], 0, 0)
    iota(A("j18"), [[0, 8], [1, 18]], 0, 0)
    iota(A("v320"), [[160, 16]], -int(MID), 10)
    iota(A("v2"), [[20, 256]], 1, 0)
    iota(A("g8"), [[0, 8], [16, 8]], 0, 0)
    iota(A("io"), [[512, 256]], 0, 0)
    iota(A("rxi"), [[1, 16], [16, 8], [0, 8]], 0, 0)
    row128, row144, j128 = A("row", 0, 128), A("row", 0, 144), A("jr")
    ts(A("ipc", 1, 2), A("ipc", 0, 1), 15, None, OP.bitwise_and)
    cp(col(0, 2), A("ipc", 0, 2))
    tt(col(2), col(0), col(1), OP.subtract)
    ts(col(3), col(2), 15.0, None, OP.add)
    ts(col(4), col(2), 0.125, col(0), OP.mult, OP.add)
    tt(A("m16"), row128, j128, OP.subtract)
    ts(I1, row128, col(0), None, OP.is_equal)
    ts(A("bo1"), A("m16"), col(2), None, OP.is_equal)
    ts(A("u1"), row144, col(3), None, OP.is_equal)
    ts(A("i18"), row144, col(4), 1 / 4096, OP.is_equal, OP.mult)
    for nm, s in (("im", -1.0), ("ih", 0.5), ("i1k", 1024.0), ("i3", 3.0),
                  ("im69", -2.0 ** 69), ("i256", -256.0), ("i512", -512.0)):
        act(A(nm), I1, AF.Copy, scale=s)
    act(A("bo16"), A("bo1"), AF.Copy, scale=0.0625)
    for t in range(NR):
        ts(col(5 + t), col(1), -0.0625, 1 + t / 16, OP.mult, OP.add)
        act(A("yc%d" % t), row128, scale=0.0, bias=col(5 + t))
        ts(A("ipc", 2 + t, 3 + t), col(1), 811.0, float(t), OP.mult, OP.add)
    ts(A("ipc", 5, 8), A("ipc", 2, 5), PL - 1, None, OP.bitwise_and)
    cp(col(8, 3), A("ipc", 5, 8))
    ts(col(11), col(8), 4.0, None, OP.mult)
    for nm, lo, x in (("sv", 0, 32.0), ("se", 0, 17 * 32.0), ("sd", 0, 32.0), ("sd", 8, 1.0), ("b8f", 0, 1 / 2048), ("b8f", 8, 1 / 2048),
                      ("sn", 0, 1 / 4096), ("b8", 0, 1.0)):
        act(A(nm, lo, lo + 8), B8, AF.Copy, scale=x)
    if any(DV):
        act(A("sd2"), A("sd"), AF.Copy, scale=2.0)
        act(A("sdm"), A("sd"), AF.Copy, scale=-1.0)
        act(A("zm", 0, 64), A("bo1", 0, 128, 2), AF.Copy, scale=-32.0)
        act(A("zm", 64, 128), A("bo1", 0, 128, 2), AF.Copy, scale=-1.0)
    act(A("ch1k"), A("row", 0, 8), scale=0.0, bias=-1023.5 / 2048)
    act(A("coff"), A("row", 0, 16), scale=0.0, bias=OFF)
    for lo in (0, 144):
        act(A("ksc", lo, lo + 144), A("j18"), scale=-1.0, bias=OFF + 15 - 2.5 * 32)
    for lo, x in ((16, 0.0), (17, -35 * 32.0), (160, 0.0), (161, 16 * 32.0)):
        act(A("ksc", lo, lo + 127, 18), A("row", 0, 8), scale=0.0, bias=OFF + x)
    ts(A("mxm"), A("j18"), 0.5, 2e9, OP.is_ge, OP.mult)
    act(A("mxm"), A("mxm"), bias=-1e9)
    ts(A("mnm"), j128, 0.5, -2e9, OP.is_ge, OP.mult)
    act(A("mnm"), A("mnm"), bias=1e9)
    fill(A("pad"), 0.0)
    fill(A("padb"), 0.0)
    fill(SU(0, 416, 417), BIG)
    act(A("ones"), row128, scale=0.0, bias=1.0)
    act(A("on32"), row128, scale=0.0, bias=1.0)
    act(A("c69"), A("row", 0, 8), scale=0.0, bias=2.0 ** 69)
    act(A("c75"), A("row", 0, 8), scale=0.0, bias=-7.5)
    act(A("pt"), j128, bias=-8.0)
    ts(A("lt"), row128, col(0), None, OP.is_ge)
    ts(col(12), col(2), -10.0, None, OP.mult)
    ts(A("v320"), A("v320"), col(12), None, OP.add)
    ts(col(13), col(1), MID, None, OP.add)
    ts(A("dumc"), A("row", 0, 16), 16.0, col(13), OP.mult, OP.add)
    ts(col(14), col(1), 16.0, 8.0, OP.mult, OP.add)
    ts(A("pc"), A("row", 0, 8), 256.0, col(14), OP.mult, OP.add)
    ts(col(15), col(0), 16.0, None, OP.mult)
    ts(col(16), col(0), 16.0, -128.0, OP.mult, OP.add)
    ts(A("ew"), A("m16"), col(15), 4096.0, OP.is_equal, OP.mult)
    ts(A("efn"), A("m16"), col(16), -512.0, OP.is_equal, OP.mult)
    act(A("efp"), A("efn"), AF.Copy, scale=-1.0)
    bon[0] = 0.0
    cp(col(17), A("thi"))
    ts(col(18), col(17), -2048.0, None, OP.add)
    ts(A("thrb"), A("ones"), col(18), None, OP.mult)
    bon[0] = BT["k"] / 2
    fill(A("e3"), 0.0)
    ts(A("rx"), A("rxi"), col(0), 0.5, OP.is_equal, OP.mult)
    ts(A("axc"), A("g8"), col(2), -0.5, OP.is_equal, OP.add)
    fill(A("half"), 0.5)
    fill(A("zero"), 0.0)
    scan(A("pw2"), A("half"), A("zero"), OP.mult, OP.add, 2.0 ** 64)
    tt(A("tmp"), A("pw2", 0, 128), I1, OP.mult)
    red(col(19), A("tmp"), OP.add)
    ts(col(20), col(19), 2.0, None, OP.mult)
    ts(A("tmp", 0, 16), A("jr", 0, 16), col(1), None, OP.is_equal)
    tt(A("tmp", 16, 32), A("tmp", 0, 16), A("pw2", 0, 16), OP.mult)
    red(col(21), A("tmp", 16, 32), OP.add)
    ts(col(24, 8), A("b8"), col(21), None, OP.mult)
    for g2 in range(8):
        ts(A("wt", g2, 64, 8), A("pw2", 63, 176, 16), col(24 + g2), None, OP.mult)
    bon[0] = 0.0

    def pushes(t):
        bon[0] = 1e5
        remote(A(TAB[t], 0, H), [(prv, A("rem%d" % t), nxt, "push%d" % t)], "pl%d" % t, LP)
        bon[0] = 0.0

    pushes(0)
    dma("y", A("X", PL, 2 * PL), hbm("mat", 0, PL), 0, after=("X", "rem0"), lat=LX)

    def kv(nm, c, x): return A(nm, 256 * c + 128 * x, 256 * c + 128 * x + 128)
    def kone(x): return P(x, 0, 128 * REP, REP)

    def dead(t):
        return [A("ra%d" % max(t - 1, 0), 0, 1), A("rr", 4, 5)][:t]

    def stage_v(t, c):
        a = NL * c
        if t == 0:
            take("kv", kv("kvn", c, 0), A("tab0", 10 * a, 10 * (a + NL), 10))
            take("bv", ck("bv", c), A("nb", 10 * a, 10 * (a + NL), 10), -MID)
        else:
            vl = cw("wl%d" % (t - 1), c)
            take("kv", kv("kvn", c, 0), ind(tabw(t), vl))
            take("bv", ck("bv", c), ind(A("nb", 0, V), vl), -MID)

    def stage_n(t, c):
        a = NL * c
        y, m = MI(c, 128, 256), MI(c, 0, 128)
        mms(y, [(A("bo16"), ck(zbuf(t), c)), (I1, A("yc%d" % t)), (A("i1k"), A("ones"))])
        take("r16", ck("r16", c), y)
        tt(m, y, ck("r16", c), OP.is_equal)
        tt(ck("nm", c), ck("bv", c), m, OP.mult)
        mms(MI(c, 384, 392), [(A("u1", 15 - q, 143 - q), A("nm", a + q, a + NL, 16)) for q in range(16)])
        take("nl", cw("nl", c), MI(c, 384, 392), MID)
        take("cd", ck("cd", c), ind(A("nb", 0, V), cw("nl", c)))
        kc = "kc%d" % c
        w = NL // SUBK
        for s in range(SUBK):
            take("k%d%d" % (t, c), A(kc, 16 * w * s, 16 * w * (s + 1)), ind(tabw(t), A("cd", a + w * s, a + w * s + w)), 4 * TINY)
        take("kn", kv("kvn", c, 1), ind(tabw(t), cw("nl", c)), TINY)
        take("cdh", ck("cdh", c), ck("cd", c), -MID)
        for nm, r in zip(("qa", "qb"), dead(t)):
            ts(A(nm, 256 * c, 256 * c + 256), A("kvn", 256 * c, 256 * c + 256), r, r, OP.is_equal, OP.mult)

    def keys(t, c, x):
        prs = []
        for lhs, nm in [(I1, "kvn"), (IM, "qa"), (IM, "qb")][:1 + t]:
            prs += [(lhs, kv(nm, c, x), P(x, j, 128 * REP, REP)) for j in range(REP)]
        mms(None, prs)

    def stage_h(t, c):
        tt(ck("pz", c), ck(zbuf(t), c), kone(1), OP.mult)
        mms(MI(c, 392, 408), [(ck("pz", c), A("b8f")), (I1, A("coff")), (I1, A("ch1k"), MI(c, 400, 408))])
        take("hH", cw("hH", c), MI(c, 400, 408))
        tt(pad("padh", c), MI(c, 392, 400), cw("hH", c), OP.subtract)
        mms(MI(c, 436, 444), wrap("padh", c))
        take("hl", cw("hl", c), MI(c, 436, 444), None, 2048.0)
        take("src", ck("src", c), ind(A("rem%d" % t), cw("hl", c)))
        for nm, r in [("sa", A("rc%d" % max(t - 1, 0), 0, 1)), ("sb", A("ra0", 0, 1))][:t]:
            ts(ck(nm, c), ck("src", c), r, None, OP.is_equal)

    def stage_cmp(t, c):
        kc = "kc%d" % c
        tk = ("w", 2 + c)
        keys(t, c, 0)

        def low(o, x):
            return [(I1, A("ksc", 144 * x, 144 * x + 144), o(0, 1)), (ck("cdh", c), A("i18"), o(0, 1)),
                    (ck("nm", c), A("sn"), o(16, 18)), (ck("nm", c), A("sn"), o(17, 18))]

        def ov(lo, st): return MI(c, 128 + lo, 272, st)
        def on(lo, st): return SU(c, lo, 144, st)
        def ek(x, b, j): return A("e%d%d" % (x + 1, c), 128 * REP * b + j, 128 * REP * (b + 1), REP)
        ad, sc = A("ad", 144 * c, 144 * c + 144), A("sc", 144 * c, 144 * c + 144)
        mms(None, low(on, 1), True, False, tk)
        for x in range(2):
            e = "e%d%d" % (x + 1, c)
            if x == 1:
                keys(t, c, 1)
                bon[0] += BT["h"][c]
                stage_h(t, c)
                bon[0] -= BT["h"][c]
            for b in range(16 // REP):
                lo, hi = 128 * REP * b, 128 * REP * (b + 1)
                nh = 2 if x < HV[c] else 1
                if x == 1 and b < NS[c]:
                    if b == 0:
                        take("knp", ck("knp", c), kone(1))
                    bk = 4 + nb_[0] % 2
                    nb_[0] += 1
                    mms(P(bk, 0, 512), [(I1, A(kc, b, H, 4))] + [(IM, ck("knp", c), P(bk, j, 512, 4)) for j in range(4)])
                    d = A("mx%d" % c, lo, hi)
                    act(d, P(bk, 0, 512), AF.Abs)
                    either("ez", lambda: ts(A(e, lo, hi), d, 0.0, None, OP.is_equal),
                           lambda: act(A(e, lo, hi), d, AF.Relu, scale=-2 / TINY, bias=1.0))
                    nh = 0
                for h in range(nh):
                    w = 128 * REP // nh
                    tt(A(e, lo + w * h, lo + w * h + w), A(kc, H // nh * h + b, H // nh * (h + 1), 16 // REP),
                       P(x, w * h, w * h + w), OP.is_equal)
                if x == 1:
                    mms(None, [(ek(1, b, j), A("sv"), on(b + 16 // REP * j, 18)) for j in range(REP)], False, hi == H, tk)
            if x == 0:
                tt(ck("e0", c), kv("kvn", c, 1), kone(0), OP.is_equal)
                mms(None, low(ov, 0) + [(ck("e0", c), A("se"), ov(17, 18))]
                    + [(ek(0, b, j), A("sv"), ov(b + 16 // REP * j, 18)) for b in range(16 // REP) for j in range(REP)])
                take("ad", ad, ov(0, 1))
                take("kvr", ck("kvr", c), kone(0))
        val = A("val", 144 * c, 144 * c + 144)
        tt(val, ad, on(0, 1), OP.min)
        scan(sc, A("mxm"), val, OP.min, OP.max)
        tot = A("sc", 144 * c + 17, 144 * c + 144, 18)
        take("th", cw("th", c), tot)
        tt(pad("padw", c), tot, cw("th", c), OP.subtract)
        act(A("fl%d" % c, 8, 16), cw("th", c), AF.Relu, scale=-1.0, bias=OFF + 1, acc=A("fs", c, c + 1))
        mms(SU(c, 420, 428), wrap("padw", c), tok=("r", 2 + c))
        take("wl", cw("wl%d" % t, c), SU(c, 420, 428), MID, 4096.0)

    def stage_w(t, c):
        a = NL * c
        tk = ("r", 2 + c)
        src = ind(tabw(t), cw("wl%d" % t, c))
        if t == 0:
            tt(ck("pi", c), src, ck("v2", c), OP.mult)
            take("kwc", ck("kwc", c), src)
            ts(ck("pj", c), ck("pi", c), col(11), None, OP.add)
            ts(ck("pk", c), ck("pj", c), 2, PL - 1, OP.arith_shift_right, OP.bitwise_and)
            take("pl", ck("pl", c), ck("pk", c))
        else:
            take("kw", ck("kw", c), src)
            prs = [(I1, ck("kw", c))]
            for nm, r in zip(("qw", "qx"), dead(t)):
                ts(ck(nm, c), ck("kw", c), r, r, OP.is_equal, OP.mult)
                prs.append((IM, ck(nm, c)))
            mms(SU(c, 0, 128), prs, tok=tk)
            tt(ck("pi", c), ck("v2", c), SU(c, 0, 128), OP.mult)
            ts(ck("pk", c), ck("pi", c), 2, PL - 1, OP.arith_shift_right, OP.bitwise_and)
            take("pl", ck("pl", c), ck("pk", c), col(8 + t))
            take("kwc", ck("kwc", c), SU(c, 0, 128))
        w = NL // SUBX
        for s in range(SUBX):
            take("x%d%d" % (c, s), A("xc%d" % c, 16 * w * s, 16 * w * (s + 1)),
                 ind(A("X", 0, PL if t == 0 else 2 * PL), A("pl", a + w * s, a + w * s + w)))
        either("hb", lambda: ts(ck("hb", c), ck("kwc", c), 0.0, BIG, OP.is_equal, OP.mult),
               lambda: act(ck("hb", c), ck("kwc", c), AF.Relu, scale=-BIG, bias=BIG))
        mms(SU(c, 288, 416, parts=16), [(A("padw%d" % c, 15, 271, 16), I1), (A("fl%d" % c), I1)], tok=tk)
        take("wT", A("wT", a, a + NL, parts=16), SU(c, 288, 416, parts=16))
        if t < NR - 1:
            take("v32", cw("v32%d" % ((t + 1) & 1), c), SU(c, 420, 428), None, 4096.0)
            wb = SU(c, 128, 256)
            mms(wb, [(A("ew", parts=16), A("wT", a, a + NL, parts=16))], tok=tk)
            take("v2", ck("v2", c), wb, 2 * MID + 1, 2.0)
            take("vr", ck("vr%d" % ((t + 1) & 1), c), wb)
            tt(ck("wm", c), ck("vr%d" % ((t + 1) & 1), c), MI(c, 0, 128), OP.mult)

    def e3(c1, c):
        o = 256 * c1 + NL * c if c1 < 8 else 2048 + NL * (c1 - 8)
        return A("e3", o, o + NL)

    def stage_e(t):
        for c1 in range(16):
            o = 256 * c1 if c1 < 8 else 2048 + NL * (c1 - 9)
            ts(A("e3", o + 16 * c1, o + L), A("vr%d" % (t & 1), 16 * c1, L), A("v32%d" % (t & 1), c1, c1 + 1), None, OP.is_equal)

    def stage_f(t, c):
        a = NL * c
        wT = A("wT", a, a + NL, parts=16)
        pr = MI(c, 408, 416)
        mms(pr, [(A("lt"), A("fl%d" % c, 8, 16)), (A("i1k"), A("fl%d" % c, 8, 16)), (A("i3"), cw("th", c))]
            + [(A("ones"), A("fl0", 8, 16))] * c)
        if t == 0:
            ts(pad("padn", c), pr, 3 * OFF + 1024.0 + CAP + 0.5, -4096.0, OP.is_lt, OP.mult)
        else:
            act(pad("pada", c), pr, AF.Sign, scale=-1.0, bias=3 * OFF + 1024.0 + CAP + 0.5)
            ax = MI(c, 448, 512)
            mms(ax, wrap("pada", c, "rx", 64) + [(I1, A("axc"))])
            tt(A("rw", 64 * c, 64 * c + 64), ax, A("wt"), OP.mult)
            if c == 0:
                act(A("rw2"), ax, AF.Relu, scale=2.0 ** 70)
            mms(MI(c, 416, 424), [(I1, A("c69")), (A("im69"), pad("pada", c))]
                + [(e3(c1, 1), A("rw2", 8 * c1, 8 * c1 + 8)) for c1 in range(8 * c)]
                + [(e3(8 * c + c1, c), A("rw", 64 * c + 8 * c1, 64 * c + 8 * c1 + 8)) for c1 in range(8)])
            ts(pad("padn", c), MI(c, 416, 424), col(20), -4096.0, OP.is_lt, OP.mult)
        mms(MI(c, 424, 432), wrap("padn", c) + [(I1, cw("dumc", c))])
        tt(cw("sy", c), MI(c, 424, 432), cw("v32%d" % (t & 1), c), OP.max)
        take("sl", cw("sl", c), cw("sy", c), MID)
        o1, o2 = MI(c, 128, 256), MI(c, 256, 384)
        mms(o1, [(I1, ck("kwc", c)), (A("i256"), ck("kvr", c)), (A("efn", parts=16), wT)])
        tt(ck("f1", c), ck("kvr", c), o1, OP.max)
        prs = [(I1, ck("src", c)), (A("i256"), ck("kvr", c))] + [(A("i512"), ck(x, c)) for x in ("sa", "sb")[:t]]
        out = ind(A(TAB[t + 1], 0, REM), cw("sl", c))
        if t < NR - 1:
            mms(o2, prs + [(A("efp", parts=16), wT)])
            relu("r2", ck("r2", c), o2, -512.0)
            tt(out, ck("f1", c), ck("r2", c), OP.add)
            mms(o1, [(I1, ck("bv", c)), (IM, ck("nm", c)), (I1, ck("wm", c))])
            take("bn", ck("bn", c), o1, MID)
            cp(ind(A("nb", 0, REM), cw("sl", c)), ck("bn", c))
        else:
            mms(o2, prs + [(A("i512"), A("ones")), (A("efp", parts=16), wT)])
            tt(ck("r2", c), ck("f1", c), o2, OP.max)
            ts(ck("qc", c), ck("r2", c), A("rb1", 0, 1), A("rr", 9, 10), OP.is_equal, OP.mult)
            tt(out, ck("r2", c), ck("qc", c), OP.add)

    def stage_d(t, c):
        a = NL * c
        z = ck(zbuf(t), c)
        xc, mx = "xc%d" % c, "mx%d" % c
        tk = ("w", 2 + c)
        byv = [(c, r) in DV[t] for r in range(2)]
        for b in range(4):
            h, r = b // 2, b % 2
            x, o = A(xc, 1024 * h + r, 1024 * h + 1024, 2), A(mx, 1024 * r + 512 * h, 1024 * r + 512 * h + 512)
            if not (r == 1 and byv[0] and byv[1]):
                bk = 4 + nb_[0] % 2
                nb_[0] += 1
                mms(P(bk, 0, 512), [(I1, x)] * (1 - byv[r])
                    + [(I1 if byv[r] else IM, A(zbuf(t), a + 64 * h, a + 64 * h + 64), P(bk, j, 512, 8)) for j in range(8)])
            if byv[r]:
                tt(o, x, P(bk, 0, 512), OP.max)
            else:
                act(o, P(bk, 0, 512), AF.Abs)
            if b == 0:
                mms(None, [(I1, A("pt"), SU(c, 0, 128)), (A("thrb"), IM, SU(c, 128, 256))]
                    + [(z, A("zm"), SU(c, r2, 256, 2)) for r2 in range(2) if byv[r2]], True, False, tk)
            if h == 1:
                if byv[r]:
                    mms(None, [(A(xc, r + 2 * j, H, 16), A("sdm"), SU(c, r + 2 * j, 256, 16)) for j in range(8)], False, False, tk)
                mms(None, [(A(mx, 1024 * r + j, 1024 * r + 1024, 8), A("sd2" if byv[r] else "sd"), SU(c, r + 2 * j, 256, 16))
                           for j in range(8)], False, r == 1, tk)
        tk = ("r", 2 + c)
        scan(ck("ds", c), A("mnm"), SU(c, 0, 128), OP.max, OP.min)
        last = A("ds", a + 15, a + NL, 16)
        rnd(cw("pH", c), last, 5)
        tt(pad("padp", c), last, cw("pH", c), OP.subtract)
        either("ug", lambda: ts(ck("ug", c), SU(c, 128, 256), 2047.5 if t == 0 else A("fs", 8 + t, 9 + t), BIG, OP.is_gt, OP.mult),
               lambda: act(ck("ug", c), SU(c, 128, 256), AF.Relu, scale=BIG, bias=-2047 * BIG if t == 0 else A("fs", 4 + t, 5 + t)))
        mms(SU(c, 288, 416), [(I1, ck("kwc", c)), (I1, ck("io", c)), (I1, ck("hb", c)), (ck("ug", c), I1)], tok=tk)
        red(SU(1, 416, 417) if c == 0 else A("rr", 0, 1), SU(c, 288, 417), OP.min)
        mms(SU(c, 428, 436), wrap("padp", c) + [(I1, A("pc"))], tok=tk)
        take("pw", cw("pw", c), SU(c, 428, 436))
        take("xs", ck("xs", c), ind(A(xc), cw("pw", c)), -0.5)
        xz = MI(c, 256, 384)
        mms(xz, [(A("ih"), z), (A("ih"), ck("xs", c))])
        if t < NR - 1:
            rnd(ck("zb", c), xz, 0)
        else:
            rnd(ck("yzf", c), xz, 0)
            dma("y", hbm("yz", a, a + NL), ck("yzf", c), 512 * NL)

    def failures(t):
        on = [(A("on32"), A("fs", c, c + 1)) for c in range(NC)]
        mms(MI(1, 432, 433), on)
        mms(MI(1, 433, 434), on + [(I1, A("c75", 0, 1))])
        rnd(A("fs", 2, 3), MI(1, 433, 434), 4)
        tt(A("fs", 3, 4), MI(1, 432, 433), A("fs", 2, 3), OP.subtract)
        take("fs", A("fs", 5 + t, 6 + t), A("fs", 3, 4), -2047 * BIG, -BIG)
        take("fs", A("fs", 9 + t, 10 + t), A("fs", 3, 4), 2047.5)

    def clean(tab, frm, nm, key, neg):
        bon[0] = BT["cl"]
        take("neg", A("rr", neg, neg + 1), key, None, -1.0)
        w = V // CLP
        for lo in range(0, V, w):
            ts(A(nm, lo, lo + w), A(frm, lo, lo + w), key, A("rr", neg, neg + 1), OP.is_equal, OP.mult)
        dma("g", A(tab, 0, V), A(frm if nm == tab else nm, 0, V), 2 * 128 * V * 2, add=True)
        bon[0] = 0.0

    def stage_rv(t):
        ra = A("ra%d" % t, 0, 1)
        rnd(A("rr", 1, 2), A("rr", 0, 1), 9)
        tt(ra, A("rr", 0, 1), A("rr", 1, 2), OP.subtract)
        if t < NR - 1:
            bon[0] = 1e5
            remote(ra, [(prv, A("rc%d" % t, 0, 1), nxt, "rws%d" % t), (nxt, A("rb%d" % t, 0, 1), prv, "rvs%d" % t)], "rvl%d" % t, LV)
            bon[0] = 0.0
        if t == 0:
            clean("tab2", "tab0", "tab2", ra, 6)
        elif t == 1:
            tt(A("rr", 3, 4), ra, A("rb0", 0, 1), OP.not_equal)
            tt(A("rr", 4, 5), A("rr", 3, 4), A("rb0", 0, 1), OP.mult)
            clean("tab3", "tab2", "cln", ra, 8)
            clean("tab3", "tab2", "clc", A("rb1", 0, 1), 9)
        else:
            for i in range(7):
                lo, hi = 384 * i, 384 * i + 384
                ts(A("cln", lo, hi), A("tab3", lo, hi), ra, ra, OP.is_equal, OP.mult)
                o = P((4, 5, 0, 1)[i % 4], 0, 384)
                mms(o, [(I1, A("tab3", lo, hi)), (IM, A("cln", lo, hi))])
                relu("fin", A("fin", lo, hi), o, 0.0)
            for q, lo, hi in (("y", 0, 768), ("y", 768, 1536), ("y", 1536, 2304), ("y", 2304, V)):
                dma(q, hbm("yk", lo, hi), A("fin", lo, hi), 256 * (hi - lo))

    stages = {"v": stage_v, "n": stage_n, "c": stage_cmp, "w": stage_w, "d": stage_d, "f": stage_f}

    def st(f, t, c):
        bon[0] = BT[f][c]
        stages[f](t, c)
        bon[0] = 0.0

    for t in range(NR):
        if t > 0:
            bon[0] = BT["e"]
            stage_e(t)
        for c in range(NC):
            st("v", t, c)
            st("n", t, c)
        for c in range(NC):
            st("c", t, c)
            st("w", t, c)
        for c in range(NC):
            st("f", t, c)
        if t < NR - 1:
            pushes(t + 1)
            failures(t)
        if t == 1:
            clean("tab3", "tab2", "tab3", A("rb0", 0, 1), 7)
        for c in range(NC):
            st("d", t, c)
        stage_rv(t)
    _emit(g, T, ops)


def _plan(ops, pred, succ, prio, back):
    n = len(ops)
    left = [len(p) for p in pred]
    fin, est, who = [0.0] * n, [0.0] * n, [None] * n
    qfree, ready, order, bank, turns = {}, {}, [], {}, [[] for _ in range(n)]

    def push(i):
        est[i] = max([fin[j] + w for j, w in pred[i]], default=0.0) + (ops[i]["lat"] if back else 0.0)
        for q in ops[i].get("alt", [ops[i]["q"]]):
            ready.setdefault(q, []).append(i)

    def start(i, q):
        return max([est[i]] + [fin[j] + WK for b in ops[i]["banks"] for q2, j in bank.get(b, {}).items() if q2 != q])

    def dur(i, q):
        return ops[i]["alt"][q][0] if "alt" in ops[i] else ops[i]["dur"]
    for i in range(n):
        if left[i] == 0:
            push(i)
    while len(order) < n:
        best = None
        for q, rs in ready.items():
            if rs:
                ss = [(start(i, q) + (LEAN if q == "v" and "alt" in ops[i] else 0.0), i) for i in rs]
                t0 = max(0.0 if q == "ext" else qfree.get(q, 0.0), min(ss)[0])
                if best is None or t0 < best[0]:
                    best = (t0, q, ss)
        t0, q, ss = best
        i = max([i for s, i in ss if s <= t0 + SLACK], key=lambda k: (prio[k], -k))
        soon = [k for s, k in ss if s <= t0 + HOLD * dur(i, q) and prio[k] > prio[i] + dur(i, q)]
        if soon:
            i = max(soon, key=lambda k: (prio[k], -k))
        o = ops[i]
        for q2 in o.get("alt", [q]):
            ready[q2].remove(i)
        st = max(0.0 if q == "ext" else qfree.get(q, 0.0), start(i, q))
        for b in o["banks"]:
            turns[i] += [j for q2, j in bank.setdefault(b, {}).items() if q2 != q]
            bank[b][q] = i
        qfree[q] = st + dur(i, q)
        fin[i] = qfree[q] + (0.0 if back else o["lat"])
        order.append(i)
        who[i] = q
        for s, w in succ[i]:
            left[s] -= 1
            if left[s] == 0:
                push(s)
    return max(fin), fin, order, turns, who


def _emit(g, T, ops):
    n = len(ops)
    pred, succ = [[] for _ in range(n)], [[] for _ in range(n)]
    for i, o in enumerate(ops):
        if "after" in o:
            o["deps"][o["after"]] = False
        for j, hard in o["deps"].items():
            pred[i].append((j, WK if hard else 0.0))
            succ[j].append((i, WK if hard else 0.0))
    if not PLAN:
        prio = [0.0] * n
        for i in range(n - 1, -1, -1):
            prio[i] = ops[i]["dur"] + ops[i]["lat"] + max([prio[s] + w for s, w in succ[i]], default=0.0)
        best = None
        rng = np.random.default_rng(SEED)
        for k in range(PASSES):
            r = _plan(ops, pred, succ, [p + o["bon"] for p, o in zip(prio, ops)], False)
            if best is None or r[0] < best[0]:
                best = r
            if k == 0 or r[0] < cur[0] + TEMP * (1 - k / PASSES):
                cur = r
            ends = np.array(cur[1])
            mid = rng.random() * cur[0]
            ends = ends + rng.random(n) * JIT * (np.abs(ends - mid) < WIN)
            prio = _plan(ops, succ, pred, list(ends), True)[1]
        PLAN.append(best)
    order = PLAN[0][2]
    for i in range(n):
        for j in PLAN[0][3][i]:
            ops[i]["deps"][j] = True
        if "alt" in ops[i]:
            ops[i]["q"] = PLAN[0][4][i]
            ops[i]["dur"], ops[i]["call"] = ops[i]["alt"][ops[i]["q"]]
    eng = {"v": g.vector, "s": g.scalar, "p": g.tensor, "g": g, "y": g.sync}
    known = {q: {} for q in eng}
    count, semof, clock = {}, {}, {}
    pos = {i: k for k, i in enumerate(order)}
    for i in order:
        o = ops[i]
        q = o["q"]
        if q == "ext":
            semof[i] = (o["sem"], o["val"])
            count[o["sem"]] = o["val"]
            clock[i] = {o["sem"]: o["val"]}
            continue
        kn = known[q]
        need = {}
        for j in sorted([j for j, hard in o["deps"].items() if hard], key=lambda j: -pos[j]):
            s, v = semof[j]
            if kn.get(s, 0) >= v:
                continue
            need[s] = max(need.get(s, 0), v)
            for s2, v2 in clock[j].items():
                if kn.get(s2, 0) < v2:
                    kn[s2] = v2
        for s, v in need.items():
            eng[q].wait_ge(T.sem[s], v)
        r = o["call"]()
        s = "q" + q if o["sem"] is None else o["sem"]
        count[s] = count.get(s, 0) + o["val"]
        if "remote" not in o:
            r.then_inc(T.sem[s], o["val"])
        semof[i] = (s, count[s])
        clock[i] = dict(kn)
        clock[i][s] = count[s]
    for s, v in count.items():
        if known["g"].get(s, 0) < v:
            g.wait_ge(T.sem[s], v)
